import numpy as np
import ml_dtypes


def mxq(x, axis, fmt="e4m3"):
    dtype, down = {"e4m3": (ml_dtypes.float8_e4m3fn, 7), "e5m2": (ml_dtypes.float8_e5m2, 14)}[fmt]
    v = np.moveaxis(np.asarray(x, np.float32).astype(ml_dtypes.bfloat16).astype(np.float64), axis, -1)
    blocks = v.reshape(v.shape[:-1] + (-1, 32))
    amax = np.abs(blocks).max(-1, keepdims=True)
    byte = np.maximum(np.where(amax > 0, np.frexp(amax)[1] - 1 + 127, 0) - down, 1)
    scale = np.exp2(byte - 127.0)
    codes = (blocks / scale).astype(np.float32).astype(dtype).astype(np.float64)
    return np.moveaxis((codes * scale).reshape(v.shape), -1, axis)


WIDE = False


def mx_kscale(k):
    if not WIDE:
        return np.ones(k)
    levels = np.array([10, -10, 5, -5, 0])
    if k % 512:
        return np.exp2(np.random.permutation(np.resize(levels, k // 32))).repeat(32)
    a = np.empty((k // 512, 16))
    for p in range(k // 512):
        a[p, :8] = np.random.permutation(np.resize(levels, 8))
        for g in range(8):
            far = levels[np.abs(levels - a[p, g]) >= 10]
            a[p, g + 8] = far[np.random.randint(len(far))]
    return np.exp2(a.ravel()).repeat(32)


def f64(x):
    return np.asarray(x).astype(np.float64)


def striped(idx):
    return np.tile(idx.reshape(-1, 16).T, (8, 1)).astype(np.uint16)


def unstriped(offs):
    return offs[:16].T.reshape(-1).astype(np.int64)


E2M1 = np.array([0.0, 0.5, 1.0, 1.5, 2.0, 3.0, 4.0, 6.0, -0.0, -0.5, -1.0, -1.5, -2.0, -3.0, -4.0, -6.0])


def pack_weight(w, fmt):
    k, n = w.shape
    w = f64(np.asarray(w, np.float32).astype(ml_dtypes.bfloat16)).reshape(k // 32, 32, n)
    amax = np.abs(w).max(1)
    if fmt == "e4m3":
        byte = np.frexp(amax)[1] - 1 + 127 - 7
    else:
        mant, ex = np.frexp(amax / 6.0)
        byte = np.where(mant > 0.5, ex, ex - 1) + 127
    byte = np.clip(np.where(amax > 0, byte, 1), 1, 254)
    scaled = (w * np.exp2(127.0 - byte)[:, None, :]).reshape(k, n).astype(np.float32)
    by_word = np.ascontiguousarray(scaled.reshape(k // 512, 128, 4, n).transpose(0, 1, 3, 2))
    if fmt == "e4m3":
        words = by_word.astype(ml_dtypes.float8_e4m3fn).view(np.uint8)
    else:
        c = by_word.astype(ml_dtypes.float4_e2m1fn).view(np.uint8) & 0xF
        words = (c[..., 0::2] | (c[..., 1::2] << 4)).reshape(k // 512, 128, 2 * n)
    return np.ascontiguousarray(words), np.ascontiguousarray(byte.astype(np.uint8).reshape(k // 512, 16, n))


def unpack_weight(words, scales, fmt):
    g, _, n = scales.shape
    words = np.ascontiguousarray(words).reshape(g, 128, n, -1)
    if fmt == "e4m3":
        vals = words.view(ml_dtypes.float8_e4m3fn).astype(np.float64)
    else:
        nib = np.empty((g, 128, n, 4), np.uint8)
        nib[..., 0::2] = words & 0xF
        nib[..., 1::2] = words >> 4
        vals = E2M1[nib]
    vals = vals * np.repeat(np.exp2(scales.astype(np.float64) - 127.0), 8, axis=1)[..., None]
    return vals.transpose(0, 1, 3, 2).reshape(g * 512, n)


def gelu(v):
    return 0.5 * v * (1.0 + np.tanh(np.sqrt(2.0 / np.pi) * (v + 0.044715 * v**3)))


def striped8(idx):
    return np.concatenate([v.reshape(-1, 16).T for v in idx]).astype(np.uint16)


def unstriped8(offs):
    return np.stack([offs[16 * g:16 * g + 16].T.reshape(-1) for g in range(8)]).astype(np.int64)


def heads(h, wgt, idx8):
    r = np.arange(h.shape[0])
    return wgt[r // 4 % 128] * h[r[:, None], idx8[r % 512 // 64]]


T, S, P, K, H, N = 2048, 1024, 512, 1024, 1024, 384

def setup_inputs():
    n = np.random.standard_normal
    s = mx_kscale(K)[:, None]
    u = mx_kscale(H)[:, None]
    tab_words, tab_scales = pack_weight(n((K, T)) * s, "e4m3")
    wd_words, wd_scales = pack_weight(n((K, H)) / np.sqrt(K) / s * u.T, "e2m1")
    wu_words, wu_scales = pack_weight(n((K, H)) / np.sqrt(K) / s, "e4m3")
    return {
        "tab_words": tab_words, "tab_scales": tab_scales,
        "offs": striped(np.random.permutation(T)[:S]),
        "wd_words": wd_words, "wd_scales": wd_scales,
        "offs2": striped8(np.stack([np.random.permutation(S)[:P] for _ in range(8)])),
        "wgt": np.repeat(np.random.uniform(0.5, 2.0, (8, P)), 16, axis=0).astype(np.float32),
        "uses": (n((K, P)) * s).astype(np.float32),
        "wu_words": wu_words, "wu_scales": wu_scales,
        "old": (n((H, P)) * u).astype(np.float32),
        "wo": (n((H, N)) / np.sqrt(H) / u).astype(np.float32),
    }

def reference(tab_words, tab_scales, offs, wd_words, wd_scales, offs2, wgt, uses,
              wu_words, wu_scales, old, wo):
    v = unpack_weight(tab_words, tab_scales, "e4m3")[:, unstriped(offs)]
    wd = unpack_weight(wd_words, wd_scales, "e2m1")
    h = wd.T @ v
    x = heads(h, f64(wgt), unstriped8(offs2))
    wu = unpack_weight(wu_words, wu_scales, "e4m3")
    gate = 1.0 / (1.0 + np.exp(-(wu.T @ mxq(f64(uses), 0, "e4m3"))))
    o = f64(old)
    z = o + gate * (x - o)
    return mxq(f64(wo), 0, "e4m3").T @ mxq(z, 0, "e4m3")

@@ -1,0 +1,296 @@
+from contextlib import ExitStack
+
+import concourse.mybir as mybir
+from concourse.masks import make_identity
+
+T, S, M, K, H, N = 2048, 1024, 512, 1024, 1024, 384
+FLOPS = 2 * (K * H * S + K * H * M + H * N * M)
+
+F32 = mybir.dt.float32
+BF16 = mybir.dt.bfloat16
+I32 = mybir.dt.int32
+U32 = mybir.dt.uint32
+U16 = mybir.dt.uint16
+U8 = mybir.dt.uint8
+FP8X4 = mybir.dt.float8_e4m3fn_x4
+FP4X4 = mybir.dt.float4_e2m1fn_x4
+ALU = mybir.AluOpType
+ACT = mybir.ActivationFunctionType
+
+P = 128
+PACK = 4
+PASS = P * PACK
+BANK = 512
+KP = K // PASS
+RP = H // PASS
+MT = M // P
+NT = N // P
+SH = S // BANK
+
+
+def tile_list_reaching_names_kernel(
+    tc, tab_words, tab_scales, offs, wd_words, wd_scales, offs2, wgt, uses, wu_words, wu_scales, old, wo, out
+):
+    nc = tc.nc
+    with ExitStack() as ctx:
+        keep = ctx.enter_context(tc.tile_pool(name="keep", bufs=1))
+        psum = ctx.enter_context(tc.psum_pool(name="psum", bufs=1))
+
+        def sb(name, shape, dtype, tag=None):
+            return keep.tile(shape, dtype, name=name, tag=tag or name, align_bytes=64)
+
+        offs_sb = keep.tile([P, S // 16], U16, name="offs_sb")
+        offs2_sb = keep.tile([P, M // 16], U16, name="offs2_sb")
+        tab_sc = sb("tab_sc", [P, T], U8)
+        wd_sc = sb("wd_sc", [P, KP, H], U8)
+        wu_sc = sb("wu_sc", [P, H], U8)
+        v_sc = [sb("v_sc%d" % a, [P, S], U8) for a in range(KP)]
+        ident = sb("ident", [P, P], F32)
+        warm = sb("warm", [P, 1], F32)
+
+        nc.vector.memset(tab_sc[:].bitcast(I32), 0)
+        nc.vector.memset(wd_sc[:].rearrange("p a c -> p (a c)").bitcast(I32), 0)
+        nc.vector.memset(wu_sc[:].bitcast(I32), 0)
+        nc.vector.memset(v_sc[1][:].bitcast(I32), 0)
+        nc.vector.memset(warm[:], 0.0)
+        nc.scalar.activation(out=warm[:], in_=warm[:], func=ACT.Sigmoid)
+
+        wd_raw = sb("wd_raw", [P, KP, 2 * H], U8)
+        nc.sync.dma_start(offs_sb[:], offs)
+        nc.sync.dma_start(offs2_sb[:], offs2)
+        nc.sync.dma_start(out=wd_raw[:].bitcast(I32), in_=wd_words.rearrange("a p c -> p a c").bitcast(I32))
+        for q in range(4):
+            nc.sync.dma_start(out=tab_sc[32 * q : 32 * q + 8, :].bitcast(I32), in_=tab_scales[:, 4 * q : 4 * q + 4, :].bitcast(I32))
+        make_identity(nc, ident[:])
+
+        tab = [sb("tab%d" % a, [P, T], I32) for a in range(KP)]
+        uses_raw = [sb("uses_raw%d" % a, [P, PACK, M], F32) for a in range(KP)]
+        wgt_sb = sb("wgt_sb", [P, M], F32)
+        wu = [sb("wu%d" % b, [P, KP, PASS], I32) for b in range(RP)]
+        old_sb = [sb("old%d" % b, [P, PACK, M], F32) for b in range(RP)]
+        wo_raw = [sb("wo_raw%d" % b, [P, PACK, N], F32) for b in range(RP)]
+
+        def rows(x, a):
+            return x[PASS * a : PASS * (a + 1), :].rearrange("(p i) c -> p i c", i=PACK)
+
+        def load_tab(a):
+            nc.sync.dma_start(out=tab[a][:], in_=tab_words[a].rearrange("p t i -> p (t i)").bitcast(I32))
+
+        def load_wu(b):
+            src = wu_words.rearrange("a p c i -> p a (c i)")[:, :, PACK * PASS * b : PACK * PASS * (b + 1)]
+            nc.sync.dma_start(out=wu[b][:], in_=src.bitcast(I32))
+
+        load_tab(0)
+        for q in range(4):
+            nc.sync.dma_start(
+                out=wd_sc[32 * q : 32 * q + 4, :, :].bitcast(I32),
+                in_=wd_scales[:, 4 * q : 4 * q + 4, :].rearrange("a r c -> r a c").bitcast(I32),
+            )
+        nc.sync.dma_start(out=uses_raw[0][:], in_=rows(uses, 0))
+        load_tab(1)
+        nc.sync.dma_start(out=wgt_sb[:], in_=wgt)
+        nc.sync.dma_start(out=uses_raw[1][:], in_=rows(uses, 1))
+        for q in range(4):
+            nc.sync.dma_start(out=wu_sc[32 * q : 32 * q + 8, :].bitcast(I32), in_=wu_scales[:, 4 * q : 4 * q + 4, :].bitcast(I32))
+        load_wu(0)
+        nc.sync.dma_start(out=old_sb[0][:], in_=rows(old, 0))
+        load_wu(1)
+        nc.sync.dma_start(out=old_sb[1][:], in_=rows(old, 1))
+        for b in range(RP):
+            nc.sync.dma_start(out=wo_raw[b][:], in_=rows(wo, b))
+
+        def interleaved(t):
+            return t.rearrange("p (c j) i -> p c i j", j=4)
+
+        def planar(t):
+            return t.rearrange("p i (c j) -> p c i j", j=4)
+
+        v = [[sb("v%d_%d" % (a, s), [P, BANK], U32) for s in range(SH)] for a in range(KP)]
+        cols = BANK // 16
+
+        def gather_words(a, s):
+            nc.vector.tensor_copy(v[a][s][:], tab[a][:].bitcast(U32).indirect(offs_sb[:, cols * s : cols * (s + 1)]))
+
+
+        wd = [sb("wd%d" % b, [P, KP, 2 * PASS], U8) for b in range(RP)]
+        wd_s = [sb("wd_s%d" % b, [P, KP, PASS], U8) for b in range(RP)]
+
+        def permute_wd_words(b):
+            nc.vector.tensor_copy(
+                out=wd[b][:].bitcast(U16).rearrange("p a (i m) -> p a i m", i=PACK),
+                in_=wd_raw[:].bitcast(U16)[:, :, PASS * b : PASS * (b + 1)].rearrange("p a (m i) -> p a i m", i=PACK),
+            )
+
+        def permute_wd_scales(b):
+            nc.vector.tensor_copy(
+                out=wd_s[b][:].rearrange("p a (i m) -> p a i m", i=PACK),
+                in_=wd_sc[:, :, PASS * b : PASS * (b + 1)].rearrange("p a (m i) -> p a i m", i=PACK),
+            )
+
+        permute_wd_words(0)
+        permute_wd_words(1)
+        nc.vector.tensor_copy(v_sc[0][:], tab_sc[:].indirect(offs_sb[:]))
+        nc.gpsimd.dma_start(out=v_sc[1][0:112, :].bitcast(I32), in_=v_sc[0][4:116, :].bitcast(I32))
+        gather_words(0, 0)
+        gather_words(0, 1)
+        permute_wd_scales(0)
+        permute_wd_scales(1)
+        gather_words(1, 0)
+        gather_words(1, 1)
+
+        uses_bf = [sb("uses_bf%d" % a, [P, M, PACK], BF16) for a in range(KP)]
+        u_codes = [sb("u_codes%d" % a, [P, M], U32) for a in range(KP)]
+        u_sc = [sb("u_sc%d" % a, [P, M], U8) for a in range(KP)]
+        neg_wgt = sb("neg_wgt", [P, M], F32)
+
+        def quantize(codes, scales, src):
+            nc.vector.quantize_mx(out=codes.bitcast(FP8X4), scales=scales, in_=src)
+
+        nc.scalar.copy(out=interleaved(uses_bf[0][:]), in_=planar(uses_raw[0][:]))
+        nc.gpsimd.tensor_scalar(out=neg_wgt[:], in0=wgt_sb[:], scalar1=-1.0, scalar2=0.0, op0=ALU.mult, op1=ALU.add)
+        nc.vector.tensor_copy(out=interleaved(uses_bf[1][:]), in_=planar(uses_raw[1][:]))
+        for a in range(KP):
+            quantize(u_codes[a][:], u_sc[a][:], uses_bf[a][:].rearrange("p m i -> p (m i)"))
+
+        h = {}
+        xneg = {}
+        gate_t = [sb("gate_t%d" % b, [P, PACK, MT, P], F32) for b in range(RP)]
+        e_t = {}
+        e_banks = {}
+
+        def mm_bank():
+            return psum.tile([P, BANK], F32, name="mm", tag="mm", bufs=4)
+
+        def make_h(b, i, halves=(0, 1)):
+            if 0 in halves:
+                if (b, i) == (0, 0):
+                    h[b, i] = sb("h_first", [P, S], F32, "uses_raw0")
+                else:
+                    h[b, i] = keep.tile([P, S], F32, name="h", tag="h", bufs=3, align_bytes=64)
+            for s in halves:
+                bank = mm_bank()
+                for a in range(KP):
+                    nc.tensor.matmul_mx(
+                        out=bank[:],
+                        lhsT=wd[b][:, a, 2 * P * i : 2 * P * (i + 1)].bitcast(FP4X4),
+                        lhsT_scale=wd_s[b][:, a, P * i : P * (i + 1)],
+                        rhs=v[a][s][:].bitcast(FP8X4),
+                        rhs_scale=v_sc[a][:, BANK * s : BANK * (s + 1)],
+                        start=(a == 0),
+                        stop=(a == KP - 1),
+                    )
+                nc.scalar.copy(out=h[b, i][:, BANK * s : BANK * (s + 1)], in_=bank[:])
+
+        def make_gate(b):
+            for t in range(MT):
+                bank = mm_bank()
+                for a in range(KP):
+                    nc.tensor.matmul_mx(
+                        out=bank[:],
+                        lhsT=u_codes[a][:, P * t : P * (t + 1)].bitcast(FP8X4),
+                        lhsT_scale=u_sc[a][:, P * t : P * (t + 1)],
+                        rhs=wu[b][:, a, :].bitcast(FP8X4),
+                        rhs_scale=wu_sc[4 * a : P, PASS * b : PASS * (b + 1)],
+                        start=(a == 0),
+                        stop=(a == KP - 1),
+                    )
+                nc.scalar.activation(
+                    out=gate_t[b][:, :, t, :], in_=bank[:].rearrange("q (p i) -> q i p", i=PACK), func=ACT.Sigmoid
+                )
+
+        def pick(b, i):
+            xneg[b, i] = keep.tile([P, M], F32, name="xneg", tag="xneg", bufs=2, align_bytes=64)
+            nc.vector.tensor_tensor(xneg[b, i][:], h[b, i][:].indirect(offs2_sb[:]), neg_wgt[:], ALU.mult)
+
+        def gated_difference(b, i):
+            d = psum.tile([P, MT, P], F32, name="d", tag="d", bufs=2)
+            for t in range(MT):
+                ms = slice(P * t, P * (t + 1))
+                nc.tensor.matmul(out=d[:, t, :], lhsT=old_sb[b][:, i, ms], rhs=ident[:], is_transpose=True, start=True, stop=False)
+                nc.tensor.matmul(out=d[:, t, :], lhsT=xneg[b, i][:, ms], rhs=ident[:], is_transpose=True, start=False, stop=True)
+            e_t[b, i] = sb("e_t%d_%d" % (b, i), [P, MT, P], F32)
+            nc.vector.tensor_tensor(e_t[b, i][:], d[:], gate_t[b][:, i, :, :], ALU.mult)
+
+        def turn_back(b, t):
+            e_banks[b, t] = psum.tile([P, PACK, P], F32, name="e", tag="e", bufs=2)
+            for i in range(PACK):
+                nc.tensor.transpose(e_banks[b, t][:, i, :], e_t[b, i][:, t, :], ident[:])
+
+        z_codes = {}
+        z_sc = {}
+        z_bf = {}
+
+        def make_z(b, t):
+            z_bf[b, t] = sb("z_bf%d_%d" % (b, t), [P, P, PACK], BF16)
+            nc.vector.tensor_tensor(
+                interleaved(z_bf[b, t][:]), planar(old_sb[b][:, :, P * t : P * (t + 1)]), planar(e_banks[b, t][:]), ALU.subtract
+            )
+
+        def quantize_z(b, t):
+            z_codes[b, t] = sb("z_codes%d_%d" % (b, t), [P, P], U32)
+            z_sc[b, t] = sb("z_sc%d_%d" % (b, t), [P, P], U8)
+            quantize(z_codes[b, t][:], z_sc[b, t][:], z_bf[b, t][:].rearrange("p m i -> p (m i)"))
+
+        wo_bf = sb("wo_bf", [P, RP * N, PACK], BF16)
+        wo_codes = sb("wo_codes", [P, RP * N], U32)
+        wo_sc = sb("wo_sc", [P, RP * N], U8)
+
+        def cast_wo(b):
+            nc.scalar.copy(out=interleaved(wo_bf[:, N * b : N * (b + 1), :]), in_=planar(wo_raw[b][:]))
+
+        def quantize_wo():
+            for c0, c1 in ((0, 512), (512, RP * N)):
+                quantize(wo_codes[:, c0:c1], wo_sc[:, c0:c1], wo_bf[:, c0:c1, :].rearrange("p n i -> p (n i)"))
+
+        def project(t):
+            bank = mm_bank()
+            for n in range(NT):
+                for b in range(RP):
+                    ns = slice(N * b + P * n, N * b + P * (n + 1))
+                    nc.tensor.matmul_mx(
+                        out=bank[:, P * n : P * (n + 1)],
+                        lhsT=wo_codes[:, ns].bitcast(FP8X4),
+                        lhsT_scale=wo_sc[:, ns],
+                        rhs=z_codes[b, t][:].bitcast(FP8X4),
+                        rhs_scale=z_sc[b, t][:],
+                        start=(b == 0),
+                        stop=(b == RP - 1),
+                    )
+            res = sb("res%d" % t, [P, NT, P], F32)
+            nc.scalar.copy(out=res[:].rearrange("p n m -> p (n m)"), in_=bank[:, 0 : NT * P])
+            nc.sync.dma_start(out=out[:, P * t : P * (t + 1)].rearrange("(n p) m -> p n m", p=P), in_=res[:])
+
+        tiles = [(b, i) for b in range(RP) for i in range(PACK)]
+        make_h(0, 0, (0,))
+        make_h(0, 1, (0,))
+        make_h(0, 0, (1,))
+        make_h(0, 1, (1,))
+        make_gate(0)
+        make_h(0, 2)
+        for j in range(len(tiles) + 1):
+            if j + 3 < len(tiles):
+                make_h(*tiles[j + 3])
+            if j == 1:
+                make_gate(1)
+            if j < len(tiles):
+                pick(*tiles[j])
+            if j >= 1:
+                gated_difference(*tiles[j - 1])
+            if PACK + 1 <= j:
+                turn_back(0, j - PACK - 1)
+                make_z(0, j - PACK - 1)
+            if PACK + 2 <= j:
+                quantize_z(0, j - PACK - 2)
+            if j == PACK + 1:
+                for b in range(RP):
+                    cast_wo(b)
+            if j == PACK + 3:
+                quantize_wo()
+        quantize_z(0, MT - 1)
+        for t in range(MT + 1):
+            if t < MT:
+                turn_back(1, t)
+                make_z(1, t)
+            if t >= 1:
+                quantize_z(1, t - 1)
+                project(t - 1)

@@ -1,7 +1,6 @@
 from contextlib import ExitStack
 
 import concourse.mybir as mybir
-from concourse.masks import make_identity
 
 T, S, M, K, H, N = 2048, 1024, 512, 1024, 1024, 384
 FLOPS = 2 * (K * H * S + K * H * M + H * N * M)
@@ -21,6 +20,7 @@ P = 128
 PACK = 4
 PASS = P * PACK
 BANK = 512
+RUN = 8
 KP = K // PASS
 RP = H // PASS
 MT = M // P
@@ -45,7 +45,6 @@ def tile_list_reaching_names_kernel(
         wd_sc = sb("wd_sc", [P, KP, H], U8)
         wu_sc = sb("wu_sc", [P, H], U8)
         v_sc = [sb("v_sc%d" % a, [P, S], U8) for a in range(KP)]
-        ident = sb("ident", [P, P], F32)
         warm = sb("warm", [P, 1], F32)
 
         nc.vector.memset(tab_sc[:].bitcast(I32), 0)
@@ -61,7 +60,6 @@ def tile_list_reaching_names_kernel(
         nc.sync.dma_start(out=wd_raw[:].bitcast(I32), in_=wd_words.rearrange("a p c -> p a c").bitcast(I32))
         for q in range(4):
             nc.sync.dma_start(out=tab_sc[32 * q : 32 * q + 8, :].bitcast(I32), in_=tab_scales[:, 4 * q : 4 * q + 4, :].bitcast(I32))
-        make_identity(nc, ident[:])
 
         tab = [sb("tab%d" % a, [P, T], I32) for a in range(KP)]
         uses_raw = [sb("uses_raw%d" % a, [P, PACK, M], F32) for a in range(KP)]
@@ -72,6 +70,11 @@ def tile_list_reaching_names_kernel(
 
         def rows(x, a):
             return x[PASS * a : PASS * (a + 1), :].rearrange("(p i) c -> p i c", i=PACK)
+
+        def load_channels(dst, x, b):
+            blocks = x[PASS * b : PASS * (b + 1), :].rearrange("(q i e) c -> i q e c", i=PACK, e=RUN)
+            for i in range(PACK):
+                nc.sync.dma_start(out=dst[:, i, :], in_=blocks[i])
 
         def load_tab(a):
             nc.sync.dma_start(out=tab[a][:], in_=tab_words[a].rearrange("p t i -> p (t i)").bitcast(I32))
@@ -89,15 +92,15 @@ def tile_list_reaching_names_kernel(
         nc.sync.dma_start(out=uses_raw[0][:], in_=rows(uses, 0))
         load_tab(1)
         nc.sync.dma_start(out=wgt_sb[:], in_=wgt)
+        load_channels(old_sb[0], old, 0)
         nc.sync.dma_start(out=uses_raw[1][:], in_=rows(uses, 1))
         for q in range(4):
             nc.sync.dma_start(out=wu_sc[32 * q : 32 * q + 8, :].bitcast(I32), in_=wu_scales[:, 4 * q : 4 * q + 4, :].bitcast(I32))
         load_wu(0)
-        nc.sync.dma_start(out=old_sb[0][:], in_=rows(old, 0))
         load_wu(1)
-        nc.sync.dma_start(out=old_sb[1][:], in_=rows(old, 1))
+        load_channels(old_sb[1], old, 1)
         for b in range(RP):
-            nc.sync.dma_start(out=wo_raw[b][:], in_=rows(wo, b))
+            load_channels(wo_raw[b], wo, b)
 
         def interleaved(t):
             return t.rearrange("p (c j) i -> p c i j", j=4)
@@ -115,22 +118,23 @@ def tile_list_reaching_names_kernel(
         wd = [sb("wd%d" % b, [P, KP, 2 * PASS], U8) for b in range(RP)]
         wd_s = [sb("wd_s%d" % b, [P, KP, PASS], U8) for b in range(RP)]
 
-        def permute_wd_words(b):
+        def permute(dst, src):
+            words = dst.shape[2] // (PASS // RUN)
             nc.vector.tensor_copy(
-                out=wd[b][:].bitcast(U16).rearrange("p a (i m) -> p a i m", i=PACK),
-                in_=wd_raw[:].bitcast(U16)[:, :, PASS * b : PASS * (b + 1)].rearrange("p a (m i) -> p a i m", i=PACK),
+                out=dst.rearrange("p a (i q w) -> p a i q w", i=PACK, w=words),
+                in_=src.rearrange("p a (q i w) -> p a i q w", i=PACK, w=words),
             )
 
+        def permute_wd_words(b):
+            permute(wd[b][:].bitcast(I32), wd_raw[:, :, 2 * PASS * b : 2 * PASS * (b + 1)].bitcast(I32))
+
         def permute_wd_scales(b):
-            nc.vector.tensor_copy(
-                out=wd_s[b][:].rearrange("p a (i m) -> p a i m", i=PACK),
-                in_=wd_sc[:, :, PASS * b : PASS * (b + 1)].rearrange("p a (m i) -> p a i m", i=PACK),
-            )
+            permute(wd_s[b][:].bitcast(I32), wd_sc[:, :, PASS * b : PASS * (b + 1)].bitcast(I32))
 
         permute_wd_words(0)
         permute_wd_words(1)
         nc.vector.tensor_copy(v_sc[0][:], tab_sc[:].indirect(offs_sb[:]))
-        nc.gpsimd.dma_start(out=v_sc[1][0:112, :].bitcast(I32), in_=v_sc[0][4:116, :].bitcast(I32))
+        nc.scalar.dma_start(out=v_sc[1][0:112, :].bitcast(I32), in_=v_sc[0][4:116, :].bitcast(I32))
         gather_words(0, 0)
         gather_words(0, 1)
         permute_wd_scales(0)
@@ -141,32 +145,38 @@ def tile_list_reaching_names_kernel(
         uses_bf = [sb("uses_bf%d" % a, [P, M, PACK], BF16) for a in range(KP)]
         u_codes = [sb("u_codes%d" % a, [P, M], U32) for a in range(KP)]
         u_sc = [sb("u_sc%d" % a, [P, M], U8) for a in range(KP)]
-        neg_wgt = sb("neg_wgt", [P, M], F32)
 
         def quantize(codes, scales, src):
             nc.vector.quantize_mx(out=codes.bitcast(FP8X4), scales=scales, in_=src)
 
-        nc.scalar.copy(out=interleaved(uses_bf[0][:]), in_=planar(uses_raw[0][:]))
-        nc.gpsimd.tensor_scalar(out=neg_wgt[:], in0=wgt_sb[:], scalar1=-1.0, scalar2=0.0, op0=ALU.mult, op1=ALU.add)
-        nc.vector.tensor_copy(out=interleaved(uses_bf[1][:]), in_=planar(uses_raw[1][:]))
-        for a in range(KP):
+        def cast_uses(a):
+            nc.scalar.copy(out=interleaved(uses_bf[a][:]), in_=planar(uses_raw[a][:]))
+
+        def quantize_uses(a):
             quantize(u_codes[a][:], u_sc[a][:], uses_bf[a][:].rearrange("p m i -> p (m i)"))
 
+        wu_p = [sb("wu_p%d" % b, [P, KP, PASS], I32) for b in range(RP)]
+        wu_s = sb("wu_s", [P, H], U8)
+
+        def permute_wu(b):
+            permute(wu_p[b][:], wu[b][:])
+
+        def permute_wu_scales():
+            permute(
+                wu_s[:].bitcast(I32).rearrange("p (b c) -> p b c", b=RP), wu_sc[:].bitcast(I32).rearrange("p (b c) -> p b c", b=RP)
+            )
+
         h = {}
-        xneg = {}
-        gate_t = [sb("gate_t%d" % b, [P, PACK, MT, P], F32) for b in range(RP)]
-        e_t = {}
-        e_banks = {}
+        x = {}
+        gate = {}
+        d = [sb("d%d" % b, [P, PACK, M], F32) for b in range(RP)]
 
         def mm_bank():
-            return psum.tile([P, BANK], F32, name="mm", tag="mm", bufs=4)
+            return psum.tile([P, BANK], F32, name="mm", tag="mm", bufs=8)
 
         def make_h(b, i, halves=(0, 1)):
             if 0 in halves:
-                if (b, i) == (0, 0):
-                    h[b, i] = sb("h_first", [P, S], F32, "uses_raw0")
-                else:
-                    h[b, i] = keep.tile([P, S], F32, name="h", tag="h", bufs=3, align_bytes=64)
+                h[b, i] = sb("h%d_%d" % (b, i), [P, S], F32, "uses_raw0" if (b, i) == (0, 0) else None)
             for s in halves:
                 bank = mm_bank()
                 for a in range(KP):
@@ -181,50 +191,39 @@ def tile_list_reaching_names_kernel(
                     )
                 nc.scalar.copy(out=h[b, i][:, BANK * s : BANK * (s + 1)], in_=bank[:])
 
-        def make_gate(b):
-            for t in range(MT):
-                bank = mm_bank()
-                for a in range(KP):
-                    nc.tensor.matmul_mx(
-                        out=bank[:],
-                        lhsT=u_codes[a][:, P * t : P * (t + 1)].bitcast(FP8X4),
-                        lhsT_scale=u_sc[a][:, P * t : P * (t + 1)],
-                        rhs=wu[b][:, a, :].bitcast(FP8X4),
-                        rhs_scale=wu_sc[4 * a : P, PASS * b : PASS * (b + 1)],
-                        start=(a == 0),
-                        stop=(a == KP - 1),
-                    )
-                nc.scalar.activation(
-                    out=gate_t[b][:, :, t, :], in_=bank[:].rearrange("q (p i) -> q i p", i=PACK), func=ACT.Sigmoid
+        def make_gate(b, i):
+            bank = mm_bank()
+            for a in range(KP):
+                nc.tensor.matmul_mx(
+                    out=bank[:],
+                    lhsT=wu_p[b][:, a, P * i : P * (i + 1)].bitcast(FP8X4),
+                    lhsT_scale=wu_s[4 * a : P, PASS * b + P * i : PASS * b + P * (i + 1)],
+                    rhs=u_codes[a][:].bitcast(FP8X4),
+                    rhs_scale=u_sc[a][:],
+                    start=(a == 0),
+                    stop=(a == KP - 1),
                 )
+            gate[b, i] = sb("gate%d_%d" % (b, i), [P, M], F32)
+            nc.scalar.activation(out=gate[b, i][:], in_=bank[:], func=ACT.Sigmoid)
 
         def pick(b, i):
-            xneg[b, i] = keep.tile([P, M], F32, name="xneg", tag="xneg", bufs=2, align_bytes=64)
-            nc.vector.tensor_tensor(xneg[b, i][:], h[b, i][:].indirect(offs2_sb[:]), neg_wgt[:], ALU.mult)
+            x[b, i] = keep.tile([P, M], F32, name="x", tag="x", bufs=4, align_bytes=64)
+            nc.vector.tensor_tensor(x[b, i][:], h[b, i][:].indirect(offs2_sb[:]), wgt_sb[:], ALU.mult)
 
-        def gated_difference(b, i):
-            d = psum.tile([P, MT, P], F32, name="d", tag="d", bufs=2)
-            for t in range(MT):
-                ms = slice(P * t, P * (t + 1))
-                nc.tensor.matmul(out=d[:, t, :], lhsT=old_sb[b][:, i, ms], rhs=ident[:], is_transpose=True, start=True, stop=False)
-                nc.tensor.matmul(out=d[:, t, :], lhsT=xneg[b, i][:, ms], rhs=ident[:], is_transpose=True, start=False, stop=True)
-            e_t[b, i] = sb("e_t%d_%d" % (b, i), [P, MT, P], F32)
-            nc.vector.tensor_tensor(e_t[b, i][:], d[:], gate_t[b][:, i, :, :], ALU.mult)
+        def difference(b, i):
+            nc.vector.tensor_tensor(d[b][:, i, :], x[b, i][:], old_sb[b][:, i, :], ALU.subtract)
 
-        def turn_back(b, t):
-            e_banks[b, t] = psum.tile([P, PACK, P], F32, name="e", tag="e", bufs=2)
-            for i in range(PACK):
-                nc.tensor.transpose(e_banks[b, t][:, i, :], e_t[b, i][:, t, :], ident[:])
+        def gated(b, i):
+            nc.vector.tensor_tensor(d[b][:, i, :], d[b][:, i, :], gate[b, i][:], ALU.mult)
 
         z_codes = {}
         z_sc = {}
         z_bf = {}
 
         def make_z(b, t):
+            ms = slice(P * t, P * (t + 1))
             z_bf[b, t] = sb("z_bf%d_%d" % (b, t), [P, P, PACK], BF16)
-            nc.vector.tensor_tensor(
-                interleaved(z_bf[b, t][:]), planar(old_sb[b][:, :, P * t : P * (t + 1)]), planar(e_banks[b, t][:]), ALU.subtract
-            )
+            nc.vector.tensor_tensor(interleaved(z_bf[b, t][:]), planar(d[b][:, :, ms]), planar(old_sb[b][:, :, ms]), ALU.add)
 
         def quantize_z(b, t):
             z_codes[b, t] = sb("z_codes%d_%d" % (b, t), [P, P], U32)
@@ -242,55 +241,68 @@ def tile_list_reaching_names_kernel(
             for c0, c1 in ((0, 512), (512, RP * N)):
                 quantize(wo_codes[:, c0:c1], wo_sc[:, c0:c1], wo_bf[:, c0:c1, :].rearrange("p n i -> p (n i)"))
 
-        def project(t):
-            bank = mm_bank()
+        out_bank = {}
+
+        def project(b, t):
+            if b == 0:
+                out_bank[t] = mm_bank()
             for n in range(NT):
-                for b in range(RP):
-                    ns = slice(N * b + P * n, N * b + P * (n + 1))
-                    nc.tensor.matmul_mx(
-                        out=bank[:, P * n : P * (n + 1)],
-                        lhsT=wo_codes[:, ns].bitcast(FP8X4),
-                        lhsT_scale=wo_sc[:, ns],
-                        rhs=z_codes[b, t][:].bitcast(FP8X4),
-                        rhs_scale=z_sc[b, t][:],
-                        start=(b == 0),
-                        stop=(b == RP - 1),
-                    )
+                ns = slice(N * b + P * n, N * b + P * (n + 1))
+                nc.tensor.matmul_mx(
+                    out=out_bank[t][:, P * n : P * (n + 1)],
+                    lhsT=wo_codes[:, ns].bitcast(FP8X4),
+                    lhsT_scale=wo_sc[:, ns],
+                    rhs=z_codes[b, t][:].bitcast(FP8X4),
+                    rhs_scale=z_sc[b, t][:],
+                    start=(b == 0 and n == 0),
+                    stop=(b == RP - 1 and n == NT - 1),
+                )
+
+        def store(t):
             res = sb("res%d" % t, [P, NT, P], F32)
-            nc.scalar.copy(out=res[:].rearrange("p n m -> p (n m)"), in_=bank[:, 0 : NT * P])
+            nc.scalar.copy(out=res[:].rearrange("p n m -> p (n m)"), in_=out_bank[t][:, 0 : NT * P])
             nc.sync.dma_start(out=out[:, P * t : P * (t + 1)].rearrange("(n p) m -> p n m", p=P), in_=res[:])
 
         tiles = [(b, i) for b in range(RP) for i in range(PACK)]
+        cast_uses(0)
+        quantize_uses(0)
         make_h(0, 0, (0,))
         make_h(0, 1, (0,))
         make_h(0, 0, (1,))
         make_h(0, 1, (1,))
-        make_gate(0)
-        make_h(0, 2)
         for j in range(len(tiles) + 1):
-            if j + 3 < len(tiles):
-                make_h(*tiles[j + 3])
-            if j == 1:
-                make_gate(1)
+            if j + 2 < len(tiles):
+                make_h(*tiles[j + 2])
             if j < len(tiles):
                 pick(*tiles[j])
             if j >= 1:
-                gated_difference(*tiles[j - 1])
-            if PACK + 1 <= j:
-                turn_back(0, j - PACK - 1)
-                make_z(0, j - PACK - 1)
-            if PACK + 2 <= j:
-                quantize_z(0, j - PACK - 2)
-            if j == PACK + 1:
-                for b in range(RP):
-                    cast_wo(b)
-            if j == PACK + 3:
+                difference(*tiles[j - 1])
+            if j == 1:
+                cast_uses(1)
+                quantize_uses(1)
+                permute_wu_scales()
+            if j in (2, 4):
+                permute_wu(j // 2 - 1)
+        for b in range(RP):
+            for i in range(PACK):
+                make_gate(b, i)
+        for b in range(RP):
+            cast_wo(b)
+        for b in range(RP):
+            for i in range(PACK):
+                gated(b, i)
+            if b == 0:
+                for t in range(MT):
+                    make_z(0, t)
+                for t in range(MT):
+                    quantize_z(0, t)
                 quantize_wo()
-        quantize_z(0, MT - 1)
+                for t in range(MT):
+                    project(0, t)
         for t in range(MT + 1):
             if t < MT:
-                turn_back(1, t)
                 make_z(1, t)
             if t >= 1:
                 quantize_z(1, t - 1)
-                project(t - 1)
+                project(1, t - 1)
+                store(t - 1)

@@ -1,6 +1,7 @@
 from contextlib import ExitStack
 
 import concourse.mybir as mybir
+from concourse.masks import make_identity
 
 T, S, M, K, H, N = 2048, 1024, 512, 1024, 1024, 384
 FLOPS = 2 * (K * H * S + K * H * M + H * N * M)
@@ -50,16 +51,18 @@ def tile_list_reaching_names_kernel(
         nc.vector.memset(tab_sc[:].bitcast(I32), 0)
         nc.vector.memset(wd_sc[:].rearrange("p a c -> p (a c)").bitcast(I32), 0)
         nc.vector.memset(wu_sc[:].bitcast(I32), 0)
-        nc.vector.memset(v_sc[1][:].bitcast(I32), 0)
         nc.vector.memset(warm[:], 0.0)
         nc.scalar.activation(out=warm[:], in_=warm[:], func=ACT.Sigmoid)
 
         wd_raw = sb("wd_raw", [P, KP, 2 * H], U8)
         nc.sync.dma_start(offs_sb[:], offs)
-        nc.sync.dma_start(offs2_sb[:], offs2)
         nc.sync.dma_start(out=wd_raw[:].bitcast(I32), in_=wd_words.rearrange("a p c -> p a c").bitcast(I32))
-        for q in range(4):
+        for q in range(2):
             nc.sync.dma_start(out=tab_sc[32 * q : 32 * q + 8, :].bitcast(I32), in_=tab_scales[:, 4 * q : 4 * q + 4, :].bitcast(I32))
+        for q in range(2, 4):
+            for a in range(KP):
+                row = 32 * q - 4 * a
+                nc.sync.dma_start(out=tab_sc[row : row + 4, :].bitcast(I32), in_=tab_scales[a, 4 * q : 4 * q + 4, :].bitcast(I32))
 
         tab = [sb("tab%d" % a, [P, T], I32) for a in range(KP)]
         uses_raw = [sb("uses_raw%d" % a, [P, PACK, M], F32) for a in range(KP)]
@@ -89,24 +92,25 @@ def tile_list_reaching_names_kernel(
                 out=wd_sc[32 * q : 32 * q + 4, :, :].bitcast(I32),
                 in_=wd_scales[:, 4 * q : 4 * q + 4, :].rearrange("a r c -> r a c").bitcast(I32),
             )
-        nc.sync.dma_start(out=uses_raw[0][:], in_=rows(uses, 0))
         load_tab(1)
+        nc.sync.dma_start(out=uses_raw[0][:], in_=rows(uses, 0))
         nc.sync.dma_start(out=wgt_sb[:], in_=wgt)
-        load_channels(old_sb[0], old, 0)
+        nc.sync.dma_start(offs2_sb[:], offs2)
         nc.sync.dma_start(out=uses_raw[1][:], in_=rows(uses, 1))
+        load_channels(old_sb[0], old, 0)
         for q in range(4):
             nc.sync.dma_start(out=wu_sc[32 * q : 32 * q + 8, :].bitcast(I32), in_=wu_scales[:, 4 * q : 4 * q + 4, :].bitcast(I32))
         load_wu(0)
-        load_wu(1)
         load_channels(old_sb[1], old, 1)
+        load_wu(1)
         for b in range(RP):
             load_channels(wo_raw[b], wo, b)
 
         def interleaved(t):
-            return t.rearrange("p (c j) i -> p c i j", j=4)
+            return t.rearrange("p (c j) i -> p c i j", j=2)
 
         def planar(t):
-            return t.rearrange("p i (c j) -> p c i j", j=4)
+            return t.rearrange("p i (c j) -> p c i j", j=2)
 
         v = [[sb("v%d_%d" % (a, s), [P, BANK], U32) for s in range(SH)] for a in range(KP)]
         cols = BANK // 16
@@ -131,16 +135,17 @@ def tile_list_reaching_names_kernel(
         def permute_wd_scales(b):
             permute(wd_s[b][:].bitcast(I32), wd_sc[:, :, PASS * b : PASS * (b + 1)].bitcast(I32))
 
-        permute_wd_words(0)
-        permute_wd_words(1)
+        for b in range(RP):
+            permute_wd_words(b)
         nc.vector.tensor_copy(v_sc[0][:], tab_sc[:].indirect(offs_sb[:]))
-        nc.scalar.dma_start(out=v_sc[1][0:112, :].bitcast(I32), in_=v_sc[0][4:116, :].bitcast(I32))
+        nc.scalar.dma_start(out=v_sc[1][0:64, :].bitcast(I32), in_=v_sc[0][4:68, :].bitcast(I32))
+        nc.scalar.dma_start(out=v_sc[1][64:P, :].bitcast(I32), in_=v_sc[0][60:124, :].bitcast(I32))
         gather_words(0, 0)
         gather_words(0, 1)
         permute_wd_scales(0)
-        permute_wd_scales(1)
         gather_words(1, 0)
         gather_words(1, 1)
+        permute_wd_scales(1)
 
         uses_bf = [sb("uses_bf%d" % a, [P, M, PACK], BF16) for a in range(KP)]
         u_codes = [sb("u_codes%d" % a, [P, M], U32) for a in range(KP)]
@@ -150,33 +155,34 @@ def tile_list_reaching_names_kernel(
             nc.vector.quantize_mx(out=codes.bitcast(FP8X4), scales=scales, in_=src)
 
         def cast_uses(a):
-            nc.scalar.copy(out=interleaved(uses_bf[a][:]), in_=planar(uses_raw[a][:]))
+            split = M if a == 0 else M // 2
+            nc.scalar.copy(out=interleaved(uses_bf[a][:, 0:split, :]), in_=planar(uses_raw[a][:, :, 0:split]))
+            if split < M:
+                nc.vector.tensor_copy(out=interleaved(uses_bf[a][:, split:M, :]), in_=planar(uses_raw[a][:, :, split:M]))
 
         def quantize_uses(a):
             quantize(u_codes[a][:], u_sc[a][:], uses_bf[a][:].rearrange("p m i -> p (m i)"))
 
-        wu_p = [sb("wu_p%d" % b, [P, KP, PASS], I32) for b in range(RP)]
-        wu_s = sb("wu_s", [P, H], U8)
-
-        def permute_wu(b):
-            permute(wu_p[b][:], wu[b][:])
-
-        def permute_wu_scales():
-            permute(
-                wu_s[:].bitcast(I32).rearrange("p (b c) -> p b c", b=RP), wu_sc[:].bitcast(I32).rearrange("p (b c) -> p b c", b=RP)
-            )
+        ident = sb("ident", [P, P], F32)
+        neg_wgt = sb("neg_wgt", [P, M], F32)
+        make_identity(nc, ident[:])
+        nc.gpsimd.tensor_scalar(out=neg_wgt[:], in0=wgt_sb[:], scalar1=-1.0, scalar2=0.0, op0=ALU.mult, op1=ALU.add)
 
         h = {}
         x = {}
-        gate = {}
-        d = [sb("d%d" % b, [P, PACK, M], F32) for b in range(RP)]
+        gate_t = [sb("gate_t%d" % b, [P, PACK, MT, P], F32) for b in range(RP)]
+        d_t = {}
+        e_t = {}
+
+        def turn_bank():
+            return psum.tile([P, PACK, P], F32, name="turn", tag="turn", bufs=4)
 
         def mm_bank():
-            return psum.tile([P, BANK], F32, name="mm", tag="mm", bufs=8)
+            return psum.tile([P, BANK], F32, name="mm", tag="mm", bufs=4)
 
         def make_h(b, i, halves=(0, 1)):
             if 0 in halves:
-                h[b, i] = sb("h%d_%d" % (b, i), [P, S], F32, "uses_raw0" if (b, i) == (0, 0) else None)
+                h[b, i] = sb("h%d_%d" % (b, i), [P, S], F32)
             for s in halves:
                 bank = mm_bank()
                 for a in range(KP):
@@ -189,32 +195,41 @@ def tile_list_reaching_names_kernel(
                         start=(a == 0),
                         stop=(a == KP - 1),
                     )
-                nc.scalar.copy(out=h[b, i][:, BANK * s : BANK * (s + 1)], in_=bank[:])
+                copy = nc.vector.tensor_copy if (b, i, s) == (0, 0, 1) else nc.scalar.copy
+                copy(out=h[b, i][:, BANK * s : BANK * (s + 1)], in_=bank[:])
 
-        def make_gate(b, i):
+        def make_gate(b, t):
             bank = mm_bank()
             for a in range(KP):
                 nc.tensor.matmul_mx(
                     out=bank[:],
-                    lhsT=wu_p[b][:, a, P * i : P * (i + 1)].bitcast(FP8X4),
-                    lhsT_scale=wu_s[4 * a : P, PASS * b + P * i : PASS * b + P * (i + 1)],
-                    rhs=u_codes[a][:].bitcast(FP8X4),
-                    rhs_scale=u_sc[a][:],
+                    lhsT=u_codes[a][:, P * t : P * (t + 1)].bitcast(FP8X4),
+                    lhsT_scale=u_sc[a][:, P * t : P * (t + 1)],
+                    rhs=wu[b][:, a, :].bitcast(FP8X4),
+                    rhs_scale=wu_sc[4 * a : P, PASS * b : PASS * (b + 1)],
                     start=(a == 0),
                     stop=(a == KP - 1),
                 )
-            gate[b, i] = sb("gate%d_%d" % (b, i), [P, M], F32)
-            nc.scalar.activation(out=gate[b, i][:], in_=bank[:], func=ACT.Sigmoid)
+            nc.scalar.activation(
+                out=gate_t[b][:, :, t, :].rearrange("m i (q e) -> m i q e", e=RUN),
+                in_=bank[:].rearrange("m (q i e) -> m i q e", i=PACK, e=RUN),
+                func=ACT.Sigmoid,
+            )
 
         def pick(b, i):
-            x[b, i] = keep.tile([P, M], F32, name="x", tag="x", bufs=4, align_bytes=64)
-            nc.vector.tensor_tensor(x[b, i][:], h[b, i][:].indirect(offs2_sb[:]), wgt_sb[:], ALU.mult)
+            x[b, i] = sb("x%d_%d" % (b, i), [P, M], F32)
+            nc.vector.tensor_tensor(x[b, i][:], h[b, i][:].indirect(offs2_sb[:]), neg_wgt[:], ALU.mult)
 
         def difference(b, i):
-            nc.vector.tensor_tensor(d[b][:, i, :], x[b, i][:], old_sb[b][:, i, :], ALU.subtract)
+            d_t[b, i] = turn_bank()
+            for t in range(MT):
+                ms = slice(P * t, P * (t + 1))
+                nc.tensor.matmul(out=d_t[b, i][:, t, :], lhsT=old_sb[b][:, i, ms], rhs=ident[:], is_transpose=True, start=True, stop=False)
+                nc.tensor.matmul(out=d_t[b, i][:, t, :], lhsT=x[b, i][:, ms], rhs=ident[:], is_transpose=True, start=False, stop=True)
 
         def gated(b, i):
-            nc.vector.tensor_tensor(d[b][:, i, :], d[b][:, i, :], gate[b, i][:], ALU.mult)
+            e_t[b, i] = sb("e_t%d_%d" % (b, i), [P, MT, P], F32)
+            nc.vector.tensor_tensor(e_t[b, i][:], d_t[b, i][:], gate_t[b][:, i, :, :], ALU.mult)
 
         z_codes = {}
         z_sc = {}
@@ -223,7 +238,10 @@ def tile_list_reaching_names_kernel(
         def make_z(b, t):
             ms = slice(P * t, P * (t + 1))
             z_bf[b, t] = sb("z_bf%d_%d" % (b, t), [P, P, PACK], BF16)
-            nc.vector.tensor_tensor(interleaved(z_bf[b, t][:]), planar(d[b][:, :, ms]), planar(old_sb[b][:, :, ms]), ALU.add)
+            e = mm_bank()[:].rearrange("p (i m) -> p i m", i=PACK)
+            for i in range(PACK):
+                nc.tensor.transpose(e[:, i, :], e_t[b, i][:, t, :], ident[:])
+            nc.vector.tensor_tensor(interleaved(z_bf[b, t][:]), planar(old_sb[b][:, :, ms]), planar(e), ALU.subtract)
 
         def quantize_z(b, t):
             z_codes[b, t] = sb("z_codes%d_%d" % (b, t), [P, P], U32)
@@ -245,7 +263,7 @@ def tile_list_reaching_names_kernel(
 
         def project(b, t):
             if b == 0:
-                out_bank[t] = mm_bank()
+                out_bank[t] = turn_bank()[:].rearrange("p i m -> p (i m)")
             for n in range(NT):
                 ns = slice(N * b + P * n, N * b + P * (n + 1))
                 nc.tensor.matmul_mx(
@@ -264,41 +282,36 @@ def tile_list_reaching_names_kernel(
             nc.sync.dma_start(out=out[:, P * t : P * (t + 1)].rearrange("(n p) m -> p n m", p=P), in_=res[:])
 
         tiles = [(b, i) for b in range(RP) for i in range(PACK)]
-        cast_uses(0)
-        quantize_uses(0)
         make_h(0, 0, (0,))
         make_h(0, 1, (0,))
         make_h(0, 0, (1,))
         make_h(0, 1, (1,))
-        for j in range(len(tiles) + 1):
+        for j in range(len(tiles)):
             if j + 2 < len(tiles):
                 make_h(*tiles[j + 2])
-            if j < len(tiles):
-                pick(*tiles[j])
-            if j >= 1:
+            pick(*tiles[j])
+            if 1 <= j <= PACK:
                 difference(*tiles[j - 1])
-            if j == 1:
-                cast_uses(1)
-                quantize_uses(1)
-                permute_wu_scales()
-            if j in (2, 4):
-                permute_wu(j // 2 - 1)
+            if j in (1, 3):
+                cast_uses(j // 2)
+                quantize_uses(j // 2)
         for b in range(RP):
-            for i in range(PACK):
-                make_gate(b, i)
+            for t in range(MT):
+                make_gate(b, t)
         for b in range(RP):
             cast_wo(b)
-        for b in range(RP):
-            for i in range(PACK):
-                gated(b, i)
-            if b == 0:
-                for t in range(MT):
-                    make_z(0, t)
-                for t in range(MT):
-                    quantize_z(0, t)
-                quantize_wo()
-                for t in range(MT):
-                    project(0, t)
+        for i in range(PACK):
+            gated(0, i)
+            difference(1, i)
+        for i in range(PACK):
+            gated(1, i)
+        for t in range(MT):
+            make_z(0, t)
+        for t in range(MT):
+            quantize_z(0, t)
+        quantize_wo()
+        for t in range(MT):
+            project(0, t)
         for t in range(MT + 1):
             if t < MT:
                 make_z(1, t)

@@ -27,6 +27,7 @@ RP = H // PASS
 MT = M // P
 NT = N // P
 SH = S // BANK
+TURNED = (0,)
 
 
 def tile_list_reaching_names_kernel(
@@ -42,37 +43,25 @@ def tile_list_reaching_names_kernel(
 
         offs_sb = keep.tile([P, S // 16], U16, name="offs_sb")
         offs2_sb = keep.tile([P, M // 16], U16, name="offs2_sb")
-        tab_sc = sb("tab_sc", [P, T], U8)
-        wd_sc = sb("wd_sc", [P, KP, H], U8)
-        wu_sc = sb("wu_sc", [P, H], U8)
-        v_sc = [sb("v_sc%d" % a, [P, S], U8) for a in range(KP)]
+        tab_sc = sb("tab_sc", [P, T], U8, tag="early")
+        wd_sc = sb("wd_sc", [P, KP, H], U8, tag="weight_sc")
+        picked_sc = sb("picked_sc", [P, S], U8)
+        v_sc = sb("v_sc", [P, KP, S], U8)
         warm = sb("warm", [P, 1], F32)
 
-        nc.vector.memset(tab_sc[:].bitcast(I32), 0)
-        nc.vector.memset(wd_sc[:].rearrange("p a c -> p (a c)").bitcast(I32), 0)
-        nc.vector.memset(wu_sc[:].bitcast(I32), 0)
+        nc.gpsimd.memset(wd_sc[:].rearrange("p a c -> p (a c)").bitcast(I32), 0)
+        nc.gpsimd.memset(tab_sc[32:64, :].bitcast(I32), 0)
         nc.vector.memset(warm[:], 0.0)
+        nc.vector.memset(tab_sc[64:P, :].bitcast(I32), 0)
+        nc.vector.memset(v_sc[:].rearrange("p a c -> p (a c)").bitcast(I32), 0)
         nc.scalar.activation(out=warm[:], in_=warm[:], func=ACT.Sigmoid)
 
-        wd_raw = sb("wd_raw", [P, KP, 2 * H], U8)
-        nc.sync.dma_start(offs_sb[:], offs)
-        nc.sync.dma_start(out=wd_raw[:].bitcast(I32), in_=wd_words.rearrange("a p c -> p a c").bitcast(I32))
-        for q in range(2):
-            nc.sync.dma_start(out=tab_sc[32 * q : 32 * q + 8, :].bitcast(I32), in_=tab_scales[:, 4 * q : 4 * q + 4, :].bitcast(I32))
-        for q in range(2, 4):
-            for a in range(KP):
-                row = 32 * q - 4 * a
-                nc.sync.dma_start(out=tab_sc[row : row + 4, :].bitcast(I32), in_=tab_scales[a, 4 * q : 4 * q + 4, :].bitcast(I32))
+        wd_raw = {}
+        tab = [sb("tab%d" % a, [P, T], I32, tag="words%d" % a) for a in range(KP)]
 
-        tab = [sb("tab%d" % a, [P, T], I32) for a in range(KP)]
-        uses_raw = [sb("uses_raw%d" % a, [P, PACK, M], F32) for a in range(KP)]
-        wgt_sb = sb("wgt_sb", [P, M], F32)
-        wu = [sb("wu%d" % b, [P, KP, PASS], I32) for b in range(RP)]
-        old_sb = [sb("old%d" % b, [P, PACK, M], F32) for b in range(RP)]
-        wo_raw = [sb("wo_raw%d" % b, [P, PACK, N], F32) for b in range(RP)]
-
-        def rows(x, a):
-            return x[PASS * a : PASS * (a + 1), :].rearrange("(p i) c -> p i c", i=PACK)
+        def load_uses(a):
+            rows = uses[PASS * a : PASS * (a + 1), :].rearrange("(p i) c -> p i c", i=PACK)
+            nc.sync.dma_start(out=uses_raw[a], in_=rows)
 
         def load_channels(dst, x, b):
             blocks = x[PASS * b : PASS * (b + 1), :].rearrange("(q i e) c -> i q e c", i=PACK, e=RUN)
@@ -82,29 +71,38 @@ def tile_list_reaching_names_kernel(
         def load_tab(a):
             nc.sync.dma_start(out=tab[a][:], in_=tab_words[a].rearrange("p t i -> p (t i)").bitcast(I32))
 
+        def load_wd(b):
+            wd_raw[b] = sb("wd_raw%d" % b, [P, KP, 2 * PASS], U8, tag="wd_raw")
+            src = wd_words.rearrange("a p c -> p a c")[:, :, 2 * PASS * b : 2 * PASS * (b + 1)]
+            nc.sync.dma_start(out=wd_raw[b][:].bitcast(I32), in_=src.bitcast(I32))
+
         def load_wu(b):
             src = wu_words.rearrange("a p c i -> p a (c i)")[:, :, PACK * PASS * b : PACK * PASS * (b + 1)]
             nc.sync.dma_start(out=wu[b][:], in_=src.bitcast(I32))
 
+        nc.sync.dma_start(out=tab_sc[0:32, :].bitcast(I32), in_=tab_scales.rearrange("a q c -> q a c").bitcast(I32))
+        nc.sync.dma_start(offs_sb[:], offs)
         load_tab(0)
+        load_wd(0)
+        nc.sync.dma_start(offs2_sb[:], offs2)
         for q in range(4):
             nc.sync.dma_start(
                 out=wd_sc[32 * q : 32 * q + 4, :, :].bitcast(I32),
                 in_=wd_scales[:, 4 * q : 4 * q + 4, :].rearrange("a r c -> r a c").bitcast(I32),
             )
         load_tab(1)
-        nc.sync.dma_start(out=uses_raw[0][:], in_=rows(uses, 0))
-        nc.sync.dma_start(out=wgt_sb[:], in_=wgt)
-        nc.sync.dma_start(offs2_sb[:], offs2)
-        nc.sync.dma_start(out=uses_raw[1][:], in_=rows(uses, 1))
-        load_channels(old_sb[0], old, 0)
+        nc.vector.tensor_copy(picked_sc[:], tab_sc[:].indirect(offs_sb[:]))
         for q in range(4):
-            nc.sync.dma_start(out=wu_sc[32 * q : 32 * q + 8, :].bitcast(I32), in_=wu_scales[:, 4 * q : 4 * q + 4, :].bitcast(I32))
-        load_wu(0)
-        load_channels(old_sb[1], old, 1)
-        load_wu(1)
-        for b in range(RP):
-            load_channels(wo_raw[b], wo, b)
+            nc.sync.dma_start(out=v_sc[32 * q : 32 * q + 4, :, :].bitcast(I32), in_=picked_sc[8 * q : 8 * q + 8, :].bitcast(I32))
+        late = sb("late", [P, M + PACK * (KP * M + RP * M + RP * N)], F32, tag="early")
+
+        def part(start, width):
+            return late[:, start : start + PACK * width].rearrange("p (i c) -> p i c", i=PACK)
+
+        wgt_sb = late[:, 0:M]
+        uses_raw = [part(M + PACK * M * a, M) for a in range(KP)]
+        old_sb = [part(M + PACK * (KP * M + M * b), M) for b in range(RP)]
+        wo_raw = [part(M + PACK * (KP * M + RP * M + N * b), N) for b in range(RP)]
 
         def interleaved(t):
             return t.rearrange("p (c j) i -> p c i j", j=2)
@@ -112,12 +110,11 @@ def tile_list_reaching_names_kernel(
         def planar(t):
             return t.rearrange("p i (c j) -> p c i j", j=2)
 
-        v = [[sb("v%d_%d" % (a, s), [P, BANK], U32) for s in range(SH)] for a in range(KP)]
+        v = [sb("v%d" % a, [P, S], U32) for a in range(KP)]
         cols = BANK // 16
 
         def gather_words(a, s):
-            nc.vector.tensor_copy(v[a][s][:], tab[a][:].bitcast(U32).indirect(offs_sb[:, cols * s : cols * (s + 1)]))
-
+            nc.vector.tensor_copy(v[a][:, BANK * s : BANK * (s + 1)], tab[a][:].bitcast(U32).indirect(offs_sb[:, cols * s : cols * (s + 1)]))
 
         wd = [sb("wd%d" % b, [P, KP, 2 * PASS], U8) for b in range(RP)]
         wd_s = [sb("wd_s%d" % b, [P, KP, PASS], U8) for b in range(RP)]
@@ -129,23 +126,32 @@ def tile_list_reaching_names_kernel(
                 in_=src.rearrange("p a (q i w) -> p a i q w", i=PACK, w=words),
             )
 
-        def permute_wd_words(b):
-            permute(wd[b][:].bitcast(I32), wd_raw[:, :, 2 * PASS * b : 2 * PASS * (b + 1)].bitcast(I32))
-
-        def permute_wd_scales(b):
+        def permute_wd(b):
+            permute(wd[b][:].bitcast(I32), wd_raw[b][:].bitcast(I32))
             permute(wd_s[b][:].bitcast(I32), wd_sc[:, :, PASS * b : PASS * (b + 1)].bitcast(I32))
 
-        for b in range(RP):
-            permute_wd_words(b)
-        nc.vector.tensor_copy(v_sc[0][:], tab_sc[:].indirect(offs_sb[:]))
-        nc.scalar.dma_start(out=v_sc[1][0:64, :].bitcast(I32), in_=v_sc[0][4:68, :].bitcast(I32))
-        nc.scalar.dma_start(out=v_sc[1][64:P, :].bitcast(I32), in_=v_sc[0][60:124, :].bitcast(I32))
         gather_words(0, 0)
+        permute_wd(0)
+        load_wd(1)
+        nc.sync.dma_start(out=wgt_sb, in_=wgt)
+        load_uses(0)
         gather_words(0, 1)
-        permute_wd_scales(0)
         gather_words(1, 0)
         gather_words(1, 1)
-        permute_wd_scales(1)
+        permute_wd(1)
+
+        wu = [sb("wu%d" % b, [P, KP, PASS], I32, tag="words%d" % b) for b in range(RP)]
+        wu_sc = sb("wu_sc", [P, H], U8, tag="weight_sc")
+        nc.vector.memset(wu_sc[:].bitcast(I32), 0)
+        load_channels(old_sb[0], old, 0)
+        load_uses(1)
+        for q in range(4):
+            nc.sync.dma_start(out=wu_sc[32 * q : 32 * q + 8, :].bitcast(I32), in_=wu_scales[:, 4 * q : 4 * q + 4, :].bitcast(I32))
+        load_wu(0)
+        load_channels(old_sb[1], old, 1)
+        load_wu(1)
+        for b in range(RP):
+            load_channels(wo_raw[b], wo, b)
 
         uses_bf = [sb("uses_bf%d" % a, [P, M, PACK], BF16) for a in range(KP)]
         u_codes = [sb("u_codes%d" % a, [P, M], U32) for a in range(KP)]
@@ -154,11 +160,8 @@ def tile_list_reaching_names_kernel(
         def quantize(codes, scales, src):
             nc.vector.quantize_mx(out=codes.bitcast(FP8X4), scales=scales, in_=src)
 
-        def cast_uses(a):
-            split = M if a == 0 else M // 2
-            nc.scalar.copy(out=interleaved(uses_bf[a][:, 0:split, :]), in_=planar(uses_raw[a][:, :, 0:split]))
-            if split < M:
-                nc.vector.tensor_copy(out=interleaved(uses_bf[a][:, split:M, :]), in_=planar(uses_raw[a][:, :, split:M]))
+        def cast_uses(a, copy, c0=0, c1=M):
+            copy(out=interleaved(uses_bf[a][:, c0:c1, :]), in_=planar(uses_raw[a][:, :, c0:c1]))
 
         def quantize_uses(a):
             quantize(u_codes[a][:], u_sc[a][:], uses_bf[a][:].rearrange("p m i -> p (m i)"))
@@ -166,94 +169,135 @@ def tile_list_reaching_names_kernel(
         ident = sb("ident", [P, P], F32)
         neg_wgt = sb("neg_wgt", [P, M], F32)
         make_identity(nc, ident[:])
-        nc.gpsimd.tensor_scalar(out=neg_wgt[:], in0=wgt_sb[:], scalar1=-1.0, scalar2=0.0, op0=ALU.mult, op1=ALU.add)
+        nc.scalar.activation(out=neg_wgt[:], in_=wgt_sb, func=ACT.Copy, scale=-1.0)
 
         h = {}
+        h_bank = {}
         x = {}
-        gate_t = [sb("gate_t%d" % b, [P, PACK, MT, P], F32) for b in range(RP)]
+        gate = [sb("gate%d" % b, [P, PACK, M], F32) for b in range(RP)]
+        x_all = [sb("x%d" % b, [P, PACK, M], F32) for b in range(RP)]
+        d_all = sb("d_all", [P, PACK, M], F32)
         d_t = {}
         e_t = {}
 
-        def turn_bank():
-            return psum.tile([P, PACK, P], F32, name="turn", tag="turn", bufs=4)
+        def new_bank(kind):
+            return psum.tile([P, BANK], F32, name=kind, tag=kind, bufs=4)
 
-        def mm_bank():
-            return psum.tile([P, BANK], F32, name="mm", tag="mm", bufs=4)
+        def h_pass(b, i, s, a):
+            if a == 0:
+                h_bank[b, i, s] = new_bank("mm")
+            nc.tensor.matmul_mx(
+                out=h_bank[b, i, s][:],
+                lhsT=wd[b][:, a, 2 * P * i : 2 * P * (i + 1)].bitcast(FP4X4),
+                lhsT_scale=wd_s[b][:, a, P * i : P * (i + 1)],
+                rhs=v[a][:, BANK * s : BANK * (s + 1)].bitcast(FP8X4),
+                rhs_scale=v_sc[:, a, BANK * s : BANK * (s + 1)],
+                start=(a == 0),
+                stop=(a == KP - 1),
+            )
 
-        def make_h(b, i, halves=(0, 1)):
-            if 0 in halves:
+        def h_copy(b, i, s, copy=nc.scalar.copy):
+            if s == 0:
                 h[b, i] = sb("h%d_%d" % (b, i), [P, S], F32)
-            for s in halves:
-                bank = mm_bank()
+            copy(out=h[b, i][:, BANK * s : BANK * (s + 1)], in_=h_bank[b, i, s][:])
+
+        def make_h(b, i):
+            for s in range(SH):
                 for a in range(KP):
+                    h_pass(b, i, s, a)
+                h_copy(b, i, s)
+
+        wu_p = {}
+        wu_s = {}
+
+        def permute_wu(b):
+            wu_p[b] = sb("wu_p%d" % b, [P, KP, PASS], I32)
+            wu_s[b] = sb("wu_s%d" % b, [P, 1, PASS], U8)
+            permute(wu_p[b][:], wu[b][:])
+            permute(wu_s[b][:].bitcast(I32), wu_sc[:, PASS * b : PASS * (b + 1)].rearrange("p (o c) -> p o c", o=1).bitcast(I32))
+
+        def make_gate(b, j):
+            bank = new_bank("mm")
+            js = slice(P * j, P * (j + 1))
+            for a in range(KP):
+                if b in TURNED:
                     nc.tensor.matmul_mx(
                         out=bank[:],
-                        lhsT=wd[b][:, a, 2 * P * i : 2 * P * (i + 1)].bitcast(FP4X4),
-                        lhsT_scale=wd_s[b][:, a, P * i : P * (i + 1)],
-                        rhs=v[a][s][:].bitcast(FP8X4),
-                        rhs_scale=v_sc[a][:, BANK * s : BANK * (s + 1)],
+                        lhsT=u_codes[a][:, js].bitcast(FP8X4),
+                        lhsT_scale=u_sc[a][:, js],
+                        rhs=wu[b][:, a, :].bitcast(FP8X4),
+                        rhs_scale=wu_sc[4 * a : P, PASS * b : PASS * (b + 1)],
                         start=(a == 0),
                         stop=(a == KP - 1),
                     )
-                copy = nc.vector.tensor_copy if (b, i, s) == (0, 0, 1) else nc.scalar.copy
-                copy(out=h[b, i][:, BANK * s : BANK * (s + 1)], in_=bank[:])
-
-        def make_gate(b, t):
-            bank = mm_bank()
-            for a in range(KP):
-                nc.tensor.matmul_mx(
-                    out=bank[:],
-                    lhsT=u_codes[a][:, P * t : P * (t + 1)].bitcast(FP8X4),
-                    lhsT_scale=u_sc[a][:, P * t : P * (t + 1)],
-                    rhs=wu[b][:, a, :].bitcast(FP8X4),
-                    rhs_scale=wu_sc[4 * a : P, PASS * b : PASS * (b + 1)],
-                    start=(a == 0),
-                    stop=(a == KP - 1),
+                else:
+                    nc.tensor.matmul_mx(
+                        out=bank[:],
+                        lhsT=wu_p[b][:, a, js].bitcast(FP8X4),
+                        lhsT_scale=wu_s[b][4 * a : P, 0, js],
+                        rhs=u_codes[a][:].bitcast(FP8X4),
+                        rhs_scale=u_sc[a][:],
+                        start=(a == 0),
+                        stop=(a == KP - 1),
+                    )
+            if b in TURNED:
+                nc.scalar.activation(
+                    out=gate[b][:, j, :].rearrange("m (i q e) -> m i q e", i=PACK, e=RUN),
+                    in_=bank[:].rearrange("m (q i e) -> m i q e", i=PACK, e=RUN),
+                    func=ACT.Sigmoid,
                 )
-            nc.scalar.activation(
-                out=gate_t[b][:, :, t, :].rearrange("m i (q e) -> m i q e", e=RUN),
-                in_=bank[:].rearrange("m (q i e) -> m i q e", i=PACK, e=RUN),
-                func=ACT.Sigmoid,
-            )
+            else:
+                nc.scalar.activation(out=gate[b][:, j, :], in_=bank[:], func=ACT.Sigmoid)
 
         def pick(b, i):
-            x[b, i] = sb("x%d_%d" % (b, i), [P, M], F32)
-            nc.vector.tensor_tensor(x[b, i][:], h[b, i][:].indirect(offs2_sb[:]), neg_wgt[:], ALU.mult)
+            x[b, i] = x_all[b][:, i, :]
+            nc.vector.tensor_tensor(x[b, i], h[b, i][:].indirect(offs2_sb[:]), neg_wgt[:], ALU.mult)
 
         def difference(b, i):
-            d_t[b, i] = turn_bank()
-            for t in range(MT):
-                ms = slice(P * t, P * (t + 1))
-                nc.tensor.matmul(out=d_t[b, i][:, t, :], lhsT=old_sb[b][:, i, ms], rhs=ident[:], is_transpose=True, start=True, stop=False)
-                nc.tensor.matmul(out=d_t[b, i][:, t, :], lhsT=x[b, i][:, ms], rhs=ident[:], is_transpose=True, start=False, stop=True)
+            if b in TURNED:
+                for t in range(MT):
+                    if i == 0:
+                        d_t[b, t] = new_bank("turn")
+                    ms = slice(P * t, P * (t + 1))
+                    dst = d_t[b, t][:, P * i : P * (i + 1)]
+                    nc.tensor.matmul(out=dst, lhsT=old_sb[b][:, i, ms], rhs=ident[:], is_transpose=True, start=True, stop=False)
+                    nc.tensor.matmul(out=dst, lhsT=x[b, i][:, ms], rhs=ident[:], is_transpose=True, start=False, stop=True)
+
+        def difference_flat(b, i0, i1):
+            nc.vector.tensor_tensor(d_all[:, i0:i1, :], old_sb[b][:, i0:i1, :], x_all[b][:, i0:i1, :], ALU.add)
+
+        def gated_flat(b, i0, i1):
+            nc.vector.tensor_tensor(e_all[b][:, i0:i1, :], d_all[:, i0:i1, :], gate[b][:, i0:i1, :], ALU.mult)
+
+        e_all = [sb("e%d" % b, [P, PACK, M], F32) for b in range(RP)]
 
         def gated(b, i):
-            e_t[b, i] = sb("e_t%d_%d" % (b, i), [P, MT, P], F32)
-            nc.vector.tensor_tensor(e_t[b, i][:], d_t[b, i][:], gate_t[b][:, i, :, :], ALU.mult)
+            nc.vector.tensor_tensor(e_all[b][:, i, :], d_t[b, i][:], gate[b][:, i, :], ALU.mult)
 
-        z_codes = {}
-        z_sc = {}
-        z_bf = {}
+        z_codes = [sb("z_codes%d" % b, [P, M], U32) for b in range(RP)]
+        z_sc = [sb("z_sc%d" % b, [P, M], U8) for b in range(RP)]
+        z_bf = [sb("z_bf%d" % b, [P, M, PACK], BF16) for b in range(RP)]
 
-        def make_z(b, t):
-            ms = slice(P * t, P * (t + 1))
-            z_bf[b, t] = sb("z_bf%d_%d" % (b, t), [P, P, PACK], BF16)
-            e = mm_bank()[:].rearrange("p (i m) -> p i m", i=PACK)
-            for i in range(PACK):
-                nc.tensor.transpose(e[:, i, :], e_t[b, i][:, t, :], ident[:])
-            nc.vector.tensor_tensor(interleaved(z_bf[b, t][:]), planar(old_sb[b][:, :, ms]), planar(e), ALU.subtract)
+        def make_z(b, t, tiles=1):
+            ms = slice(P * t, P * (t + tiles))
+            if b in TURNED:
+                e = new_bank("mm")[:].rearrange("p (i m) -> p i m", i=PACK)
+                for i in range(PACK):
+                    nc.tensor.transpose(e[:, i, :], e_all[b][:, t, P * i : P * (i + 1)], ident[:])
+            else:
+                e = e_all[b][:, :, ms]
+            nc.vector.tensor_tensor(interleaved(z_bf[b][:, ms, :]), planar(old_sb[b][:, :, ms]), planar(e), ALU.subtract)
 
-        def quantize_z(b, t):
-            z_codes[b, t] = sb("z_codes%d_%d" % (b, t), [P, P], U32)
-            z_sc[b, t] = sb("z_sc%d_%d" % (b, t), [P, P], U8)
-            quantize(z_codes[b, t][:], z_sc[b, t][:], z_bf[b, t][:].rearrange("p m i -> p (m i)"))
+        def quantize_z(b, t, tiles=1):
+            ms = slice(P * t, P * (t + tiles))
+            quantize(z_codes[b][:, ms], z_sc[b][:, ms], z_bf[b][:, ms, :].rearrange("p m i -> p (m i)"))
 
         wo_bf = sb("wo_bf", [P, RP * N, PACK], BF16)
         wo_codes = sb("wo_codes", [P, RP * N], U32)
         wo_sc = sb("wo_sc", [P, RP * N], U8)
 
         def cast_wo(b):
-            nc.scalar.copy(out=interleaved(wo_bf[:, N * b : N * (b + 1), :]), in_=planar(wo_raw[b][:]))
+            nc.scalar.copy(out=interleaved(wo_bf[:, N * b : N * (b + 1), :]), in_=planar(wo_raw[b]))
 
         def quantize_wo():
             for c0, c1 in ((0, 512), (512, RP * N)):
@@ -263,15 +307,15 @@ def tile_list_reaching_names_kernel(
 
         def project(b, t):
             if b == 0:
-                out_bank[t] = turn_bank()[:].rearrange("p i m -> p (i m)")
+                out_bank[t] = new_bank("turn")
             for n in range(NT):
                 ns = slice(N * b + P * n, N * b + P * (n + 1))
                 nc.tensor.matmul_mx(
                     out=out_bank[t][:, P * n : P * (n + 1)],
                     lhsT=wo_codes[:, ns].bitcast(FP8X4),
                     lhsT_scale=wo_sc[:, ns],
-                    rhs=z_codes[b, t][:].bitcast(FP8X4),
-                    rhs_scale=z_sc[b, t][:],
+                    rhs=z_codes[b][:, P * t : P * (t + 1)].bitcast(FP8X4),
+                    rhs_scale=z_sc[b][:, P * t : P * (t + 1)],
                     start=(b == 0 and n == 0),
                     stop=(b == RP - 1 and n == NT - 1),
                 )
@@ -281,41 +325,59 @@ def tile_list_reaching_names_kernel(
             nc.scalar.copy(out=res[:].rearrange("p n m -> p (n m)"), in_=out_bank[t][:, 0 : NT * P])
             nc.sync.dma_start(out=out[:, P * t : P * (t + 1)].rearrange("(n p) m -> p n m", p=P), in_=res[:])
 
-        tiles = [(b, i) for b in range(RP) for i in range(PACK)]
-        make_h(0, 0, (0,))
-        make_h(0, 1, (0,))
-        make_h(0, 0, (1,))
-        make_h(0, 1, (1,))
-        for j in range(len(tiles)):
-            if j + 2 < len(tiles):
-                make_h(*tiles[j + 2])
-            pick(*tiles[j])
-            if 1 <= j <= PACK:
-                difference(*tiles[j - 1])
-            if j in (1, 3):
-                cast_uses(j // 2)
-                quantize_uses(j // 2)
-        for b in range(RP):
-            for t in range(MT):
-                make_gate(b, t)
+        for a in range(KP):
+            for s in range(SH):
+                h_pass(0, 0, s, a)
+        h_copy(0, 0, 0)
+        h_copy(0, 0, 1, nc.vector.tensor_copy)
+        for i in range(1, PACK):
+            make_h(0, i)
+        pick(0, 0)
+        cast_uses(0, nc.vector.tensor_copy)
+        quantize_uses(0)
+        make_h(1, 0)
+        for i in range(1, PACK):
+            pick(0, i)
+        for i in range(PACK):
+            difference(0, i)
+        cast_uses(1, nc.scalar.copy)
+        quantize_uses(1)
+        make_h(1, 1)
+        make_h(1, 2)
+        for t in range(MT):
+            make_gate(0, t)
+        make_h(1, 3)
+        pick(1, 0)
+        permute_wu(1)
+        for i in range(PACK):
+            make_gate(1, i)
+        pick(1, 1)
+        gated(0, 0)
+        gated(0, 1)
+        difference_flat(1, 0, 2)
+        pick(1, 2)
+        gated(0, 2)
+        gated(0, 3)
+        pick(1, 3)
         for b in range(RP):
             cast_wo(b)
-        for i in range(PACK):
-            gated(0, i)
-            difference(1, i)
-        for i in range(PACK):
-            gated(1, i)
-        for t in range(MT):
-            make_z(0, t)
-        for t in range(MT):
-            quantize_z(0, t)
+        make_z(0, 0)
+        make_z(0, 1)
+        gated_flat(1, 0, 2)
+        difference_flat(1, 2, 4)
+        make_z(0, 2)
+        make_z(0, 3)
+        gated_flat(1, 2, 4)
+        quantize_z(0, 0, MT)
         quantize_wo()
         for t in range(MT):
             project(0, t)
-        for t in range(MT + 1):
-            if t < MT:
-                make_z(1, t)
-            if t >= 1:
-                quantize_z(1, t - 1)
-                project(1, t - 1)
-                store(t - 1)
+        make_z(1, 0, 2)
+        make_z(1, 2)
+        quantize_z(1, 0, 2)
+        make_z(1, 3)
+        quantize_z(1, 2)
+        quantize_z(1, 3)
+        for t in range(MT):
+            project(1, t)
+            store(t)

@@ -28,6 +28,7 @@ MT = M // P
 NT = N // P
 SH = S // BANK
 TURNED = (0,)
+WARM = False
 
 
 def tile_list_reaching_names_kernel(
@@ -36,6 +37,7 @@ def tile_list_reaching_names_kernel(
     nc = tc.nc
     with ExitStack() as ctx:
         keep = ctx.enter_context(tc.tile_pool(name="keep", bufs=1))
+        shared = ctx.enter_context(tc.tile_pool(name="shared", bufs=1))
         psum = ctx.enter_context(tc.psum_pool(name="psum", bufs=1))
 
         def sb(name, shape, dtype, tag=None):
@@ -43,8 +45,9 @@ def tile_list_reaching_names_kernel(
 
         offs_sb = keep.tile([P, S // 16], U16, name="offs_sb")
         offs2_sb = keep.tile([P, M // 16], U16, name="offs2_sb")
-        tab_sc = sb("tab_sc", [P, T], U8, tag="early")
-        wd_sc = sb("wd_sc", [P, KP, H], U8, tag="weight_sc")
+        floats = M + PACK * (KP * M + RP * M + RP * N)
+        tab_sc = shared.tile([P, T], U8, name="tab_sc", offset=4 * floats - T // 4, align_bytes=64)
+        wd_sc = sb("wd_sc", [P, KP, H], U8)
         picked_sc = sb("picked_sc", [P, S], U8)
         v_sc = sb("v_sc", [P, KP, S], U8)
         warm = sb("warm", [P, 1], F32)
@@ -57,7 +60,7 @@ def tile_list_reaching_names_kernel(
         nc.scalar.activation(out=warm[:], in_=warm[:], func=ACT.Sigmoid)
 
         wd_raw = {}
-        tab = [sb("tab%d" % a, [P, T], I32, tag="words%d" % a) for a in range(KP)]
+        tab = [sb("tab%d" % a, [P, T], I32) for a in range(KP)]
 
         def load_uses(a):
             rows = uses[PASS * a : PASS * (a + 1), :].rearrange("(p i) c -> p i c", i=PACK)
@@ -78,28 +81,32 @@ def tile_list_reaching_names_kernel(
 
         def load_wu(b):
             src = wu_words.rearrange("a p c i -> p a (c i)")[:, :, PACK * PASS * b : PACK * PASS * (b + 1)]
-            nc.sync.dma_start(out=wu[b][:], in_=src.bitcast(I32))
+            nc.sync.dma_start(out=wu[b], in_=src.bitcast(I32))
 
         nc.sync.dma_start(out=tab_sc[0:32, :].bitcast(I32), in_=tab_scales.rearrange("a q c -> q a c").bitcast(I32))
         nc.sync.dma_start(offs_sb[:], offs)
         load_tab(0)
         load_wd(0)
         nc.sync.dma_start(offs2_sb[:], offs2)
-        for q in range(4):
+        for q in (0, 2, 1, 3):
             nc.sync.dma_start(
                 out=wd_sc[32 * q : 32 * q + 4, :, :].bitcast(I32),
                 in_=wd_scales[:, 4 * q : 4 * q + 4, :].rearrange("a r c -> r a c").bitcast(I32),
             )
         load_tab(1)
         nc.vector.tensor_copy(picked_sc[:], tab_sc[:].indirect(offs_sb[:]))
-        for q in range(4):
+        for q in (0, 2, 1, 3):
             nc.sync.dma_start(out=v_sc[32 * q : 32 * q + 4, :, :].bitcast(I32), in_=picked_sc[8 * q : 8 * q + 8, :].bitcast(I32))
-        late = sb("late", [P, M + PACK * (KP * M + RP * M + RP * N)], F32, tag="early")
+        late = shared.tile([P, floats], F32, name="late", offset=0, align_bytes=64)
+        wu_sc = shared.tile([P, H], U8, name="wu_sc", offset=4 * floats, align_bytes=64)
+        wu_all = shared.tile([P, RP * KP * PASS], I32, name="wu_all", offset=4 * floats + H, align_bytes=64)
 
         def part(start, width):
             return late[:, start : start + PACK * width].rearrange("p (i c) -> p i c", i=PACK)
 
         wgt_sb = late[:, 0:M]
+        wu = [wu_all[:, KP * PASS * b : KP * PASS * (b + 1)].rearrange("p (a c) -> p a c", a=KP) for b in range(RP)]
+        nc.gpsimd.memset(wu_sc[:].bitcast(I32), 0)
         uses_raw = [part(M + PACK * M * a, M) for a in range(KP)]
         old_sb = [part(M + PACK * (KP * M + M * b), M) for b in range(RP)]
         wo_raw = [part(M + PACK * (KP * M + RP * M + N * b), N) for b in range(RP)]
@@ -140,16 +147,13 @@ def tile_list_reaching_names_kernel(
         gather_words(1, 1)
         permute_wd(1)
 
-        wu = [sb("wu%d" % b, [P, KP, PASS], I32, tag="words%d" % b) for b in range(RP)]
-        wu_sc = sb("wu_sc", [P, H], U8, tag="weight_sc")
-        nc.vector.memset(wu_sc[:].bitcast(I32), 0)
         load_channels(old_sb[0], old, 0)
         load_uses(1)
-        for q in range(4):
+        for q in (0, 2, 1, 3):
             nc.sync.dma_start(out=wu_sc[32 * q : 32 * q + 8, :].bitcast(I32), in_=wu_scales[:, 4 * q : 4 * q + 4, :].bitcast(I32))
         load_wu(0)
-        load_channels(old_sb[1], old, 1)
         load_wu(1)
+        load_channels(old_sb[1], old, 1)
         for b in range(RP):
             load_channels(wo_raw[b], wo, b)
 
@@ -174,14 +178,16 @@ def tile_list_reaching_names_kernel(
         h = {}
         h_bank = {}
         x = {}
-        gate = [sb("gate%d" % b, [P, PACK, M], F32) for b in range(RP)]
-        x_all = [sb("x%d" % b, [P, PACK, M], F32) for b in range(RP)]
-        d_all = sb("d_all", [P, PACK, M], F32)
+        gate = {}
+        gate_all = [sb("gate%d" % b, [P, PACK, M], F32) for b in range(RP)]
+        flat = {}
         d_t = {}
         e_t = {}
 
         def new_bank(kind):
-            return psum.tile([P, BANK], F32, name=kind, tag=kind, bufs=4)
+            if kind == "mm":
+                return psum.tile([P, BANK], F32, name="mm", tag="mm", bufs=4)
+            return psum.tile([P, BANK], F32, name="site", tag="site%d" % kind)
 
         def h_pass(b, i, s, a):
             if a == 0:
@@ -211,9 +217,9 @@ def tile_list_reaching_names_kernel(
         wu_s = {}
 
         def permute_wu(b):
-            wu_p[b] = sb("wu_p%d" % b, [P, KP, PASS], I32)
+            wu_p[b] = sb("wu_p%d" % b, [P, KP, PASS], I32, tag="h1_2")
             wu_s[b] = sb("wu_s%d" % b, [P, 1, PASS], U8)
-            permute(wu_p[b][:], wu[b][:])
+            permute(wu_p[b][:], wu[b])
             permute(wu_s[b][:].bitcast(I32), wu_sc[:, PASS * b : PASS * (b + 1)].rearrange("p (o c) -> p o c", o=1).bitcast(I32))
 
         def make_gate(b, j):
@@ -240,39 +246,45 @@ def tile_list_reaching_names_kernel(
                         start=(a == 0),
                         stop=(a == KP - 1),
                     )
+            gate[b, j] = gate_all[b][:, j, :]
             if b in TURNED:
                 nc.scalar.activation(
-                    out=gate[b][:, j, :].rearrange("m (i q e) -> m i q e", i=PACK, e=RUN),
+                    out=gate[b, j].rearrange("m (i q e) -> m i q e", i=PACK, e=RUN),
                     in_=bank[:].rearrange("m (q i e) -> m i q e", i=PACK, e=RUN),
                     func=ACT.Sigmoid,
                 )
             else:
-                nc.scalar.activation(out=gate[b][:, j, :], in_=bank[:], func=ACT.Sigmoid)
+                nc.scalar.activation(out=gate[b, j], in_=bank[:], func=ACT.Sigmoid)
 
-        def pick(b, i):
-            x[b, i] = x_all[b][:, i, :]
+        def pick(b, i, after=None):
+            x[b, i] = sb("x%d_%d" % (b, i), [P, M], F32, tag=after)[:]
             nc.vector.tensor_tensor(x[b, i], h[b, i][:].indirect(offs2_sb[:]), neg_wgt[:], ALU.mult)
 
-        def difference(b, i):
+        def difference(b, t):
             if b in TURNED:
-                for t in range(MT):
-                    if i == 0:
-                        d_t[b, t] = new_bank("turn")
-                    ms = slice(P * t, P * (t + 1))
+                d_t[b, t] = new_bank(t)
+                ms = slice(P * t, P * (t + 1))
+                for i in range(PACK):
                     dst = d_t[b, t][:, P * i : P * (i + 1)]
                     nc.tensor.matmul(out=dst, lhsT=old_sb[b][:, i, ms], rhs=ident[:], is_transpose=True, start=True, stop=False)
                     nc.tensor.matmul(out=dst, lhsT=x[b, i][:, ms], rhs=ident[:], is_transpose=True, start=False, stop=True)
 
-        def difference_flat(b, i0, i1):
-            nc.vector.tensor_tensor(d_all[:, i0:i1, :], old_sb[b][:, i0:i1, :], x_all[b][:, i0:i1, :], ALU.add)
+
+        def difference_flat(b, i):
+            if i == 0:
+                flat["d"] = sb("d_flat", [P, PACK, M], F32, tag="h1_3")
+            nc.gpsimd.tensor_tensor(flat["d"][:, i, :], old_sb[b][:, i, :], x[b, i], ALU.add)
 
         def gated_flat(b, i0, i1):
-            nc.vector.tensor_tensor(e_all[b][:, i0:i1, :], d_all[:, i0:i1, :], gate[b][:, i0:i1, :], ALU.mult)
-
-        e_all = [sb("e%d" % b, [P, PACK, M], F32) for b in range(RP)]
+            if i0 == 0:
+                flat["e"] = sb("e_flat", [P, PACK, M], F32)
+            nc.vector.tensor_tensor(flat["e"][:, i0:i1, :], flat["d"][:, i0:i1, :], gate_all[b][:, i0:i1, :], ALU.mult)
 
         def gated(b, i):
-            nc.vector.tensor_tensor(e_all[b][:, i, :], d_t[b, i][:], gate[b][:, i, :], ALU.mult)
+            if i == 0:
+                flat["e_t"] = sb("e_turned", [P, MT, PASS], F32, tag="neg_wgt")
+            e_t[b, i] = flat["e_t"][:, i, :]
+            nc.vector.tensor_tensor(e_t[b, i], d_t[b, i][:], gate[b, i], ALU.mult)
 
         z_codes = [sb("z_codes%d" % b, [P, M], U32) for b in range(RP)]
         z_sc = [sb("z_sc%d" % b, [P, M], U8) for b in range(RP)]
@@ -281,33 +293,47 @@ def tile_list_reaching_names_kernel(
         def make_z(b, t, tiles=1):
             ms = slice(P * t, P * (t + tiles))
             if b in TURNED:
-                e = new_bank("mm")[:].rearrange("p (i m) -> p i m", i=PACK)
+                bank = new_bank("mm")
+                if b == RP - 1 and WARM:
+                    nc.tensor.matmul_mx(
+                        out=bank[:],
+                        lhsT=u_codes[0][:, 0:P].bitcast(FP8X4),
+                        lhsT_scale=u_sc[0][:, 0:P],
+                        rhs=wu[b][:, 0, :].bitcast(FP8X4),
+                        rhs_scale=wu_sc[:, PASS * b : PASS * (b + 1)],
+                        start=True,
+                        stop=True,
+                    )
+                e = bank[:].rearrange("p (i m) -> p i m", i=PACK)
                 for i in range(PACK):
-                    nc.tensor.transpose(e[:, i, :], e_all[b][:, t, P * i : P * (i + 1)], ident[:])
+                    nc.tensor.transpose(e[:, i, :], e_t[b, t][:, P * i : P * (i + 1)], ident[:])
             else:
-                e = e_all[b][:, :, ms]
+                e = flat["e"][:, :, ms]
             nc.vector.tensor_tensor(interleaved(z_bf[b][:, ms, :]), planar(old_sb[b][:, :, ms]), planar(e), ALU.subtract)
 
         def quantize_z(b, t, tiles=1):
             ms = slice(P * t, P * (t + tiles))
             quantize(z_codes[b][:, ms], z_sc[b][:, ms], z_bf[b][:, ms, :].rearrange("p m i -> p (m i)"))
 
-        wo_bf = sb("wo_bf", [P, RP * N, PACK], BF16)
+        rounded = {}
         wo_codes = sb("wo_codes", [P, RP * N], U32)
         wo_sc = sb("wo_sc", [P, RP * N], U8)
 
         def cast_wo(b):
-            nc.scalar.copy(out=interleaved(wo_bf[:, N * b : N * (b + 1), :]), in_=planar(wo_raw[b]))
+            if b == 0:
+                rounded[0] = sb("wo_bf", [P, RP * N, PACK], BF16, tag="gate0")
+            for c0 in range(0, N, N // 2):
+                nc.scalar.copy(out=interleaved(rounded[0][:, N * b + c0 : N * b + c0 + N // 2, :]), in_=planar(wo_raw[b][:, :, c0 : c0 + N // 2]))
 
         def quantize_wo():
             for c0, c1 in ((0, 512), (512, RP * N)):
-                quantize(wo_codes[:, c0:c1], wo_sc[:, c0:c1], wo_bf[:, c0:c1, :].rearrange("p n i -> p (n i)"))
+                quantize(wo_codes[:, c0:c1], wo_sc[:, c0:c1], rounded[0][:, c0:c1, :].rearrange("p n i -> p (n i)"))
 
         out_bank = {}
 
         def project(b, t):
             if b == 0:
-                out_bank[t] = new_bank("turn")
+                out_bank[t] = new_bank(t)
             for n in range(NT):
                 ns = slice(N * b + P * n, N * b + P * (n + 1))
                 nc.tensor.matmul_mx(
@@ -322,7 +348,8 @@ def tile_list_reaching_names_kernel(
 
         def store(t):
             res = sb("res%d" % t, [P, NT, P], F32)
-            nc.scalar.copy(out=res[:].rearrange("p n m -> p (n m)"), in_=out_bank[t][:, 0 : NT * P])
+            copy = nc.vector.tensor_copy if t == MT - 1 else nc.scalar.copy
+            copy(out=res[:].rearrange("p n m -> p (n m)"), in_=out_bank[t][:, 0 : NT * P])
             nc.sync.dma_start(out=out[:, P * t : P * (t + 1)].rearrange("(n p) m -> p n m", p=P), in_=res[:])
 
         for a in range(KP):
@@ -335,49 +362,40 @@ def tile_list_reaching_names_kernel(
         pick(0, 0)
         cast_uses(0, nc.vector.tensor_copy)
         quantize_uses(0)
-        make_h(1, 0)
+        for i in range(PACK):
+            make_h(1, i)
         for i in range(1, PACK):
             pick(0, i)
-        for i in range(PACK):
-            difference(0, i)
+        for t in range(MT):
+            difference(0, t)
         cast_uses(1, nc.scalar.copy)
         quantize_uses(1)
-        make_h(1, 1)
-        make_h(1, 2)
         for t in range(MT):
             make_gate(0, t)
-        make_h(1, 3)
-        pick(1, 0)
+        for i in range(PACK - 1):
+            pick(1, i)
         permute_wu(1)
+        pick(1, PACK - 1)
+        for i in range(PACK):
+            difference_flat(1, i)
         for i in range(PACK):
             make_gate(1, i)
-        pick(1, 1)
-        gated(0, 0)
-        gated(0, 1)
-        difference_flat(1, 0, 2)
-        pick(1, 2)
-        gated(0, 2)
-        gated(0, 3)
-        pick(1, 3)
+        for t in range(MT):
+            gated(0, t)
+        for t in range(MT):
+            make_z(0, t)
+        quantize_z(0, 0, MT)
         for b in range(RP):
             cast_wo(b)
-        make_z(0, 0)
-        make_z(0, 1)
         gated_flat(1, 0, 2)
-        difference_flat(1, 2, 4)
-        make_z(0, 2)
-        make_z(0, 3)
         gated_flat(1, 2, 4)
-        quantize_z(0, 0, MT)
         quantize_wo()
         for t in range(MT):
             project(0, t)
-        make_z(1, 0, 2)
-        make_z(1, 2)
-        quantize_z(1, 0, 2)
-        make_z(1, 3)
-        quantize_z(1, 2)
-        quantize_z(1, 3)
-        for t in range(MT):
-            project(1, t)
-            store(t)
+        for step in range(MT + 1):
+            if step < MT:
+                make_z(1, step)
+            if step >= 1:
+                quantize_z(1, step - 1)
+                project(1, step - 1)
+                store(step - 1)

@@ -85,8 +85,8 @@ def tile_list_reaching_names_kernel(
 
         nc.sync.dma_start(out=tab_sc[0:32, :].bitcast(I32), in_=tab_scales.rearrange("a q c -> q a c").bitcast(I32))
         nc.sync.dma_start(offs_sb[:], offs)
-        load_tab(0)
         load_wd(0)
+        load_tab(0)
         nc.sync.dma_start(offs2_sb[:], offs2)
         for q in (0, 2, 1, 3):
             nc.sync.dma_start(
@@ -135,17 +135,21 @@ def tile_list_reaching_names_kernel(
 
         def permute_wd(b):
             permute(wd[b][:].bitcast(I32), wd_raw[b][:].bitcast(I32))
+
+        def permute_wd_scales(b):
             permute(wd_s[b][:].bitcast(I32), wd_sc[:, :, PASS * b : PASS * (b + 1)].bitcast(I32))
 
-        gather_words(0, 0)
         permute_wd(0)
+        gather_words(0, 0)
         load_wd(1)
         nc.sync.dma_start(out=wgt_sb, in_=wgt)
         load_uses(0)
         gather_words(0, 1)
+        permute_wd_scales(0)
         gather_words(1, 0)
         gather_words(1, 1)
         permute_wd(1)
+        permute_wd_scales(1)
 
         load_channels(old_sb[0], old, 0)
         load_uses(1)
@@ -325,8 +329,8 @@ def tile_list_reaching_names_kernel(
             for c0 in range(0, N, N // 2):
                 nc.scalar.copy(out=interleaved(rounded[0][:, N * b + c0 : N * b + c0 + N // 2, :]), in_=planar(wo_raw[b][:, :, c0 : c0 + N // 2]))
 
-        def quantize_wo():
-            for c0, c1 in ((0, 512), (512, RP * N)):
+        def quantize_wo(b):
+            for c0, c1 in ((N * b, N * b + 2 * P), (N * b + 2 * P, N * (b + 1))):
                 quantize(wo_codes[:, c0:c1], wo_sc[:, c0:c1], rounded[0][:, c0:c1, :].rearrange("p n i -> p (n i)"))
 
         out_bank = {}
@@ -352,6 +356,17 @@ def tile_list_reaching_names_kernel(
             copy(out=res[:].rearrange("p n m -> p (n m)"), in_=out_bank[t][:, 0 : NT * P])
             nc.sync.dma_start(out=out[:, P * t : P * (t + 1)].rearrange("(n p) m -> p n m", p=P), in_=res[:])
 
+        idle = new_bank(0)
+        for rep in range(4):
+            nc.tensor.matmul_mx(
+                out=idle[:],
+                lhsT=wd[0][:, 0, 0 : 2 * P].bitcast(FP4X4),
+                lhsT_scale=picked_sc[:, 0:P],
+                rhs=v[0][:, 0:BANK].bitcast(FP8X4),
+                rhs_scale=picked_sc[:, 0:BANK],
+                start=True,
+                stop=True,
+            )
         for a in range(KP):
             for s in range(SH):
                 h_pass(0, 0, s, a)
@@ -388,13 +403,15 @@ def tile_list_reaching_names_kernel(
         for b in range(RP):
             cast_wo(b)
         gated_flat(1, 0, 2)
-        gated_flat(1, 2, 4)
-        quantize_wo()
+        quantize_wo(0)
         for t in range(MT):
             project(0, t)
+        gated_flat(1, 2, 4)
         for step in range(MT + 1):
             if step < MT:
                 make_z(1, step)
+            if step == 0:
+                quantize_wo(1)
             if step >= 1:
                 quantize_z(1, step - 1)
                 project(1, step - 1)

@@ -22,13 +22,16 @@ PACK = 4
 PASS = P * PACK
 BANK = 512
 RUN = 8
+LIST = 16
 KP = K // PASS
 RP = H // PASS
 MT = M // P
 NT = N // P
 SH = S // BANK
-TURNED = (0,)
-WARM = False
+PRODUCT_BANKS = 4
+QUADRANTS = (0, 2, 1, 3)
+WARM_PASSES = 4
+EARLY_SLOTS = 2
 
 
 def tile_list_reaching_names_kernel(
@@ -37,16 +40,28 @@ def tile_list_reaching_names_kernel(
     nc = tc.nc
     with ExitStack() as ctx:
         keep = ctx.enter_context(tc.tile_pool(name="keep", bufs=1))
-        shared = ctx.enter_context(tc.tile_pool(name="shared", bufs=1))
+        placed = ctx.enter_context(tc.tile_pool(name="placed", bufs=1))
         psum = ctx.enter_context(tc.psum_pool(name="psum", bufs=1))
 
         def sb(name, shape, dtype, tag=None):
             return keep.tile(shape, dtype, name=name, tag=tag or name, align_bytes=64)
 
-        offs_sb = keep.tile([P, S // 16], U16, name="offs_sb")
-        offs2_sb = keep.tile([P, M // 16], U16, name="offs2_sb")
-        floats = M + PACK * (KP * M + RP * M + RP * N)
-        tab_sc = shared.tile([P, T], U8, name="tab_sc", offset=4 * floats - T // 4, align_bytes=64)
+        def placed_at(offset, name, shape, dtype):
+            return placed.tile(shape, dtype, name=name, offset=offset, align_bytes=64)
+
+        def sites(t, tiles=1):
+            return slice(P * t, P * (t + tiles))
+
+        float_columns = M + PACK * (M + RP * M + RP * N)
+        wu_sc_at = 4 * float_columns
+        wu_at = wu_sc_at + H
+        tab_sc_at = wu_sc_at - T // 4
+        uses1_at = wu_at + 4 * RP * KP * PASS
+        wd_raw_at = [uses1_at + 4 * PACK * M - 2 * PASS, uses1_at + 4 * PACK * M]
+
+        offs_sb = keep.tile([P, S // LIST], U16, name="offs_sb")
+        offs2_sb = keep.tile([P, M // LIST], U16, name="offs2_sb")
+        tab_sc = placed_at(tab_sc_at, "tab_sc", [P, T], U8)
         wd_sc = sb("wd_sc", [P, KP, H], U8)
         picked_sc = sb("picked_sc", [P, S], U8)
         v_sc = sb("v_sc", [P, KP, S], U8)
@@ -66,16 +81,16 @@ def tile_list_reaching_names_kernel(
             rows = uses[PASS * a : PASS * (a + 1), :].rearrange("(p i) c -> p i c", i=PACK)
             nc.sync.dma_start(out=uses_raw[a], in_=rows)
 
-        def load_channels(dst, x, b):
-            blocks = x[PASS * b : PASS * (b + 1), :].rearrange("(q i e) c -> i q e c", i=PACK, e=RUN)
+        def load_channels(dst, src, b):
+            slots = src[PASS * b : PASS * (b + 1), :].rearrange("(q i e) c -> i q e c", i=PACK, e=RUN)
             for i in range(PACK):
-                nc.sync.dma_start(out=dst[:, i, :], in_=blocks[i])
+                nc.sync.dma_start(out=dst[:, i, :], in_=slots[i])
 
         def load_tab(a):
             nc.sync.dma_start(out=tab[a][:], in_=tab_words[a].rearrange("p t i -> p (t i)").bitcast(I32))
 
         def load_wd(b):
-            wd_raw[b] = sb("wd_raw%d" % b, [P, KP, 2 * PASS], U8, tag="wd_raw")
+            wd_raw[b] = placed_at(wd_raw_at[b], "wd_raw%d" % b, [P, KP, 2 * PASS], U8)
             src = wd_words.rearrange("a p c -> p a c")[:, :, 2 * PASS * b : 2 * PASS * (b + 1)]
             nc.sync.dma_start(out=wd_raw[b][:].bitcast(I32), in_=src.bitcast(I32))
 
@@ -88,75 +103,83 @@ def tile_list_reaching_names_kernel(
         load_wd(0)
         load_tab(0)
         nc.sync.dma_start(offs2_sb[:], offs2)
-        for q in (0, 2, 1, 3):
+        for quad in QUADRANTS:
             nc.sync.dma_start(
-                out=wd_sc[32 * q : 32 * q + 4, :, :].bitcast(I32),
-                in_=wd_scales[:, 4 * q : 4 * q + 4, :].rearrange("a r c -> r a c").bitcast(I32),
+                out=wd_sc[32 * quad : 32 * quad + 4, :, :].bitcast(I32),
+                in_=wd_scales[:, 4 * quad : 4 * quad + 4, :].rearrange("a r c -> r a c").bitcast(I32),
             )
         load_tab(1)
         nc.vector.tensor_copy(picked_sc[:], tab_sc[:].indirect(offs_sb[:]))
-        for q in (0, 2, 1, 3):
-            nc.sync.dma_start(out=v_sc[32 * q : 32 * q + 4, :, :].bitcast(I32), in_=picked_sc[8 * q : 8 * q + 8, :].bitcast(I32))
-        late = shared.tile([P, floats], F32, name="late", offset=0, align_bytes=64)
-        wu_sc = shared.tile([P, H], U8, name="wu_sc", offset=4 * floats, align_bytes=64)
-        wu_all = shared.tile([P, RP * KP * PASS], I32, name="wu_all", offset=4 * floats + H, align_bytes=64)
+        for quad in QUADRANTS:
+            nc.sync.dma_start(
+                out=v_sc[32 * quad : 32 * quad + 4, :, :].bitcast(I32),
+                in_=picked_sc[8 * quad : 8 * quad + 8, :].bitcast(I32),
+            )
+        floats = placed_at(0, "floats", [P, float_columns], F32)
+        wu_sc = placed_at(wu_sc_at, "wu_sc", [P, H], U8)
+        wu_all = placed_at(wu_at, "wu_all", [P, RP * KP * PASS], I32)
 
-        def part(start, width):
-            return late[:, start : start + PACK * width].rearrange("p (i c) -> p i c", i=PACK)
+        def four_rows(start, width):
+            return floats[:, start : start + PACK * width].rearrange("p (i c) -> p i c", i=PACK)
 
-        wgt_sb = late[:, 0:M]
+        wgt_sb = floats[:, 0:M]
         wu = [wu_all[:, KP * PASS * b : KP * PASS * (b + 1)].rearrange("p (a c) -> p a c", a=KP) for b in range(RP)]
         nc.gpsimd.memset(wu_sc[:].bitcast(I32), 0)
-        uses_raw = [part(M + PACK * M * a, M) for a in range(KP)]
-        old_sb = [part(M + PACK * (KP * M + M * b), M) for b in range(RP)]
-        wo_raw = [part(M + PACK * (KP * M + RP * M + N * b), N) for b in range(RP)]
+        uses_raw = [four_rows(M, M)]
+        old_sb = [four_rows(M + PACK * (M + M * b), M) for b in range(RP)]
+        wo_raw = [four_rows(M + PACK * (M + RP * M + N * b), N) for b in range(RP)]
 
-        def interleaved(t):
-            return t.rearrange("p (c j) i -> p c i j", j=2)
+        def interleaved(tile):
+            return tile.rearrange("p (c j) i -> p c i j", j=2)
 
-        def planar(t):
-            return t.rearrange("p i (c j) -> p c i j", j=2)
+        def planar(tile):
+            return tile.rearrange("p i (c j) -> p c i j", j=2)
 
         v = [sb("v%d" % a, [P, S], U32) for a in range(KP)]
-        cols = BANK // 16
+        list_columns = BANK // LIST
 
         def gather_words(a, s):
-            nc.vector.tensor_copy(v[a][:, BANK * s : BANK * (s + 1)], tab[a][:].bitcast(U32).indirect(offs_sb[:, cols * s : cols * (s + 1)]))
+            entries = offs_sb[:, list_columns * s : list_columns * (s + 1)]
+            nc.vector.tensor_copy(v[a][:, BANK * s : BANK * (s + 1)], tab[a][:].bitcast(U32).indirect(entries))
 
         wd = [sb("wd%d" % b, [P, KP, 2 * PASS], U8) for b in range(RP)]
         wd_s = [sb("wd_s%d" % b, [P, KP, PASS], U8) for b in range(RP)]
 
-        def permute(dst, src):
+        def slot_major(dst, src):
             words = dst.shape[2] // (PASS // RUN)
             nc.vector.tensor_copy(
                 out=dst.rearrange("p a (i q w) -> p a i q w", i=PACK, w=words),
                 in_=src.rearrange("p a (q i w) -> p a i q w", i=PACK, w=words),
             )
 
-        def permute_wd(b):
-            permute(wd[b][:].bitcast(I32), wd_raw[b][:].bitcast(I32))
+        def order_wd(b):
+            slot_major(wd[b][:].bitcast(I32), wd_raw[b][:].bitcast(I32))
 
-        def permute_wd_scales(b):
-            permute(wd_s[b][:].bitcast(I32), wd_sc[:, :, PASS * b : PASS * (b + 1)].bitcast(I32))
+        def order_wd_scales(b):
+            slot_major(wd_s[b][:].bitcast(I32), wd_sc[:, :, PASS * b : PASS * (b + 1)].bitcast(I32))
 
-        permute_wd(0)
+        order_wd(0)
         gather_words(0, 0)
+        uses_raw.append(placed_at(uses1_at, "uses1", [P, PACK, M], F32)[:])
         load_wd(1)
         nc.sync.dma_start(out=wgt_sb, in_=wgt)
         load_uses(0)
         gather_words(0, 1)
-        permute_wd_scales(0)
+        order_wd_scales(0)
         gather_words(1, 0)
         gather_words(1, 1)
-        permute_wd(1)
-        permute_wd_scales(1)
+        order_wd(1)
+        order_wd_scales(1)
 
         load_channels(old_sb[0], old, 0)
         load_uses(1)
-        for q in (0, 2, 1, 3):
-            nc.sync.dma_start(out=wu_sc[32 * q : 32 * q + 8, :].bitcast(I32), in_=wu_scales[:, 4 * q : 4 * q + 4, :].bitcast(I32))
-        load_wu(0)
-        load_wu(1)
+        for quad in QUADRANTS:
+            nc.sync.dma_start(
+                out=wu_sc[32 * quad : 32 * quad + 8, :].bitcast(I32),
+                in_=wu_scales[:, 4 * quad : 4 * quad + 4, :].bitcast(I32),
+            )
+        for b in range(RP):
+            load_wu(b)
         load_channels(old_sb[1], old, 1)
         for b in range(RP):
             load_channels(wo_raw[b], wo, b)
@@ -166,13 +189,13 @@ def tile_list_reaching_names_kernel(
         u_sc = [sb("u_sc%d" % a, [P, M], U8) for a in range(KP)]
 
         def quantize(codes, scales, src):
-            nc.vector.quantize_mx(out=codes.bitcast(FP8X4), scales=scales, in_=src)
+            nc.vector.quantize_mx(out=codes.bitcast(FP8X4), scales=scales, in_=src.rearrange("p c i -> p (c i)"))
 
-        def cast_uses(a, copy, c0=0, c1=M):
-            copy(out=interleaved(uses_bf[a][:, c0:c1, :]), in_=planar(uses_raw[a][:, :, c0:c1]))
+        def round_uses(a, copy):
+            copy(out=interleaved(uses_bf[a][:]), in_=planar(uses_raw[a]))
 
         def quantize_uses(a):
-            quantize(u_codes[a][:], u_sc[a][:], uses_bf[a][:].rearrange("p m i -> p (m i)"))
+            quantize(u_codes[a][:], u_sc[a][:], uses_bf[a][:])
 
         ident = sb("ident", [P, P], F32)
         neg_wgt = sb("neg_wgt", [P, M], F32)
@@ -181,21 +204,18 @@ def tile_list_reaching_names_kernel(
 
         h = {}
         h_bank = {}
-        x = {}
-        gate = {}
-        gate_all = [sb("gate%d" % b, [P, PACK, M], F32) for b in range(RP)]
-        flat = {}
-        d_t = {}
-        e_t = {}
+        gate = [sb("gate%d" % b, [P, MT, PASS], F32) for b in range(RP)]
+        neg_x = [sb("neg_x%d" % b, [P, PACK, M], F32) for b in range(RP)]
 
-        def new_bank(kind):
-            if kind == "mm":
-                return psum.tile([P, BANK], F32, name="mm", tag="mm", bufs=4)
-            return psum.tile([P, BANK], F32, name="site", tag="site%d" % kind)
+        def product_bank():
+            return psum.tile([P, BANK], F32, name="product", tag="product", bufs=PRODUCT_BANKS)
+
+        def site_bank(t):
+            return psum.tile([P, BANK], F32, name="site", tag="site%d" % t)
 
         def h_pass(b, i, s, a):
             if a == 0:
-                h_bank[b, i, s] = new_bank("mm")
+                h_bank[b, i, s] = product_bank()
             nc.tensor.matmul_mx(
                 out=h_bank[b, i, s][:],
                 lhsT=wd[b][:, a, 2 * P * i : 2 * P * (i + 1)].bitcast(FP4X4),
@@ -207,7 +227,9 @@ def tile_list_reaching_names_kernel(
             )
 
         def h_copy(b, i, s, copy=nc.scalar.copy):
-            if s == 0:
+            if s == 0 and b == 1 and i >= EARLY_SLOTS:
+                h[b, i] = placed_at(uses1_at + 4 * S * (i - EARLY_SLOTS), "h%d_%d" % (b, i), [P, S], F32)
+            elif s == 0:
                 h[b, i] = sb("h%d_%d" % (b, i), [P, S], F32)
             copy(out=h[b, i][:, BANK * s : BANK * (s + 1)], in_=h_bank[b, i, s][:])
 
@@ -217,135 +239,59 @@ def tile_list_reaching_names_kernel(
                     h_pass(b, i, s, a)
                 h_copy(b, i, s)
 
-        wu_p = {}
-        wu_s = {}
+        def pick(b, i):
+            nc.vector.tensor_tensor(neg_x[b][:, i, :], h[b, i][:].indirect(offs2_sb[:]), neg_wgt[:], ALU.mult)
 
-        def permute_wu(b):
-            wu_p[b] = sb("wu_p%d" % b, [P, KP, PASS], I32, tag="h1_2")
-            wu_s[b] = sb("wu_s%d" % b, [P, 1, PASS], U8)
-            permute(wu_p[b][:], wu[b])
-            permute(wu_s[b][:].bitcast(I32), wu_sc[:, PASS * b : PASS * (b + 1)].rearrange("p (o c) -> p o c", o=1).bitcast(I32))
-
-        def make_gate(b, j):
-            bank = new_bank("mm")
-            js = slice(P * j, P * (j + 1))
+        def make_gate(b, t):
+            bank = product_bank()
             for a in range(KP):
-                if b in TURNED:
-                    nc.tensor.matmul_mx(
-                        out=bank[:],
-                        lhsT=u_codes[a][:, js].bitcast(FP8X4),
-                        lhsT_scale=u_sc[a][:, js],
-                        rhs=wu[b][:, a, :].bitcast(FP8X4),
-                        rhs_scale=wu_sc[4 * a : P, PASS * b : PASS * (b + 1)],
-                        start=(a == 0),
-                        stop=(a == KP - 1),
-                    )
-                else:
-                    nc.tensor.matmul_mx(
-                        out=bank[:],
-                        lhsT=wu_p[b][:, a, js].bitcast(FP8X4),
-                        lhsT_scale=wu_s[b][4 * a : P, 0, js],
-                        rhs=u_codes[a][:].bitcast(FP8X4),
-                        rhs_scale=u_sc[a][:],
-                        start=(a == 0),
-                        stop=(a == KP - 1),
-                    )
-            gate[b, j] = gate_all[b][:, j, :]
-            if b in TURNED:
-                nc.scalar.activation(
-                    out=gate[b, j].rearrange("m (i q e) -> m i q e", i=PACK, e=RUN),
-                    in_=bank[:].rearrange("m (q i e) -> m i q e", i=PACK, e=RUN),
-                    func=ACT.Sigmoid,
+                nc.tensor.matmul_mx(
+                    out=bank[:],
+                    lhsT=u_codes[a][:, sites(t)].bitcast(FP8X4),
+                    lhsT_scale=u_sc[a][:, sites(t)],
+                    rhs=wu[b][:, a, :].bitcast(FP8X4),
+                    rhs_scale=wu_sc[4 * a : P, PASS * b : PASS * (b + 1)],
+                    start=(a == 0),
+                    stop=(a == KP - 1),
                 )
-            else:
-                nc.scalar.activation(out=gate[b, j], in_=bank[:], func=ACT.Sigmoid)
+            nc.scalar.activation(
+                out=gate[b][:, t, :].rearrange("m (i q e) -> m i q e", i=PACK, e=RUN),
+                in_=bank[:].rearrange("m (q i e) -> m i q e", i=PACK, e=RUN),
+                func=ACT.Sigmoid,
+            )
 
-        def pick(b, i, after=None):
-            x[b, i] = sb("x%d_%d" % (b, i), [P, M], F32, tag=after)[:]
-            nc.vector.tensor_tensor(x[b, i], h[b, i][:].indirect(offs2_sb[:]), neg_wgt[:], ALU.mult)
-
-        def difference(b, t):
-            if b in TURNED:
-                d_t[b, t] = new_bank(t)
-                ms = slice(P * t, P * (t + 1))
-                for i in range(PACK):
-                    dst = d_t[b, t][:, P * i : P * (i + 1)]
-                    nc.tensor.matmul(out=dst, lhsT=old_sb[b][:, i, ms], rhs=ident[:], is_transpose=True, start=True, stop=False)
-                    nc.tensor.matmul(out=dst, lhsT=x[b, i][:, ms], rhs=ident[:], is_transpose=True, start=False, stop=True)
-
-
-        def difference_flat(b, i):
-            if i == 0:
-                flat["d"] = sb("d_flat", [P, PACK, M], F32, tag="h1_3")
-            nc.gpsimd.tensor_tensor(flat["d"][:, i, :], old_sb[b][:, i, :], x[b, i], ALU.add)
-
-        def gated_flat(b, i0, i1):
-            if i0 == 0:
-                flat["e"] = sb("e_flat", [P, PACK, M], F32)
-            nc.vector.tensor_tensor(flat["e"][:, i0:i1, :], flat["d"][:, i0:i1, :], gate_all[b][:, i0:i1, :], ALU.mult)
-
-        def gated(b, i):
-            if i == 0:
-                flat["e_t"] = sb("e_turned", [P, MT, PASS], F32, tag="neg_wgt")
-            e_t[b, i] = flat["e_t"][:, i, :]
-            nc.vector.tensor_tensor(e_t[b, i], d_t[b, i][:], gate[b, i], ALU.mult)
+        def turn(bank, src):
+            view = bank[:].rearrange("p (i m) -> p i m", i=PACK)
+            for i in range(PACK):
+                nc.tensor.transpose(view[:, i, :], src[:, P * i : P * (i + 1)], ident[:])
+            return view
 
         z_codes = [sb("z_codes%d" % b, [P, M], U32) for b in range(RP)]
         z_sc = [sb("z_sc%d" % b, [P, M], U8) for b in range(RP)]
         z_bf = [sb("z_bf%d" % b, [P, M, PACK], BF16) for b in range(RP)]
 
-        def make_z(b, t, tiles=1):
-            ms = slice(P * t, P * (t + tiles))
-            if b in TURNED:
-                bank = new_bank("mm")
-                if b == RP - 1 and WARM:
-                    nc.tensor.matmul_mx(
-                        out=bank[:],
-                        lhsT=u_codes[0][:, 0:P].bitcast(FP8X4),
-                        lhsT_scale=u_sc[0][:, 0:P],
-                        rhs=wu[b][:, 0, :].bitcast(FP8X4),
-                        rhs_scale=wu_sc[:, PASS * b : PASS * (b + 1)],
-                        start=True,
-                        stop=True,
-                    )
-                e = bank[:].rearrange("p (i m) -> p i m", i=PACK)
-                for i in range(PACK):
-                    nc.tensor.transpose(e[:, i, :], e_t[b, t][:, P * i : P * (i + 1)], ident[:])
-            else:
-                e = flat["e"][:, :, ms]
-            nc.vector.tensor_tensor(interleaved(z_bf[b][:, ms, :]), planar(old_sb[b][:, :, ms]), planar(e), ALU.subtract)
+        def make_z(b, t, step):
+            dst = interleaved(z_bf[b][:, sites(t), :])
+            nc.vector.tensor_tensor(dst, planar(old_sb[b][:, :, sites(t)]), planar(step), ALU.subtract)
 
         def quantize_z(b, t, tiles=1):
-            ms = slice(P * t, P * (t + tiles))
-            quantize(z_codes[b][:, ms], z_sc[b][:, ms], z_bf[b][:, ms, :].rearrange("p m i -> p (m i)"))
+            quantize(z_codes[b][:, sites(t, tiles)], z_sc[b][:, sites(t, tiles)], z_bf[b][:, sites(t, tiles), :])
 
-        rounded = {}
         wo_codes = sb("wo_codes", [P, RP * N], U32)
         wo_sc = sb("wo_sc", [P, RP * N], U8)
-
-        def cast_wo(b):
-            if b == 0:
-                rounded[0] = sb("wo_bf", [P, RP * N, PACK], BF16, tag="gate0")
-            for c0 in range(0, N, N // 2):
-                nc.scalar.copy(out=interleaved(rounded[0][:, N * b + c0 : N * b + c0 + N // 2, :]), in_=planar(wo_raw[b][:, :, c0 : c0 + N // 2]))
-
-        def quantize_wo(b):
-            for c0, c1 in ((N * b, N * b + 2 * P), (N * b + 2 * P, N * (b + 1))):
-                quantize(wo_codes[:, c0:c1], wo_sc[:, c0:c1], rounded[0][:, c0:c1, :].rearrange("p n i -> p (n i)"))
-
         out_bank = {}
 
         def project(b, t):
             if b == 0:
-                out_bank[t] = new_bank(t)
+                out_bank[t] = site_bank(t)
             for n in range(NT):
-                ns = slice(N * b + P * n, N * b + P * (n + 1))
+                rows = slice(N * b + P * n, N * b + P * (n + 1))
                 nc.tensor.matmul_mx(
                     out=out_bank[t][:, P * n : P * (n + 1)],
-                    lhsT=wo_codes[:, ns].bitcast(FP8X4),
-                    lhsT_scale=wo_sc[:, ns],
-                    rhs=z_codes[b][:, P * t : P * (t + 1)].bitcast(FP8X4),
-                    rhs_scale=z_sc[b][:, P * t : P * (t + 1)],
+                    lhsT=wo_codes[:, rows].bitcast(FP8X4),
+                    lhsT_scale=wo_sc[:, rows],
+                    rhs=z_codes[b][:, sites(t)].bitcast(FP8X4),
+                    rhs_scale=z_sc[b][:, sites(t)],
                     start=(b == 0 and n == 0),
                     stop=(b == RP - 1 and n == NT - 1),
                 )
@@ -354,12 +300,12 @@ def tile_list_reaching_names_kernel(
             res = sb("res%d" % t, [P, NT, P], F32)
             copy = nc.vector.tensor_copy if t == MT - 1 else nc.scalar.copy
             copy(out=res[:].rearrange("p n m -> p (n m)"), in_=out_bank[t][:, 0 : NT * P])
-            nc.sync.dma_start(out=out[:, P * t : P * (t + 1)].rearrange("(n p) m -> p n m", p=P), in_=res[:])
+            nc.sync.dma_start(out=out[:, sites(t)].rearrange("(n p) m -> p n m", p=P), in_=res[:])
 
-        idle = new_bank(0)
-        for rep in range(4):
+        unread = site_bank(0)
+        for repeat in range(WARM_PASSES):
             nc.tensor.matmul_mx(
-                out=idle[:],
+                out=unread[:],
                 lhsT=wd[0][:, 0, 0 : 2 * P].bitcast(FP4X4),
                 lhsT_scale=picked_sc[:, 0:P],
                 rhs=v[0][:, 0:BANK].bitcast(FP8X4),
@@ -367,6 +313,7 @@ def tile_list_reaching_names_kernel(
                 start=True,
                 stop=True,
             )
+
         for a in range(KP):
             for s in range(SH):
                 h_pass(0, 0, s, a)
@@ -375,44 +322,82 @@ def tile_list_reaching_names_kernel(
         for i in range(1, PACK):
             make_h(0, i)
         pick(0, 0)
-        cast_uses(0, nc.vector.tensor_copy)
-        quantize_uses(0)
-        for i in range(PACK):
+        round_uses(0, nc.vector.tensor_copy)
+        for i in range(EARLY_SLOTS):
             make_h(1, i)
-        for i in range(1, PACK):
+        for i in range(EARLY_SLOTS, PACK):
+            for s in range(SH):
+                for a in range(KP):
+                    h_pass(1, i, s, a)
+        pick(0, 1)
+        quantize_uses(0)
+        for i in range(2, PACK):
             pick(0, i)
+
+        turned_difference = []
         for t in range(MT):
-            difference(0, t)
-        cast_uses(1, nc.scalar.copy)
+            turned_difference.append(site_bank(t))
+            for i in range(PACK):
+                dst = turned_difference[t][:, P * i : P * (i + 1)]
+                for src, first in ((old_sb[0], True), (neg_x[0], False)):
+                    nc.tensor.matmul(
+                        out=dst, lhsT=src[:, i, sites(t)], rhs=ident[:], is_transpose=True, start=first, stop=not first
+                    )
+        round_uses(1, nc.scalar.copy)
         quantize_uses(1)
+        for i in range(EARLY_SLOTS, PACK):
+            for s in range(SH):
+                h_copy(1, i, s)
         for t in range(MT):
             make_gate(0, t)
-        for i in range(PACK - 1):
+        for i in range(PACK):
             pick(1, i)
-        permute_wu(1)
-        pick(1, PACK - 1)
-        for i in range(PACK):
-            difference_flat(1, i)
-        for i in range(PACK):
-            make_gate(1, i)
+
+        difference = placed_at(uses1_at, "difference", [P, PACK, M], F32)
         for t in range(MT):
-            gated(0, t)
+            nc.gpsimd.tensor_tensor(difference[:, :, sites(t)], old_sb[1][:, :, sites(t)], neg_x[1][:, :, sites(t)], ALU.add)
         for t in range(MT):
-            make_z(0, t)
-        quantize_z(0, 0, MT)
+            make_gate(1, t)
+
+        turned_step = sb("turned_step", [P, MT, PASS], F32, tag="neg_wgt")
+        for t in range(MT):
+            nc.vector.tensor_tensor(turned_step[:, t, :], turned_difference[t][:], gate[0][:, t, :], ALU.mult)
+        for t in range(MT):
+            make_z(0, t, turn(product_bank(), turned_step[:, t, :]))
+        gate_back = [turn(site_bank(t), gate[1][:, t, :]) for t in range(MT)]
+
+        wo_bf = sb("wo_bf", [P, RP * N, PACK], BF16, tag="gate0")
+        piece = N // 2
         for b in range(RP):
-            cast_wo(b)
-        gated_flat(1, 0, 2)
+            for c in range(0, N, piece):
+                nc.scalar.copy(
+                    out=interleaved(wo_bf[:, N * b + c : N * b + c + piece, :]), in_=planar(wo_raw[b][:, :, c : c + piece])
+                )
+
+        def quantize_wo(b):
+            for c0, c1 in ((N * b, N * b + 2 * P), (N * b + 2 * P, N * (b + 1))):
+                quantize(wo_codes[:, c0:c1], wo_sc[:, c0:c1], wo_bf[:, c0:c1, :])
+
+        step = sb("step", [P, PACK, M], F32)
+
+        def make_step(t):
+            nc.vector.tensor_tensor(step[:, :, sites(t)], gate_back[t], difference[:, :, sites(t)], ALU.mult)
+
+        for t in range(MT // 2):
+            make_step(t)
+        quantize_z(0, 0, MT)
         quantize_wo(0)
+        for t in range(MT // 2, MT):
+            make_step(t)
         for t in range(MT):
             project(0, t)
-        gated_flat(1, 2, 4)
-        for step in range(MT + 1):
-            if step < MT:
-                make_z(1, step)
-            if step == 0:
+
+        for t in range(MT + 1):
+            if t < MT:
+                make_z(1, t, step[:, :, sites(t)])
+            if t == 0:
                 quantize_wo(1)
-            if step >= 1:
-                quantize_z(1, step - 1)
-                project(1, step - 1)
-                store(step - 1)
+            else:
+                quantize_z(1, t - 1)
+                project(1, t - 1)
+                store(t - 1)

@@ -56,7 +56,9 @@ def tile_list_reaching_names_kernel(
         wu_sc_at = 4 * float_columns
         wu_at = wu_sc_at + H
         tab_sc_at = wu_sc_at - T // 4
-        uses1_at = wu_at + 4 * RP * KP * PASS
+        difference_at = wu_at + 4 * RP * KP * PASS
+        uses1_at = difference_at + 2 * S
+        turned_step_at = difference_at + 4 * PACK * M
         wd_raw_at = [uses1_at + 4 * PACK * M - 2 * PASS, uses1_at + 4 * PACK * M]
 
         offs_sb = keep.tile([P, S // LIST], U16, name="offs_sb")
@@ -130,10 +132,10 @@ def tile_list_reaching_names_kernel(
         wo_raw = [four_rows(M + PACK * (M + RP * M + N * b), N) for b in range(RP)]
 
         def interleaved(tile):
-            return tile.rearrange("p (c j) i -> p c i j", j=2)
+            return tile.rearrange("p (c j) i -> p c i j", j=PACK)
 
         def planar(tile):
-            return tile.rearrange("p i (c j) -> p c i j", j=2)
+            return tile.rearrange("p i (c j) -> p c i j", j=PACK)
 
         v = [sb("v%d" % a, [P, S], U32) for a in range(KP)]
         list_columns = BANK // LIST
@@ -161,15 +163,13 @@ def tile_list_reaching_names_kernel(
         order_wd(0)
         gather_words(0, 0)
         uses_raw.append(placed_at(uses1_at, "uses1", [P, PACK, M], F32)[:])
-        load_wd(1)
-        nc.sync.dma_start(out=wgt_sb, in_=wgt)
         load_uses(0)
+        nc.sync.dma_start(out=wgt_sb, in_=wgt)
+        load_wd(1)
         gather_words(0, 1)
         order_wd_scales(0)
         gather_words(1, 0)
         gather_words(1, 1)
-        order_wd(1)
-        order_wd_scales(1)
 
         load_channels(old_sb[0], old, 0)
         load_uses(1)
@@ -198,24 +198,25 @@ def tile_list_reaching_names_kernel(
             quantize(u_codes[a][:], u_sc[a][:], uses_bf[a][:])
 
         ident = sb("ident", [P, P], F32)
-        neg_wgt = sb("neg_wgt", [P, M], F32)
         make_identity(nc, ident[:])
-        nc.scalar.activation(out=neg_wgt[:], in_=wgt_sb, func=ACT.Copy, scale=-1.0)
 
         h = {}
         h_bank = {}
         gate = [sb("gate%d" % b, [P, MT, PASS], F32) for b in range(RP)]
         neg_x = [sb("neg_x%d" % b, [P, PACK, M], F32) for b in range(RP)]
 
-        def product_bank():
-            return psum.tile([P, BANK], F32, name="product", tag="product", bufs=PRODUCT_BANKS)
+        def bank_tile(n):
+            return psum.tile([P, BANK], F32, name="bank", tag="bank%d" % n)
+
+        def product_bank(t):
+            return bank_tile(MT + t)
 
         def site_bank(t):
-            return psum.tile([P, BANK], F32, name="site", tag="site%d" % t)
+            return bank_tile(t)
 
         def h_pass(b, i, s, a):
             if a == 0:
-                h_bank[b, i, s] = product_bank()
+                h_bank[b, i, s] = bank_tile(SH * i + s)
             nc.tensor.matmul_mx(
                 out=h_bank[b, i, s][:],
                 lhsT=wd[b][:, a, 2 * P * i : 2 * P * (i + 1)].bitcast(FP4X4),
@@ -226,12 +227,16 @@ def tile_list_reaching_names_kernel(
                 stop=(a == KP - 1),
             )
 
-        def h_copy(b, i, s, copy=nc.scalar.copy):
+        def h_copy(b, i, s):
             if s == 0 and b == 1 and i >= EARLY_SLOTS:
                 h[b, i] = placed_at(uses1_at + 4 * S * (i - EARLY_SLOTS), "h%d_%d" % (b, i), [P, S], F32)
             elif s == 0:
                 h[b, i] = sb("h%d_%d" % (b, i), [P, S], F32)
-            copy(out=h[b, i][:, BANK * s : BANK * (s + 1)], in_=h_bank[b, i, s][:])
+            dst, src = h[b, i][:, BANK * s : BANK * (s + 1)], h_bank[b, i, s][:]
+            if b == 1:
+                nc.scalar.copy(out=dst, in_=src)
+            else:
+                nc.scalar.activation(out=dst, in_=src, func=ACT.Copy, scale=-1.0)
 
         def make_h(b, i):
             for s in range(SH):
@@ -240,10 +245,10 @@ def tile_list_reaching_names_kernel(
                 h_copy(b, i, s)
 
         def pick(b, i):
-            nc.vector.tensor_tensor(neg_x[b][:, i, :], h[b, i][:].indirect(offs2_sb[:]), neg_wgt[:], ALU.mult)
+            nc.vector.tensor_tensor(neg_x[b][:, i, :], h[b, i][:].indirect(offs2_sb[:]), wgt_sb, ALU.mult)
 
         def make_gate(b, t):
-            bank = product_bank()
+            bank = product_bank(t)
             for a in range(KP):
                 nc.tensor.matmul_mx(
                     out=bank[:],
@@ -302,7 +307,7 @@ def tile_list_reaching_names_kernel(
             copy(out=res[:].rearrange("p n m -> p (n m)"), in_=out_bank[t][:, 0 : NT * P])
             nc.sync.dma_start(out=out[:, sites(t)].rearrange("(n p) m -> p n m", p=P), in_=res[:])
 
-        unread = site_bank(0)
+        unread = bank_tile(2 * MT - 1)
         for repeat in range(WARM_PASSES):
             nc.tensor.matmul_mx(
                 out=unread[:],
@@ -318,11 +323,13 @@ def tile_list_reaching_names_kernel(
             for s in range(SH):
                 h_pass(0, 0, s, a)
         h_copy(0, 0, 0)
-        h_copy(0, 0, 1, nc.vector.tensor_copy)
+        h_copy(0, 0, 1)
         for i in range(1, PACK):
             make_h(0, i)
-        pick(0, 0)
         round_uses(0, nc.vector.tensor_copy)
+        pick(0, 0)
+        order_wd(1)
+        order_wd_scales(1)
         for i in range(EARLY_SLOTS):
             make_h(1, i)
         for i in range(EARLY_SLOTS, PACK):
@@ -334,15 +341,19 @@ def tile_list_reaching_names_kernel(
         for i in range(2, PACK):
             pick(0, i)
 
-        turned_difference = []
+        turned_difference = [site_bank(t) for t in range(MT)]
+
+        def add_turned(src, t, i, start, stop):
+            dst = turned_difference[t][:, P * i : P * (i + 1)]
+            nc.tensor.matmul(out=dst, lhsT=src[:, i, sites(t)], rhs=ident[:], is_transpose=True, start=start, stop=stop)
+
         for t in range(MT):
-            turned_difference.append(site_bank(t))
             for i in range(PACK):
-                dst = turned_difference[t][:, P * i : P * (i + 1)]
-                for src, first in ((old_sb[0], True), (neg_x[0], False)):
-                    nc.tensor.matmul(
-                        out=dst, lhsT=src[:, i, sites(t)], rhs=ident[:], is_transpose=True, start=first, stop=not first
-                    )
+                add_turned(old_sb[0], t, i, i == 0, False)
+            for i in range(PACK - 1):
+                add_turned(neg_x[0], t, i, False, False)
+        for t in range(MT):
+            add_turned(neg_x[0], t, PACK - 1, False, True)
         round_uses(1, nc.scalar.copy)
         quantize_uses(1)
         for i in range(EARLY_SLOTS, PACK):
@@ -353,18 +364,18 @@ def tile_list_reaching_names_kernel(
         for i in range(PACK):
             pick(1, i)
 
-        difference = placed_at(uses1_at, "difference", [P, PACK, M], F32)
+        difference = placed_at(difference_at, "difference", [P, PACK, M], F32)
         for t in range(MT):
-            nc.gpsimd.tensor_tensor(difference[:, :, sites(t)], old_sb[1][:, :, sites(t)], neg_x[1][:, :, sites(t)], ALU.add)
+            nc.gpsimd.tensor_tensor(difference[:, :, sites(t)], old_sb[1][:, :, sites(t)], neg_x[1][:, :, sites(t)], ALU.subtract)
         for t in range(MT):
             make_gate(1, t)
 
-        turned_step = sb("turned_step", [P, MT, PASS], F32, tag="neg_wgt")
+        turned_step = placed_at(turned_step_at, "turned_step", [P, MT, PASS], F32)
         for t in range(MT):
             nc.vector.tensor_tensor(turned_step[:, t, :], turned_difference[t][:], gate[0][:, t, :], ALU.mult)
         for t in range(MT):
-            make_z(0, t, turn(product_bank(), turned_step[:, t, :]))
-        gate_back = [turn(site_bank(t), gate[1][:, t, :]) for t in range(MT)]
+            make_z(0, t, turn(site_bank(t), turned_step[:, t, :]))
+        gate_back = [turn(product_bank(t), gate[1][:, t, :]) for t in range(MT)]
 
         wo_bf = sb("wo_bf", [P, RP * N, PACK], BF16, tag="gate0")
         piece = N // 2

@@ -52,14 +52,14 @@ def tile_list_reaching_names_kernel(
         def sites(t, tiles=1):
             return slice(P * t, P * (t + tiles))
 
-        float_columns = M + PACK * (M + RP * M + RP * N)
+        float_columns = M + PACK * (M + RP * M + RP * N + M // 2)
         wu_sc_at = 4 * float_columns
         wu_at = wu_sc_at + H
         tab_sc_at = wu_sc_at - T // 4
         difference_at = wu_at + 4 * RP * KP * PASS
-        uses1_at = difference_at + 2 * S
+        uses1_at = difference_at + 4 * S
         turned_step_at = difference_at + 4 * PACK * M
-        wd_raw_at = [uses1_at + 4 * PACK * M - 2 * PASS, uses1_at + 4 * PACK * M]
+        wd_raw_at = [uses1_at + 2 * PACK * M - 2 * PASS, uses1_at + 2 * PACK * M]
 
         offs_sb = keep.tile([P, S // LIST], U16, name="offs_sb")
         offs2_sb = keep.tile([P, M // LIST], U16, name="offs2_sb")
@@ -79,9 +79,9 @@ def tile_list_reaching_names_kernel(
         wd_raw = {}
         tab = [sb("tab%d" % a, [P, T], I32) for a in range(KP)]
 
-        def load_uses(a):
-            rows = uses[PASS * a : PASS * (a + 1), :].rearrange("(p i) c -> p i c", i=PACK)
-            nc.sync.dma_start(out=uses_raw[a], in_=rows)
+        def load_uses(a, dst, c0, c1):
+            rows = uses[PASS * a : PASS * (a + 1), c0:c1].rearrange("(p i) c -> p i c", i=PACK)
+            nc.sync.dma_start(out=dst, in_=rows)
 
         def load_channels(dst, src, b):
             slots = src[PASS * b : PASS * (b + 1), :].rearrange("(q i e) c -> i q e c", i=PACK, e=RUN)
@@ -132,10 +132,10 @@ def tile_list_reaching_names_kernel(
         wo_raw = [four_rows(M + PACK * (M + RP * M + N * b), N) for b in range(RP)]
 
         def interleaved(tile):
-            return tile.rearrange("p (c j) i -> p c i j", j=PACK)
+            return tile.rearrange("p (c j) i -> p c i j", j=2)
 
         def planar(tile):
-            return tile.rearrange("p i (c j) -> p c i j", j=PACK)
+            return tile.rearrange("p i (c j) -> p c i j", j=2)
 
         v = [sb("v%d" % a, [P, S], U32) for a in range(KP)]
         list_columns = BANK // LIST
@@ -162,17 +162,19 @@ def tile_list_reaching_names_kernel(
 
         order_wd(0)
         gather_words(0, 0)
-        uses_raw.append(placed_at(uses1_at, "uses1", [P, PACK, M], F32)[:])
-        load_uses(0)
+        uses1_scalar = placed_at(uses1_at, "uses1", [P, PACK, M // 2], F32)[:]
+        uses1_vector = four_rows(M + PACK * (M + RP * M + RP * N), M // 2)
         nc.sync.dma_start(out=wgt_sb, in_=wgt)
         load_wd(1)
+        load_uses(0, uses_raw[0], 0, M)
         gather_words(0, 1)
         order_wd_scales(0)
         gather_words(1, 0)
         gather_words(1, 1)
 
         load_channels(old_sb[0], old, 0)
-        load_uses(1)
+        load_uses(1, uses1_scalar, 0, M // 2)
+        load_uses(1, uses1_vector, M // 2, M)
         for quad in QUADRANTS:
             nc.sync.dma_start(
                 out=wu_sc[32 * quad : 32 * quad + 8, :].bitcast(I32),
@@ -191,14 +193,16 @@ def tile_list_reaching_names_kernel(
         def quantize(codes, scales, src):
             nc.vector.quantize_mx(out=codes.bitcast(FP8X4), scales=scales, in_=src.rearrange("p c i -> p (c i)"))
 
-        def round_uses(a, copy):
-            copy(out=interleaved(uses_bf[a][:]), in_=planar(uses_raw[a]))
+        def round_uses(a, copy, src, c0, c1):
+            copy(out=interleaved(uses_bf[a][:, c0:c1, :]), in_=planar(src))
 
         def quantize_uses(a):
             quantize(u_codes[a][:], u_sc[a][:], uses_bf[a][:])
 
         ident = sb("ident", [P, P], F32)
         make_identity(nc, ident[:])
+        neg_wgt = sb("neg_wgt", [P, M], F32)
+        nc.scalar.activation(out=neg_wgt[:], in_=wgt_sb, func=ACT.Copy, scale=-1.0)
 
         h = {}
         h_bank = {}
@@ -227,16 +231,12 @@ def tile_list_reaching_names_kernel(
                 stop=(a == KP - 1),
             )
 
-        def h_copy(b, i, s):
+        def h_copy(b, i, s, copy=nc.scalar.copy):
             if s == 0 and b == 1 and i >= EARLY_SLOTS:
-                h[b, i] = placed_at(uses1_at + 4 * S * (i - EARLY_SLOTS), "h%d_%d" % (b, i), [P, S], F32)
+                h[b, i] = placed_at(uses1_at - 2 * S + 4 * S * (i - EARLY_SLOTS), "h%d_%d" % (b, i), [P, S], F32)
             elif s == 0:
                 h[b, i] = sb("h%d_%d" % (b, i), [P, S], F32)
-            dst, src = h[b, i][:, BANK * s : BANK * (s + 1)], h_bank[b, i, s][:]
-            if b == 1:
-                nc.scalar.copy(out=dst, in_=src)
-            else:
-                nc.scalar.activation(out=dst, in_=src, func=ACT.Copy, scale=-1.0)
+            copy(out=h[b, i][:, BANK * s : BANK * (s + 1)], in_=h_bank[b, i, s][:])
 
         def make_h(b, i):
             for s in range(SH):
@@ -245,7 +245,7 @@ def tile_list_reaching_names_kernel(
                 h_copy(b, i, s)
 
         def pick(b, i):
-            nc.vector.tensor_tensor(neg_x[b][:, i, :], h[b, i][:].indirect(offs2_sb[:]), wgt_sb, ALU.mult)
+            nc.vector.tensor_tensor(neg_x[b][:, i, :], h[b, i][:].indirect(offs2_sb[:]), neg_wgt[:], ALU.mult)
 
         def make_gate(b, t):
             bank = product_bank(t)
@@ -323,11 +323,11 @@ def tile_list_reaching_names_kernel(
             for s in range(SH):
                 h_pass(0, 0, s, a)
         h_copy(0, 0, 0)
-        h_copy(0, 0, 1)
+        h_copy(0, 0, 1, nc.vector.tensor_copy)
         for i in range(1, PACK):
             make_h(0, i)
-        round_uses(0, nc.vector.tensor_copy)
         pick(0, 0)
+        round_uses(0, nc.vector.tensor_copy, uses_raw[0], 0, M)
         order_wd(1)
         order_wd_scales(1)
         for i in range(EARLY_SLOTS):
@@ -354,7 +354,8 @@ def tile_list_reaching_names_kernel(
                 add_turned(neg_x[0], t, i, False, False)
         for t in range(MT):
             add_turned(neg_x[0], t, PACK - 1, False, True)
-        round_uses(1, nc.scalar.copy)
+        round_uses(1, nc.scalar.copy, uses1_scalar, 0, M // 2)
+        round_uses(1, nc.vector.tensor_copy, uses1_vector, M // 2, M)
         quantize_uses(1)
         for i in range(EARLY_SLOTS, PACK):
             for s in range(SH):
@@ -366,7 +367,7 @@ def tile_list_reaching_names_kernel(
 
         difference = placed_at(difference_at, "difference", [P, PACK, M], F32)
         for t in range(MT):
-            nc.gpsimd.tensor_tensor(difference[:, :, sites(t)], old_sb[1][:, :, sites(t)], neg_x[1][:, :, sites(t)], ALU.subtract)
+            nc.gpsimd.tensor_tensor(difference[:, :, sites(t)], old_sb[1][:, :, sites(t)], neg_x[1][:, :, sites(t)], ALU.add)
         for t in range(MT):
             make_gate(1, t)
 

@@ -171,6 +171,8 @@ def tile_list_reaching_names_kernel(
         order_wd_scales(0)
         gather_words(1, 0)
         gather_words(1, 1)
+        order_wd(1)
+        order_wd_scales(1)
 
         load_channels(old_sb[0], old, 0)
         load_uses(1, uses1_scalar, 0, M // 2)
@@ -186,7 +188,7 @@ def tile_list_reaching_names_kernel(
         for b in range(RP):
             load_channels(wo_raw[b], wo, b)
 
-        uses_bf = [sb("uses_bf%d" % a, [P, M, PACK], BF16) for a in range(KP)]
+        uses_bf = {1: sb("uses_bf1", [P, M, PACK], BF16)}
         u_codes = [sb("u_codes%d" % a, [P, M], U32) for a in range(KP)]
         u_sc = [sb("u_sc%d" % a, [P, M], U8) for a in range(KP)]
 
@@ -196,8 +198,8 @@ def tile_list_reaching_names_kernel(
         def round_uses(a, copy, src, c0, c1):
             copy(out=interleaved(uses_bf[a][:, c0:c1, :]), in_=planar(src))
 
-        def quantize_uses(a):
-            quantize(u_codes[a][:], u_sc[a][:], uses_bf[a][:])
+        def quantize_uses(a, c0, c1):
+            quantize(u_codes[a][:, c0:c1], u_sc[a][:, c0:c1], uses_bf[a][:, c0:c1, :])
 
         ident = sb("ident", [P, P], F32)
         make_identity(nc, ident[:])
@@ -327,9 +329,8 @@ def tile_list_reaching_names_kernel(
         for i in range(1, PACK):
             make_h(0, i)
         pick(0, 0)
+        uses_bf[0] = sb("uses_bf0", [P, M, PACK], BF16, tag="h0_0")
         round_uses(0, nc.vector.tensor_copy, uses_raw[0], 0, M)
-        order_wd(1)
-        order_wd_scales(1)
         for i in range(EARLY_SLOTS):
             make_h(1, i)
         for i in range(EARLY_SLOTS, PACK):
@@ -337,7 +338,7 @@ def tile_list_reaching_names_kernel(
                 for a in range(KP):
                     h_pass(1, i, s, a)
         pick(0, 1)
-        quantize_uses(0)
+        quantize_uses(0, 0, M)
         for i in range(2, PACK):
             pick(0, i)
 
@@ -355,11 +356,12 @@ def tile_list_reaching_names_kernel(
         for t in range(MT):
             add_turned(neg_x[0], t, PACK - 1, False, True)
         round_uses(1, nc.scalar.copy, uses1_scalar, 0, M // 2)
-        round_uses(1, nc.vector.tensor_copy, uses1_vector, M // 2, M)
-        quantize_uses(1)
+        quantize_uses(1, 0, M // 2)
         for i in range(EARLY_SLOTS, PACK):
             for s in range(SH):
                 h_copy(1, i, s)
+        round_uses(1, nc.scalar.copy, uses1_vector, M // 2, M)
+        quantize_uses(1, M // 2, M)
         for t in range(MT):
             make_gate(0, t)
         for i in range(PACK):
@@ -374,7 +376,8 @@ def tile_list_reaching_names_kernel(
         turned_step = placed_at(turned_step_at, "turned_step", [P, MT, PASS], F32)
         for t in range(MT):
             nc.vector.tensor_tensor(turned_step[:, t, :], turned_difference[t][:], gate[0][:, t, :], ALU.mult)
-        for t in range(MT):
+        last = MT - 1
+        for t in range(last):
             make_z(0, t, turn(site_bank(t), turned_step[:, t, :]))
         gate_back = [turn(product_bank(t), gate[1][:, t, :]) for t in range(MT)]
 
@@ -387,23 +390,36 @@ def tile_list_reaching_names_kernel(
                 )
 
         def quantize_wo(b):
-            for c0, c1 in ((N * b, N * b + 2 * P), (N * b + 2 * P, N * (b + 1))):
-                quantize(wo_codes[:, c0:c1], wo_sc[:, c0:c1], wo_bf[:, c0:c1, :])
+            c0, c1 = ((0, PACK * P), (PACK * P, RP * N))[b]
+            quantize(wo_codes[:, c0:c1], wo_sc[:, c0:c1], wo_bf[:, c0:c1, :])
 
         step = sb("step", [P, PACK, M], F32)
 
         def make_step(t):
             nc.vector.tensor_tensor(step[:, :, sites(t)], gate_back[t], difference[:, :, sites(t)], ALU.mult)
 
-        for t in range(MT // 2):
-            make_step(t)
-        quantize_z(0, 0, MT)
-        quantize_wo(0)
-        for t in range(MT // 2, MT):
-            make_step(t)
         for t in range(MT):
-            project(0, t)
+            make_step(t)
+        neg_old = sb("neg_old", [P, PASS], F32)
+        bank = site_bank(last)
+        for i in range(PACK):
+            nc.tensor.transpose(bank[:, P * i : P * (i + 1)], old_sb[0][:, i, sites(last)], ident[:])
+        nc.scalar.activation(out=neg_old[:], in_=bank[:], func=ACT.Copy, scale=-1.0)
+        bank = site_bank(last)
+        for i in range(PACK):
+            for src, first in ((turned_step[:, last, :], True), (neg_old[:], False)):
+                nc.tensor.matmul(
+                    out=bank[:, P * i : P * (i + 1)], lhsT=src[:, P * i : P * (i + 1)], rhs=ident[:],
+                    is_transpose=True, start=first, stop=not first,
+                )
+        nc.scalar.activation(
+            out=z_bf[0][:, sites(last), :], in_=bank[:].rearrange("p (i m) -> p m i", i=PACK), func=ACT.Copy, scale=-1.0
+        )
 
+        quantize_z(0, 0, 2)
+        quantize_wo(0)
+        project(0, 0)
+        project(0, 1)
         for t in range(MT + 1):
             if t < MT:
                 make_z(1, t, step[:, :, sites(t)])
@@ -413,3 +429,6 @@ def tile_list_reaching_names_kernel(
                 quantize_z(1, t - 1)
                 project(1, t - 1)
                 store(t - 1)
+            if t in (0, 2):
+                quantize_z(0, 2 + t // 2)
+                project(0, 2 + t // 2)

@@ -28,9 +28,8 @@ RP = H // PASS
 MT = M // P
 NT = N // P
 SH = S // BANK
-PRODUCT_BANKS = 4
 QUADRANTS = (0, 2, 1, 3)
-WARM_PASSES = 4
+WARM_PASSES = 3
 EARLY_SLOTS = 2
 
 
@@ -52,14 +51,14 @@ def tile_list_reaching_names_kernel(
         def sites(t, tiles=1):
             return slice(P * t, P * (t + tiles))
 
-        float_columns = M + PACK * (M + RP * M + RP * N + M // 2)
+        float_columns = M + PACK * (M + RP * M + RP * N)
         wu_sc_at = 4 * float_columns
         wu_at = wu_sc_at + H
         tab_sc_at = wu_sc_at - T // 4
         difference_at = wu_at + 4 * RP * KP * PASS
-        uses1_at = difference_at + 4 * S
+        uses1_at = difference_at + 2 * S
         turned_step_at = difference_at + 4 * PACK * M
-        wd_raw_at = [uses1_at + 2 * PACK * M - 2 * PASS, uses1_at + 2 * PACK * M]
+        wd_raw_at = [uses1_at + 4 * PACK * M - 2 * PASS, uses1_at + 4 * PACK * M]
 
         offs_sb = keep.tile([P, S // LIST], U16, name="offs_sb")
         offs2_sb = keep.tile([P, M // LIST], U16, name="offs2_sb")
@@ -79,9 +78,9 @@ def tile_list_reaching_names_kernel(
         wd_raw = {}
         tab = [sb("tab%d" % a, [P, T], I32) for a in range(KP)]
 
-        def load_uses(a, dst, c0, c1):
-            rows = uses[PASS * a : PASS * (a + 1), c0:c1].rearrange("(p i) c -> p i c", i=PACK)
-            nc.sync.dma_start(out=dst, in_=rows)
+        def load_uses(a):
+            rows = uses[PASS * a : PASS * (a + 1), :].rearrange("(p i) c -> p i c", i=PACK)
+            nc.sync.dma_start(out=uses_raw[a], in_=rows)
 
         def load_channels(dst, src, b):
             slots = src[PASS * b : PASS * (b + 1), :].rearrange("(q i e) c -> i q e c", i=PACK, e=RUN)
@@ -162,11 +161,10 @@ def tile_list_reaching_names_kernel(
 
         order_wd(0)
         gather_words(0, 0)
-        uses1_scalar = placed_at(uses1_at, "uses1", [P, PACK, M // 2], F32)[:]
-        uses1_vector = four_rows(M + PACK * (M + RP * M + RP * N), M // 2)
+        uses_raw.append(placed_at(uses1_at, "uses1", [P, PACK, M], F32)[:])
         nc.sync.dma_start(out=wgt_sb, in_=wgt)
         load_wd(1)
-        load_uses(0, uses_raw[0], 0, M)
+        load_uses(0)
         gather_words(0, 1)
         order_wd_scales(0)
         gather_words(1, 0)
@@ -175,8 +173,7 @@ def tile_list_reaching_names_kernel(
         order_wd_scales(1)
 
         load_channels(old_sb[0], old, 0)
-        load_uses(1, uses1_scalar, 0, M // 2)
-        load_uses(1, uses1_vector, M // 2, M)
+        load_uses(1)
         for quad in QUADRANTS:
             nc.sync.dma_start(
                 out=wu_sc[32 * quad : 32 * quad + 8, :].bitcast(I32),
@@ -195,11 +192,11 @@ def tile_list_reaching_names_kernel(
         def quantize(codes, scales, src):
             nc.vector.quantize_mx(out=codes.bitcast(FP8X4), scales=scales, in_=src.rearrange("p c i -> p (c i)"))
 
-        def round_uses(a, copy, src, c0, c1):
-            copy(out=interleaved(uses_bf[a][:, c0:c1, :]), in_=planar(src))
+        def round_uses(a, copy):
+            copy(out=interleaved(uses_bf[a][:]), in_=planar(uses_raw[a]))
 
-        def quantize_uses(a, c0, c1):
-            quantize(u_codes[a][:, c0:c1], u_sc[a][:, c0:c1], uses_bf[a][:, c0:c1, :])
+        def quantize_uses(a):
+            quantize(u_codes[a][:], u_sc[a][:], uses_bf[a][:])
 
         ident = sb("ident", [P, P], F32)
         make_identity(nc, ident[:])
@@ -214,7 +211,7 @@ def tile_list_reaching_names_kernel(
         def bank_tile(n):
             return psum.tile([P, BANK], F32, name="bank", tag="bank%d" % n)
 
-        def product_bank(t):
+        def gate_bank(t):
             return bank_tile(MT + t)
 
         def site_bank(t):
@@ -235,7 +232,7 @@ def tile_list_reaching_names_kernel(
 
         def h_copy(b, i, s, copy=nc.scalar.copy):
             if s == 0 and b == 1 and i >= EARLY_SLOTS:
-                h[b, i] = placed_at(uses1_at - 2 * S + 4 * S * (i - EARLY_SLOTS), "h%d_%d" % (b, i), [P, S], F32)
+                h[b, i] = placed_at(uses1_at + 4 * S * (i - EARLY_SLOTS), "h%d_%d" % (b, i), [P, S], F32)
             elif s == 0:
                 h[b, i] = sb("h%d_%d" % (b, i), [P, S], F32)
             copy(out=h[b, i][:, BANK * s : BANK * (s + 1)], in_=h_bank[b, i, s][:])
@@ -250,7 +247,7 @@ def tile_list_reaching_names_kernel(
             nc.vector.tensor_tensor(neg_x[b][:, i, :], h[b, i][:].indirect(offs2_sb[:]), neg_wgt[:], ALU.mult)
 
         def make_gate(b, t):
-            bank = product_bank(t)
+            bank = gate_bank(t)
             for a in range(KP):
                 nc.tensor.matmul_mx(
                     out=bank[:],
@@ -321,16 +318,23 @@ def tile_list_reaching_names_kernel(
                 stop=True,
             )
 
+        for s in range(SH):
+            h_pass(0, 0, s, 0)
+        h_pass(0, 0, 0, 1)
         for a in range(KP):
-            for s in range(SH):
-                h_pass(0, 0, s, a)
+            h_pass(0, 1, 0, a)
+        h_pass(0, 1, 1, 0)
+        for i in range(2):
+            h_pass(0, i, 1, 1)
         h_copy(0, 0, 0)
         h_copy(0, 0, 1, nc.vector.tensor_copy)
-        for i in range(1, PACK):
+        for s in range(SH):
+            h_copy(0, 1, s)
+        for i in range(2, PACK):
             make_h(0, i)
         pick(0, 0)
         uses_bf[0] = sb("uses_bf0", [P, M, PACK], BF16, tag="h0_0")
-        round_uses(0, nc.vector.tensor_copy, uses_raw[0], 0, M)
+        round_uses(0, nc.vector.tensor_copy)
         for i in range(EARLY_SLOTS):
             make_h(1, i)
         for i in range(EARLY_SLOTS, PACK):
@@ -338,7 +342,7 @@ def tile_list_reaching_names_kernel(
                 for a in range(KP):
                     h_pass(1, i, s, a)
         pick(0, 1)
-        quantize_uses(0, 0, M)
+        quantize_uses(0)
         for i in range(2, PACK):
             pick(0, i)
 
@@ -355,21 +359,19 @@ def tile_list_reaching_names_kernel(
                 add_turned(neg_x[0], t, i, False, False)
         for t in range(MT):
             add_turned(neg_x[0], t, PACK - 1, False, True)
-        round_uses(1, nc.scalar.copy, uses1_scalar, 0, M // 2)
-        quantize_uses(1, 0, M // 2)
+        round_uses(1, nc.scalar.copy)
+        quantize_uses(1)
         for i in range(EARLY_SLOTS, PACK):
             for s in range(SH):
                 h_copy(1, i, s)
-        round_uses(1, nc.scalar.copy, uses1_vector, M // 2, M)
-        quantize_uses(1, M // 2, M)
         for t in range(MT):
             make_gate(0, t)
         for i in range(PACK):
             pick(1, i)
 
         difference = placed_at(difference_at, "difference", [P, PACK, M], F32)
-        for t in range(MT):
-            nc.gpsimd.tensor_tensor(difference[:, :, sites(t)], old_sb[1][:, :, sites(t)], neg_x[1][:, :, sites(t)], ALU.add)
+        for part in (sites(0), sites(1), sites(2, 2)):
+            nc.gpsimd.tensor_tensor(difference[:, :, part], old_sb[1][:, :, part], neg_x[1][:, :, part], ALU.add)
         for t in range(MT):
             make_gate(1, t)
 
@@ -379,18 +381,39 @@ def tile_list_reaching_names_kernel(
         last = MT - 1
         for t in range(last):
             make_z(0, t, turn(site_bank(t), turned_step[:, t, :]))
-        gate_back = [turn(product_bank(t), gate[1][:, t, :]) for t in range(MT)]
+        gate_back = [turn(gate_bank(t), gate[1][:, t, :]) for t in range(MT)]
 
         wo_bf = sb("wo_bf", [P, RP * N, PACK], BF16, tag="gate0")
         piece = N // 2
-        for b in range(RP):
-            for c in range(0, N, piece):
-                nc.scalar.copy(
-                    out=interleaved(wo_bf[:, N * b + c : N * b + c + piece, :]), in_=planar(wo_raw[b][:, :, c : c + piece])
-                )
 
-        def quantize_wo(b):
-            c0, c1 = ((0, PACK * P), (PACK * P, RP * N))[b]
+        def round_wo(b):
+            for c in range(0, N, piece):
+                dst, src = wo_bf[:, N * b + c : N * b + c + piece, :], wo_raw[b][:, :, c : c + piece]
+                if b == RP - 1 and c == 0:
+                    nc.gpsimd.tensor_scalar(dst, src.rearrange("p i c -> p c i"), 1.0, 0.0, ALU.mult, ALU.add)
+                else:
+                    nc.scalar.copy(out=interleaved(dst), in_=planar(src))
+
+        round_wo(0)
+        neg_old = sb("neg_old", [P, PASS], F32)
+        bank = site_bank(last)
+        for i in range(PACK):
+            nc.tensor.transpose(bank[:, P * i : P * (i + 1)], old_sb[0][:, i, sites(last)], ident[:])
+        nc.scalar.activation(out=neg_old[:], in_=bank[:], func=ACT.Copy, scale=-1.0)
+        round_wo(1)
+        bank = site_bank(last)
+        for i in range(PACK):
+            for src, first in ((turned_step[:, last, :], True), (neg_old[:], False)):
+                slot = slice(P * i, P * (i + 1))
+                nc.tensor.matmul(
+                    out=bank[:, slot], lhsT=src[:, slot], rhs=ident[:], is_transpose=True, start=first, stop=not first
+                )
+        nc.scalar.activation(
+            out=z_bf[0][:, sites(last), :], in_=bank[:].rearrange("p (i m) -> p m i", i=PACK), func=ACT.Copy, scale=-1.0
+        )
+
+        def quantize_wo(part):
+            c0, c1 = ((0, PASS), (PASS, RP * N))[part]
             quantize(wo_codes[:, c0:c1], wo_sc[:, c0:c1], wo_bf[:, c0:c1, :])
 
         step = sb("step", [P, PACK, M], F32)
@@ -400,35 +423,26 @@ def tile_list_reaching_names_kernel(
 
         for t in range(MT):
             make_step(t)
-        neg_old = sb("neg_old", [P, PASS], F32)
-        bank = site_bank(last)
-        for i in range(PACK):
-            nc.tensor.transpose(bank[:, P * i : P * (i + 1)], old_sb[0][:, i, sites(last)], ident[:])
-        nc.scalar.activation(out=neg_old[:], in_=bank[:], func=ACT.Copy, scale=-1.0)
-        bank = site_bank(last)
-        for i in range(PACK):
-            for src, first in ((turned_step[:, last, :], True), (neg_old[:], False)):
-                nc.tensor.matmul(
-                    out=bank[:, P * i : P * (i + 1)], lhsT=src[:, P * i : P * (i + 1)], rhs=ident[:],
-                    is_transpose=True, start=first, stop=not first,
-                )
-        nc.scalar.activation(
-            out=z_bf[0][:, sites(last), :], in_=bank[:].rearrange("p (i m) -> p m i", i=PACK), func=ACT.Copy, scale=-1.0
-        )
 
         quantize_z(0, 0, 2)
+        make_z(1, 0, step[:, :, sites(0)])
         quantize_wo(0)
-        project(0, 0)
-        project(0, 1)
-        for t in range(MT + 1):
-            if t < MT:
-                make_z(1, t, step[:, :, sites(t)])
-            if t == 0:
-                quantize_wo(1)
-            else:
-                quantize_z(1, t - 1)
-                project(1, t - 1)
-                store(t - 1)
-            if t in (0, 2):
-                quantize_z(0, 2 + t // 2)
-                project(0, 2 + t // 2)
+        quantize_z(0, 2)
+        for t in range(last):
+            project(0, t)
+        make_z(1, 1, step[:, :, sites(1)])
+        quantize_wo(1)
+
+        def finish(t):
+            quantize_z(1, t)
+            project(1, t)
+            store(t)
+
+        finish(0)
+        make_z(1, 2, step[:, :, sites(2)])
+        finish(1)
+        quantize_z(0, last)
+        project(0, last)
+        make_z(1, last, step[:, :, sites(last)])
+        finish(2)
+        finish(last)

@@ -78,9 +78,9 @@ def tile_list_reaching_names_kernel(
         wd_raw = {}
         tab = [sb("tab%d" % a, [P, T], I32) for a in range(KP)]
 
-        def load_uses(a):
-            rows = uses[PASS * a : PASS * (a + 1), :].rearrange("(p i) c -> p i c", i=PACK)
-            nc.sync.dma_start(out=uses_raw[a], in_=rows)
+        def load_uses(a, dst, cols=slice(0, M)):
+            rows = uses[PASS * a : PASS * (a + 1), cols].rearrange("(p i) c -> p i c", i=PACK)
+            nc.sync.dma_start(out=dst, in_=rows)
 
         def load_channels(dst, src, b):
             slots = src[PASS * b : PASS * (b + 1), :].rearrange("(q i e) c -> i q e c", i=PACK, e=RUN)
@@ -126,7 +126,8 @@ def tile_list_reaching_names_kernel(
         wgt_sb = floats[:, 0:M]
         wu = [wu_all[:, KP * PASS * b : KP * PASS * (b + 1)].rearrange("p (a c) -> p a c", a=KP) for b in range(RP)]
         nc.gpsimd.memset(wu_sc[:].bitcast(I32), 0)
-        uses_raw = [four_rows(M, M)]
+        uses_raw = [None]
+        uses0 = [four_rows(M + PACK * (M // 2) * c, M // 2) for c in range(2)]
         old_sb = [four_rows(M + PACK * (M + M * b), M) for b in range(RP)]
         wo_raw = [four_rows(M + PACK * (M + RP * M + N * b), N) for b in range(RP)]
 
@@ -162,9 +163,10 @@ def tile_list_reaching_names_kernel(
         order_wd(0)
         gather_words(0, 0)
         uses_raw.append(placed_at(uses1_at, "uses1", [P, PACK, M], F32)[:])
-        nc.sync.dma_start(out=wgt_sb, in_=wgt)
         load_wd(1)
-        load_uses(0)
+        load_uses(0, uses0[0], sites(0, 2))
+        nc.sync.dma_start(out=wgt_sb, in_=wgt)
+        load_uses(0, uses0[1], sites(2, 2))
         gather_words(0, 1)
         order_wd_scales(0)
         gather_words(1, 0)
@@ -173,7 +175,7 @@ def tile_list_reaching_names_kernel(
         order_wd_scales(1)
 
         load_channels(old_sb[0], old, 0)
-        load_uses(1)
+        load_uses(1, uses_raw[1])
         for quad in QUADRANTS:
             nc.sync.dma_start(
                 out=wu_sc[32 * quad : 32 * quad + 8, :].bitcast(I32),
@@ -200,8 +202,6 @@ def tile_list_reaching_names_kernel(
 
         ident = sb("ident", [P, P], F32)
         make_identity(nc, ident[:])
-        neg_wgt = sb("neg_wgt", [P, M], F32)
-        nc.scalar.activation(out=neg_wgt[:], in_=wgt_sb, func=ACT.Copy, scale=-1.0)
 
         h = {}
         h_bank = {}
@@ -230,12 +230,13 @@ def tile_list_reaching_names_kernel(
                 stop=(a == KP - 1),
             )
 
-        def h_copy(b, i, s, copy=nc.scalar.copy):
+        def h_copy(b, i, s):
             if s == 0 and b == 1 and i >= EARLY_SLOTS:
                 h[b, i] = placed_at(uses1_at + 4 * S * (i - EARLY_SLOTS), "h%d_%d" % (b, i), [P, S], F32)
             elif s == 0:
                 h[b, i] = sb("h%d_%d" % (b, i), [P, S], F32)
-            copy(out=h[b, i][:, BANK * s : BANK * (s + 1)], in_=h_bank[b, i, s][:])
+            dst = h[b, i][:, BANK * s : BANK * (s + 1)]
+            nc.scalar.activation(out=dst, in_=h_bank[b, i, s][:], func=ACT.Copy, scale=-1.0)
 
         def make_h(b, i):
             for s in range(SH):
@@ -244,7 +245,7 @@ def tile_list_reaching_names_kernel(
                 h_copy(b, i, s)
 
         def pick(b, i):
-            nc.vector.tensor_tensor(neg_x[b][:, i, :], h[b, i][:].indirect(offs2_sb[:]), neg_wgt[:], ALU.mult)
+            nc.vector.tensor_tensor(neg_x[b][:, i, :], h[b, i][:].indirect(offs2_sb[:]), wgt_sb, ALU.mult)
 
         def make_gate(b, t):
             bank = gate_bank(t)
@@ -327,14 +328,17 @@ def tile_list_reaching_names_kernel(
         for i in range(2):
             h_pass(0, i, 1, 1)
         h_copy(0, 0, 0)
-        h_copy(0, 0, 1, nc.vector.tensor_copy)
+        h_copy(0, 0, 1)
         for s in range(SH):
             h_copy(0, 1, s)
         for i in range(2, PACK):
             make_h(0, i)
+        early_bf = sb("early_bf", [P, M // 2, PACK], BF16)
+        nc.vector.tensor_copy(out=interleaved(early_bf[:]), in_=planar(uses0[0]))
         pick(0, 0)
-        uses_bf[0] = sb("uses_bf0", [P, M, PACK], BF16, tag="h0_0")
-        round_uses(0, nc.vector.tensor_copy)
+        quantize(u_codes[0][:, sites(0, 2)], u_sc[0][:, sites(0, 2)], early_bf[:])
+        late_bf = sb("late_bf", [P, M // 2, PACK], BF16, tag="h0_0")
+        nc.vector.tensor_copy(out=interleaved(late_bf[:]), in_=planar(uses0[1]))
         for i in range(EARLY_SLOTS):
             make_h(1, i)
         for i in range(EARLY_SLOTS, PACK):
@@ -342,7 +346,7 @@ def tile_list_reaching_names_kernel(
                 for a in range(KP):
                     h_pass(1, i, s, a)
         pick(0, 1)
-        quantize_uses(0)
+        quantize(u_codes[0][:, sites(2, 2)], u_sc[0][:, sites(2, 2)], late_bf[:])
         for i in range(2, PACK):
             pick(0, i)
 

@@ -52,17 +52,17 @@ def tile_list_reaching_names_kernel(
             return slice(P * t, P * (t + tiles))
 
         float_columns = M + PACK * (M + RP * M + RP * N)
-        wu_sc_at = 4 * float_columns
-        wu_at = wu_sc_at + H
-        tab_sc_at = wu_sc_at - T // 4
-        difference_at = wu_at + 4 * RP * KP * PASS
+        difference_at = 4 * float_columns
         uses1_at = difference_at + 2 * S
         turned_step_at = difference_at + 4 * PACK * M
-        wd_raw_at = [uses1_at + 4 * PACK * M - 2 * PASS, uses1_at + 4 * PACK * M]
+        wd1_at = uses1_at + 4 * PACK * M
+        wu_sc_at = turned_step_at + 4 * MT * PASS
+        wu_at = wu_sc_at + H
+        tab_sc_at = difference_at - 64
 
         offs_sb = keep.tile([P, S // LIST], U16, name="offs_sb")
         offs2_sb = keep.tile([P, M // LIST], U16, name="offs2_sb")
-        tab_sc = placed_at(tab_sc_at, "tab_sc", [P, T], U8)
+        tab_sc = placed_at(tab_sc_at, "tab_sc", [P, wu_at + 64 - tab_sc_at], U8)[:, 0:T]
         wd_sc = sb("wd_sc", [P, KP, H], U8)
         picked_sc = sb("picked_sc", [P, S], U8)
         v_sc = sb("v_sc", [P, KP, S], U8)
@@ -91,7 +91,8 @@ def tile_list_reaching_names_kernel(
             nc.sync.dma_start(out=tab[a][:], in_=tab_words[a].rearrange("p t i -> p (t i)").bitcast(I32))
 
         def load_wd(b):
-            wd_raw[b] = placed_at(wd_raw_at[b], "wd_raw%d" % b, [P, KP, 2 * PASS], U8)
+            shape = [P, KP, 2 * PASS]
+            wd_raw[b] = placed_at(wd1_at, "wd_raw1", shape, U8) if b else sb("wd_raw0", shape, U8)
             src = wd_words.rearrange("a p c -> p a c")[:, :, 2 * PASS * b : 2 * PASS * (b + 1)]
             nc.sync.dma_start(out=wd_raw[b][:].bitcast(I32), in_=src.bitcast(I32))
 
@@ -101,7 +102,6 @@ def tile_list_reaching_names_kernel(
 
         nc.sync.dma_start(out=tab_sc[0:32, :].bitcast(I32), in_=tab_scales.rearrange("a q c -> q a c").bitcast(I32))
         nc.sync.dma_start(offs_sb[:], offs)
-        load_wd(0)
         load_tab(0)
         nc.sync.dma_start(offs2_sb[:], offs2)
         for quad in QUADRANTS:
@@ -110,7 +110,8 @@ def tile_list_reaching_names_kernel(
                 in_=wd_scales[:, 4 * quad : 4 * quad + 4, :].rearrange("a r c -> r a c").bitcast(I32),
             )
         load_tab(1)
-        nc.vector.tensor_copy(picked_sc[:], tab_sc[:].indirect(offs_sb[:]))
+        load_wd(0)
+        nc.vector.tensor_copy(picked_sc[:], tab_sc.indirect(offs_sb[:]))
         for quad in QUADRANTS:
             nc.sync.dma_start(
                 out=v_sc[32 * quad : 32 * quad + 4, :, :].bitcast(I32),
@@ -147,20 +148,19 @@ def tile_list_reaching_names_kernel(
         wd = [sb("wd%d" % b, [P, KP, 2 * PASS], U8) for b in range(RP)]
         wd_s = [sb("wd_s%d" % b, [P, KP, PASS], U8) for b in range(RP)]
 
-        def slot_major(dst, src):
+        def slot_major(dst, src, slots=slice(0, PACK)):
             words = dst.shape[2] // (PASS // RUN)
-            nc.vector.tensor_copy(
-                out=dst.rearrange("p a (i q w) -> p a i q w", i=PACK, w=words),
-                in_=src.rearrange("p a (q i w) -> p a i q w", i=PACK, w=words),
+            nc.gpsimd.tensor_copy(
+                out=dst.rearrange("p a (i q w) -> p a i q w", i=PACK, w=words)[:, :, slots],
+                in_=src.rearrange("p a (q i w) -> p a i q w", i=PACK, w=words)[:, :, slots],
             )
 
-        def order_wd(b):
-            slot_major(wd[b][:].bitcast(I32), wd_raw[b][:].bitcast(I32))
+        def order_wd(b, slots=slice(0, PACK)):
+            slot_major(wd[b][:].bitcast(I32), wd_raw[b][:].bitcast(I32), slots)
 
         def order_wd_scales(b):
             slot_major(wd_s[b][:].bitcast(I32), wd_sc[:, :, PASS * b : PASS * (b + 1)].bitcast(I32))
 
-        order_wd(0)
         gather_words(0, 0)
         uses_raw.append(placed_at(uses1_at, "uses1", [P, PACK, M], F32)[:])
         load_wd(1)
@@ -168,11 +168,13 @@ def tile_list_reaching_names_kernel(
         nc.sync.dma_start(out=wgt_sb, in_=wgt)
         load_uses(0, uses0[1], sites(2, 2))
         gather_words(0, 1)
-        order_wd_scales(0)
         gather_words(1, 0)
         gather_words(1, 1)
+        for b in range(RP):
+            order_wd_scales(b)
+        order_wd(0, slice(0, 2))
+        order_wd(0, slice(2, PACK))
         order_wd(1)
-        order_wd_scales(1)
 
         load_channels(old_sb[0], old, 0)
         load_uses(1, uses_raw[1])
@@ -236,7 +238,10 @@ def tile_list_reaching_names_kernel(
             elif s == 0:
                 h[b, i] = sb("h%d_%d" % (b, i), [P, S], F32)
             dst = h[b, i][:, BANK * s : BANK * (s + 1)]
-            nc.scalar.activation(out=dst, in_=h_bank[b, i, s][:], func=ACT.Copy, scale=-1.0)
+            if (b, i, s) == (0, 0, 1):
+                nc.vector.tensor_scalar_mul(dst, h_bank[b, i, s][:], -1.0)
+            else:
+                nc.scalar.activation(out=dst, in_=h_bank[b, i, s][:], func=ACT.Copy, scale=-1.0)
 
         def make_h(b, i):
             for s in range(SH):
@@ -311,7 +316,7 @@ def tile_list_reaching_names_kernel(
         for repeat in range(WARM_PASSES):
             nc.tensor.matmul_mx(
                 out=unread[:],
-                lhsT=wd[0][:, 0, 0 : 2 * P].bitcast(FP4X4),
+                lhsT=v[0][:, 0:P].bitcast(FP8X4),
                 lhsT_scale=picked_sc[:, 0:P],
                 rhs=v[0][:, 0:BANK].bitcast(FP8X4),
                 rhs_scale=picked_sc[:, 0:BANK],
@@ -319,18 +324,11 @@ def tile_list_reaching_names_kernel(
                 stop=True,
             )
 
+        for i, s, a in ((0, 0, 0), (0, 0, 1), (1, 0, 0), (1, 0, 1), (0, 1, 0), (0, 1, 1), (1, 1, 0), (1, 1, 1)):
+            h_pass(0, i, s, a)
         for s in range(SH):
-            h_pass(0, 0, s, 0)
-        h_pass(0, 0, 0, 1)
-        for a in range(KP):
-            h_pass(0, 1, 0, a)
-        h_pass(0, 1, 1, 0)
-        for i in range(2):
-            h_pass(0, i, 1, 1)
-        h_copy(0, 0, 0)
-        h_copy(0, 0, 1)
-        for s in range(SH):
-            h_copy(0, 1, s)
+            for i in range(2):
+                h_copy(0, i, s)
         for i in range(2, PACK):
             make_h(0, i)
         early_bf = sb("early_bf", [P, M // 2, PACK], BF16)

@@ -176,8 +176,8 @@ def tile_list_reaching_names_kernel(
         order_wd(0, slice(2, PACK))
         order_wd(1)
 
-        load_channels(old_sb[0], old, 0)
         load_uses(1, uses_raw[1])
+        load_channels(old_sb[0], old, 0)
         for quad in QUADRANTS:
             nc.sync.dma_start(
                 out=wu_sc[32 * quad : 32 * quad + 8, :].bitcast(I32),

@@ -148,18 +148,13 @@ def tile_list_reaching_names_kernel(
         wd = [sb("wd%d" % b, [P, KP, 2 * PASS], U8) for b in range(RP)]
         wd_s = [sb("wd_s%d" % b, [P, KP, PASS], U8) for b in range(RP)]
 
-        def slot_major(dst, src, slots=slice(0, PACK)):
+        def slot_major(dst, src):
+            dst, src = dst.bitcast(U32), src.bitcast(U32)
             words = dst.shape[2] // (PASS // RUN)
-            nc.gpsimd.tensor_copy(
-                out=dst.rearrange("p a (i q w) -> p a i q w", i=PACK, w=words)[:, :, slots],
-                in_=src.rearrange("p a (q i w) -> p a i q w", i=PACK, w=words)[:, :, slots],
+            nc.scalar.copy(
+                out=dst.rearrange("p a (i q w) -> p a i q w", i=PACK, w=words),
+                in_=src.rearrange("p a (q i w) -> p a i q w", i=PACK, w=words),
             )
-
-        def order_wd(b, slots=slice(0, PACK)):
-            slot_major(wd[b][:].bitcast(I32), wd_raw[b][:].bitcast(I32), slots)
-
-        def order_wd_scales(b):
-            slot_major(wd_s[b][:].bitcast(I32), wd_sc[:, :, PASS * b : PASS * (b + 1)].bitcast(I32))
 
         gather_words(0, 0)
         uses_raw.append(placed_at(uses1_at, "uses1", [P, PACK, M], F32)[:])
@@ -171,10 +166,9 @@ def tile_list_reaching_names_kernel(
         gather_words(1, 0)
         gather_words(1, 1)
         for b in range(RP):
-            order_wd_scales(b)
-        order_wd(0, slice(0, 2))
-        order_wd(0, slice(2, PACK))
-        order_wd(1)
+            slot_major(wd_s[b][:], wd_sc[:, :, PASS * b : PASS * (b + 1)])
+        for b in range(RP):
+            slot_major(wd[b][:], wd_raw[b][:])
 
         load_uses(1, uses_raw[1])
         load_channels(old_sb[0], old, 0)

@@ -21,7 +21,6 @@ P = 128
 PACK = 4
 PASS = P * PACK
 BANK = 512
-RUN = 8
 LIST = 16
 KP = K // PASS
 RP = H // PASS
@@ -83,9 +82,7 @@ def tile_list_reaching_names_kernel(
             nc.sync.dma_start(out=dst, in_=rows)
 
         def load_channels(dst, src, b):
-            slots = src[PASS * b : PASS * (b + 1), :].rearrange("(q i e) c -> i q e c", i=PACK, e=RUN)
-            for i in range(PACK):
-                nc.sync.dma_start(out=dst[:, i, :], in_=slots[i])
+            nc.sync.dma_start(out=dst, in_=src[PASS * b : PASS * (b + 1), :].rearrange("(p i) c -> p i c", i=PACK))
 
         def load_tab(a):
             nc.sync.dma_start(out=tab[a][:], in_=tab_words[a].rearrange("p t i -> p (t i)").bitcast(I32))
@@ -148,13 +145,14 @@ def tile_list_reaching_names_kernel(
         wd = [sb("wd%d" % b, [P, KP, 2 * PASS], U8) for b in range(RP)]
         wd_s = [sb("wd_s%d" % b, [P, KP, PASS], U8) for b in range(RP)]
 
-        def slot_major(dst, src):
-            dst, src = dst.bitcast(U32), src.bitcast(U32)
-            words = dst.shape[2] // (PASS // RUN)
-            nc.scalar.copy(
-                out=dst.rearrange("p a (i q w) -> p a i q w", i=PACK, w=words),
-                in_=src.rearrange("p a (q i w) -> p a i q w", i=PACK, w=words),
+        def slot_major(copy, dst, src, slots=slice(0, PACK)):
+            copy(
+                out=dst.rearrange("p a (i c) -> p a i c", i=PACK)[:, :, slots],
+                in_=src.rearrange("p a (c i) -> p a i c", i=PACK)[:, :, slots],
             )
+
+        def order_wd(b, pair):
+            slot_major(nc.scalar.copy, wd[b][:].bitcast(U16), wd_raw[b][:].bitcast(U16), slice(2 * pair, 2 * pair + 2))
 
         gather_words(0, 0)
         uses_raw.append(placed_at(uses1_at, "uses1", [P, PACK, M], F32)[:])
@@ -166,9 +164,9 @@ def tile_list_reaching_names_kernel(
         gather_words(1, 0)
         gather_words(1, 1)
         for b in range(RP):
-            slot_major(wd_s[b][:], wd_sc[:, :, PASS * b : PASS * (b + 1)])
-        for b in range(RP):
-            slot_major(wd[b][:], wd_raw[b][:])
+            slot_major(nc.gpsimd.tensor_copy, wd_s[b][:], wd_sc[:, :, PASS * b : PASS * (b + 1)])
+        for pair in range(2):
+            order_wd(0, pair)
 
         load_uses(1, uses_raw[1])
         load_channels(old_sb[0], old, 0)
@@ -259,8 +257,8 @@ def tile_list_reaching_names_kernel(
                     stop=(a == KP - 1),
                 )
             nc.scalar.activation(
-                out=gate[b][:, t, :].rearrange("m (i q e) -> m i q e", i=PACK, e=RUN),
-                in_=bank[:].rearrange("m (q i e) -> m i q e", i=PACK, e=RUN),
+                out=gate[b][:, t, :].rearrange("m (i p) -> m i p", i=PACK),
+                in_=bank[:].rearrange("m (p i) -> m i p", i=PACK),
                 func=ACT.Sigmoid,
             )
 
@@ -323,8 +321,10 @@ def tile_list_reaching_names_kernel(
         for s in range(SH):
             for i in range(2):
                 h_copy(0, i, s)
+        order_wd(1, 0)
         for i in range(2, PACK):
             make_h(0, i)
+        order_wd(1, 1)
         early_bf = sb("early_bf", [P, M // 2, PACK], BF16)
         nc.vector.tensor_copy(out=interleaved(early_bf[:]), in_=planar(uses0[0]))
         pick(0, 0)

@@ -81,8 +81,8 @@ def tile_list_reaching_names_kernel(
             rows = uses[PASS * a : PASS * (a + 1), cols].rearrange("(p i) c -> p i c", i=PACK)
             nc.sync.dma_start(out=dst, in_=rows)
 
-        def load_channels(dst, src, b):
-            nc.sync.dma_start(out=dst, in_=src[PASS * b : PASS * (b + 1), :].rearrange("(p i) c -> p i c", i=PACK))
+        def load_channels(dst, src, b, cols=slice(None)):
+            nc.sync.dma_start(out=dst, in_=src[PASS * b : PASS * (b + 1), cols].rearrange("(p i) c -> p i c", i=PACK))
 
         def load_tab(a):
             nc.sync.dma_start(out=tab[a][:], in_=tab_words[a].rearrange("p t i -> p (t i)").bitcast(I32))
@@ -126,7 +126,12 @@ def tile_list_reaching_names_kernel(
         nc.gpsimd.memset(wu_sc[:].bitcast(I32), 0)
         uses_raw = [None]
         uses0 = [four_rows(M + PACK * (M // 2) * c, M // 2) for c in range(2)]
-        old_sb = [four_rows(M + PACK * (M + M * b), M) for b in range(RP)]
+        old0 = four_rows(M + PACK * M, M)
+        old1 = [four_rows(M + PACK * (2 * M + M // 2 * c), M // 2) for c in range(2)]
+
+        def old_sites(b, t, tiles=1):
+            return old1[t // 2][:, :, sites(t % 2, tiles)] if b else old0[:, :, sites(t, tiles)]
+
         wo_raw = [four_rows(M + PACK * (M + RP * M + N * b), N) for b in range(RP)]
 
         def interleaved(tile):
@@ -142,17 +147,17 @@ def tile_list_reaching_names_kernel(
             entries = offs_sb[:, list_columns * s : list_columns * (s + 1)]
             nc.vector.tensor_copy(v[a][:, BANK * s : BANK * (s + 1)], tab[a][:].bitcast(U32).indirect(entries))
 
-        wd = [sb("wd%d" % b, [P, KP, 2 * PASS], U8) for b in range(RP)]
+        wd = [[sb("wd%d_%d" % (b, pair), [P, KP, PASS], U8) for pair in range(2)] for b in range(RP)]
         wd_s = [sb("wd_s%d" % b, [P, KP, PASS], U8) for b in range(RP)]
 
         def slot_major(copy, dst, src, slots=slice(0, PACK)):
             copy(
-                out=dst.rearrange("p a (i c) -> p a i c", i=PACK)[:, :, slots],
+                out=dst.rearrange("p a (i c) -> p a i c", c=P),
                 in_=src.rearrange("p a (c i) -> p a i c", i=PACK)[:, :, slots],
             )
 
         def order_wd(b, pair):
-            slot_major(nc.scalar.copy, wd[b][:].bitcast(U16), wd_raw[b][:].bitcast(U16), slice(2 * pair, 2 * pair + 2))
+            slot_major(nc.scalar.copy, wd[b][pair][:].bitcast(U16), wd_raw[b][:].bitcast(U16), slice(2 * pair, 2 * pair + 2))
 
         gather_words(0, 0)
         uses_raw.append(placed_at(uses1_at, "uses1", [P, PACK, M], F32)[:])
@@ -169,7 +174,7 @@ def tile_list_reaching_names_kernel(
             order_wd(0, pair)
 
         load_uses(1, uses_raw[1])
-        load_channels(old_sb[0], old, 0)
+        load_channels(old0, old, 0)
         for quad in QUADRANTS:
             nc.sync.dma_start(
                 out=wu_sc[32 * quad : 32 * quad + 8, :].bitcast(I32),
@@ -177,7 +182,8 @@ def tile_list_reaching_names_kernel(
             )
         for b in range(RP):
             load_wu(b)
-        load_channels(old_sb[1], old, 1)
+        for c in range(2):
+            load_channels(old1[c], old, 1, sites(2 * c, 2))
         for b in range(RP):
             load_channels(wo_raw[b], wo, b)
 
@@ -216,7 +222,7 @@ def tile_list_reaching_names_kernel(
                 h_bank[b, i, s] = bank_tile(SH * i + s)
             nc.tensor.matmul_mx(
                 out=h_bank[b, i, s][:],
-                lhsT=wd[b][:, a, 2 * P * i : 2 * P * (i + 1)].bitcast(FP4X4),
+                lhsT=wd[b][i // 2][:, a, 2 * P * (i % 2) : 2 * P * (i % 2 + 1)].bitcast(FP4X4),
                 lhsT_scale=wd_s[b][:, a, P * i : P * (i + 1)],
                 rhs=v[a][:, BANK * s : BANK * (s + 1)].bitcast(FP8X4),
                 rhs_scale=v_sc[:, a, BANK * s : BANK * (s + 1)],
@@ -274,7 +280,7 @@ def tile_list_reaching_names_kernel(
 
         def make_z(b, t, step):
             dst = interleaved(z_bf[b][:, sites(t), :])
-            nc.vector.tensor_tensor(dst, planar(old_sb[b][:, :, sites(t)]), planar(step), ALU.subtract)
+            nc.vector.tensor_tensor(dst, planar(old_sites(b, t)), planar(step), ALU.subtract)
 
         def quantize_z(b, t, tiles=1):
             quantize(z_codes[b][:, sites(t, tiles)], z_sc[b][:, sites(t, tiles)], z_bf[b][:, sites(t, tiles), :])
@@ -284,24 +290,30 @@ def tile_list_reaching_names_kernel(
         out_bank = {}
 
         def project(b, t):
+            apart = t == MT - 1
             if b == 0:
-                out_bank[t] = site_bank(t)
+                out_bank[t] = [gate_bank(n)[:, 0:P] for n in range(NT)] if apart else site_bank(t)
             for n in range(NT):
                 rows = slice(N * b + P * n, N * b + P * (n + 1))
                 nc.tensor.matmul_mx(
-                    out=out_bank[t][:, P * n : P * (n + 1)],
+                    out=out_bank[t][n] if apart else out_bank[t][:, P * n : P * (n + 1)],
                     lhsT=wo_codes[:, rows].bitcast(FP8X4),
                     lhsT_scale=wo_sc[:, rows],
                     rhs=z_codes[b][:, sites(t)].bitcast(FP8X4),
                     rhs_scale=z_sc[b][:, sites(t)],
-                    start=(b == 0 and n == 0),
-                    stop=(b == RP - 1 and n == NT - 1),
+                    start=(b == 0 and (apart or n == 0)),
+                    stop=(b == RP - 1 and (apart or n == NT - 1)),
                 )
 
         def store(t):
+            if t == MT - 1:
+                for n in range(NT):
+                    res = sb("last_res%d" % n, [P, P], F32)
+                    (nc.scalar.copy if n % 2 else nc.vector.tensor_copy)(out=res[:], in_=out_bank[t][n])
+                    nc.sync.dma_start(out=out[P * n : P * (n + 1), sites(t)], in_=res[:])
+                return
             res = sb("res%d" % t, [P, NT, P], F32)
-            copy = nc.vector.tensor_copy if t == MT - 1 else nc.scalar.copy
-            copy(out=res[:].rearrange("p n m -> p (n m)"), in_=out_bank[t][:, 0 : NT * P])
+            nc.scalar.copy(out=res[:].rearrange("p n m -> p (n m)"), in_=out_bank[t][:, 0 : NT * P])
             nc.sync.dma_start(out=out[:, sites(t)].rearrange("(n p) m -> p n m", p=P), in_=res[:])
 
         unread = bank_tile(2 * MT - 1)
@@ -350,7 +362,7 @@ def tile_list_reaching_names_kernel(
 
         for t in range(MT):
             for i in range(PACK):
-                add_turned(old_sb[0], t, i, i == 0, False)
+                add_turned(old0, t, i, i == 0, False)
             for i in range(PACK - 1):
                 add_turned(neg_x[0], t, i, False, False)
         for t in range(MT):
@@ -366,8 +378,9 @@ def tile_list_reaching_names_kernel(
             pick(1, i)
 
         difference = placed_at(difference_at, "difference", [P, PACK, M], F32)
-        for part in (sites(0), sites(1), sites(2, 2)):
-            nc.gpsimd.tensor_tensor(difference[:, :, part], old_sb[1][:, :, part], neg_x[1][:, :, part], ALU.add)
+        for t, tiles in ((0, 1), (1, 1), (2, 2)):
+            part = sites(t, tiles)
+            nc.gpsimd.tensor_tensor(difference[:, :, part], old_sites(1, t, tiles), neg_x[1][:, :, part], ALU.add)
         for t in range(MT):
             make_gate(1, t)
 
@@ -394,7 +407,7 @@ def tile_list_reaching_names_kernel(
         neg_old = sb("neg_old", [P, PASS], F32)
         bank = site_bank(last)
         for i in range(PACK):
-            nc.tensor.transpose(bank[:, P * i : P * (i + 1)], old_sb[0][:, i, sites(last)], ident[:])
+            nc.tensor.transpose(bank[:, P * i : P * (i + 1)], old0[:, i, sites(last)], ident[:])
         nc.scalar.activation(out=neg_old[:], in_=bank[:], func=ACT.Copy, scale=-1.0)
         round_wo(1)
         bank = site_bank(last)
@@ -437,8 +450,8 @@ def tile_list_reaching_names_kernel(
         finish(0)
         make_z(1, 2, step[:, :, sites(2)])
         finish(1)
+        finish(2)
+        make_z(1, last, step[:, :, sites(last)])
         quantize_z(0, last)
         project(0, last)
-        make_z(1, last, step[:, :, sites(last)])
-        finish(2)
         finish(last)

@@ -211,15 +211,16 @@ def tile_list_reaching_names_kernel(
         def bank_tile(n):
             return psum.tile([P, BANK], F32, name="bank", tag="bank%d" % n)
 
-        def gate_bank(t):
-            return bank_tile(MT + t)
+        def feed_bank(n):
+            return bank_tile(MT + n)
 
         def site_bank(t):
             return bank_tile(t)
 
+
         def h_pass(b, i, s, a):
             if a == 0:
-                h_bank[b, i, s] = bank_tile(SH * i + s)
+                h_bank[b, i, s] = (site_bank if b == 0 and i < 2 else feed_bank)(SH * (i % 2) + s)
             nc.tensor.matmul_mx(
                 out=h_bank[b, i, s][:],
                 lhsT=wd[b][i // 2][:, a, 2 * P * (i % 2) : 2 * P * (i % 2 + 1)].bitcast(FP4X4),
@@ -251,7 +252,7 @@ def tile_list_reaching_names_kernel(
             nc.vector.tensor_tensor(neg_x[b][:, i, :], h[b, i][:].indirect(offs2_sb[:]), wgt_sb, ALU.mult)
 
         def make_gate(b, t):
-            bank = gate_bank(t)
+            bank = feed_bank(t)
             for a in range(KP):
                 nc.tensor.matmul_mx(
                     out=bank[:],
@@ -292,7 +293,7 @@ def tile_list_reaching_names_kernel(
         def project(b, t):
             apart = t == MT - 1
             if b == 0:
-                out_bank[t] = [gate_bank(n)[:, 0:P] for n in range(NT)] if apart else site_bank(t)
+                out_bank[t] = [feed_bank(n)[:, 0:P] for n in range(NT)] if apart else site_bank(t)
             for n in range(NT):
                 rows = slice(N * b + P * n, N * b + P * (n + 1))
                 nc.tensor.matmul_mx(
@@ -354,19 +355,23 @@ def tile_list_reaching_names_kernel(
         for i in range(2, PACK):
             pick(0, i)
 
-        turned_difference = [site_bank(t) for t in range(MT)]
+        turned_difference = {}
 
         def add_turned(src, t, i, start, stop):
             dst = turned_difference[t][:, P * i : P * (i + 1)]
             nc.tensor.matmul(out=dst, lhsT=src[:, i, sites(t)], rhs=ident[:], is_transpose=True, start=start, stop=stop)
 
-        for t in range(MT):
-            for i in range(PACK):
-                add_turned(old0, t, i, i == 0, False)
-            for i in range(PACK - 1):
-                add_turned(neg_x[0], t, i, False, False)
-        for t in range(MT):
-            add_turned(neg_x[0], t, PACK - 1, False, True)
+        def make_turned_differences(tiles):
+            for t in tiles:
+                turned_difference[t] = site_bank(t)
+                for i in range(PACK):
+                    add_turned(old0, t, i, i == 0, False)
+                for i in range(PACK - 1):
+                    add_turned(neg_x[0], t, i, False, False)
+            for t in tiles:
+                add_turned(neg_x[0], t, PACK - 1, False, True)
+
+        make_turned_differences(range(MT))
         round_uses(1, nc.scalar.copy)
         quantize_uses(1)
         for i in range(EARLY_SLOTS, PACK):
@@ -390,7 +395,7 @@ def tile_list_reaching_names_kernel(
         last = MT - 1
         for t in range(last):
             make_z(0, t, turn(site_bank(t), turned_step[:, t, :]))
-        gate_back = [turn(gate_bank(t), gate[1][:, t, :]) for t in range(MT)]
+        gate_back = [turn(feed_bank(t), gate[1][:, t, :]) for t in range(MT)]
 
         wo_bf = sb("wo_bf", [P, RP * N, PACK], BF16, tag="gate0")
         piece = N // 2

@@ -29,6 +29,7 @@ NT = N // P
 SH = S // BANK
 QUADRANTS = (0, 2, 1, 3)
 WARM_PASSES = 3
+LATE_WARM_PASSES = 2
 EARLY_SLOTS = 2
 
 
@@ -317,17 +318,20 @@ def tile_list_reaching_names_kernel(
             nc.scalar.copy(out=res[:].rearrange("p n m -> p (n m)"), in_=out_bank[t][:, 0 : NT * P])
             nc.sync.dma_start(out=out[:, sites(t)].rearrange("(n p) m -> p n m", p=P), in_=res[:])
 
-        unread = bank_tile(2 * MT - 1)
-        for repeat in range(WARM_PASSES):
+        def warm_up(bank, lhsT, lhsT_scale, rhs, rhs_scale):
             nc.tensor.matmul_mx(
-                out=unread[:],
-                lhsT=v[0][:, 0:P].bitcast(FP8X4),
-                lhsT_scale=picked_sc[:, 0:P],
-                rhs=v[0][:, 0:BANK].bitcast(FP8X4),
-                rhs_scale=picked_sc[:, 0:BANK],
+                out=bank[:],
+                lhsT=lhsT.bitcast(FP8X4),
+                lhsT_scale=lhsT_scale,
+                rhs=rhs.bitcast(FP8X4),
+                rhs_scale=rhs_scale,
                 start=True,
                 stop=True,
             )
+
+        unread = feed_bank(MT - 1)
+        for repeat in range(WARM_PASSES):
+            warm_up(unread, v[0][:, 0:P], picked_sc[:, 0:P], v[0][:, 0:BANK], picked_sc[:, 0:BANK])
 
         for i, s, a in ((0, 0, 0), (0, 0, 1), (1, 0, 0), (1, 0, 1), (0, 1, 0), (0, 1, 1), (1, 1, 0), (1, 1, 1)):
             h_pass(0, i, s, a)
@@ -371,7 +375,11 @@ def tile_list_reaching_names_kernel(
             for t in tiles:
                 add_turned(neg_x[0], t, PACK - 1, False, True)
 
-        make_turned_differences(range(MT))
+        make_turned_differences(range(MT - 1))
+        unread = site_bank(MT - 1)
+        for repeat in range(LATE_WARM_PASSES):
+            warm_up(unread, u_codes[0][:, 0:P], u_sc[0][:, 0:P], wu[0][:, 0, :], wu_sc[:, 0:PASS])
+        make_turned_differences([MT - 1])
         round_uses(1, nc.scalar.copy)
         quantize_uses(1)
         for i in range(EARLY_SLOTS, PACK):

@@ -28,7 +28,6 @@ MT = M // P
 NT = N // P
 SH = S // BANK
 QUADRANTS = (0, 2, 1, 3)
-WARM_PASSES = 3
 LATE_WARM_PASSES = 2
 EARLY_SLOTS = 2
 
@@ -330,8 +329,8 @@ def tile_list_reaching_names_kernel(
             )
 
         unread = feed_bank(MT - 1)
-        for repeat in range(WARM_PASSES):
-            warm_up(unread, v[0][:, 0:P], picked_sc[:, 0:P], v[0][:, 0:BANK], picked_sc[:, 0:BANK])
+        for s in (0, 1, 1):
+            warm_up(unread, v[0][:, 0:P], picked_sc[:, 0:P], v[0][:, BANK * s : BANK * (s + 1)], picked_sc[:, 0:BANK])
 
         for i, s, a in ((0, 0, 0), (0, 0, 1), (1, 0, 0), (1, 0, 1), (0, 1, 0), (0, 1, 1), (1, 1, 0), (1, 1, 1)):
             h_pass(0, i, s, a)

from contextlib import ExitStack

import concourse.mybir as mybir
from concourse.masks import make_identity

T, S, M, K, H, N = 2048, 1024, 512, 1024, 1024, 384
FLOPS = 2 * (K * H * S + K * H * M + H * N * M)

F32 = mybir.dt.float32
BF16 = mybir.dt.bfloat16
I32 = mybir.dt.int32
U32 = mybir.dt.uint32
U16 = mybir.dt.uint16
U8 = mybir.dt.uint8
FP8X4 = mybir.dt.float8_e4m3fn_x4
FP4X4 = mybir.dt.float4_e2m1fn_x4
ALU = mybir.AluOpType
ACT = mybir.ActivationFunctionType

P = 128
PACK = 4
PASS = P * PACK
BANK = 512
LIST = 16
KP = K // PASS
RP = H // PASS
MT = M // P
NT = N // P
SH = S // BANK
QUADRANTS = (0, 2, 1, 3)
LATE_WARM_PASSES = 2
EARLY_SLOTS = 2


def tile_list_reaching_names_kernel(
    tc, tab_words, tab_scales, offs, wd_words, wd_scales, offs2, wgt, uses, wu_words, wu_scales, old, wo, out
):
    nc = tc.nc
    with ExitStack() as ctx:
        keep = ctx.enter_context(tc.tile_pool(name="keep", bufs=1))
        placed = ctx.enter_context(tc.tile_pool(name="placed", bufs=1))
        psum = ctx.enter_context(tc.psum_pool(name="psum", bufs=1))

        def sb(name, shape, dtype, tag=None):
            return keep.tile(shape, dtype, name=name, tag=tag or name, align_bytes=64)

        def placed_at(offset, name, shape, dtype):
            return placed.tile(shape, dtype, name=name, offset=offset, align_bytes=64)

        def sites(t, tiles=1):
            return slice(P * t, P * (t + tiles))

        float_columns = M + PACK * (M + RP * M + RP * N)
        difference_at = 4 * float_columns
        uses1_at = difference_at + 2 * S
        turned_step_at = difference_at + 4 * PACK * M
        wd1_at = uses1_at + 4 * PACK * M
        wu_sc_at = turned_step_at + 4 * MT * PASS
        wu_at = wu_sc_at + H
        tab_sc_at = difference_at - 64

        offs_sb = keep.tile([P, S // LIST], U16, name="offs_sb")
        offs2_sb = keep.tile([P, M // LIST], U16, name="offs2_sb")
        tab_sc = placed_at(tab_sc_at, "tab_sc", [P, wu_at + 64 - tab_sc_at], U8)[:, 0:T]
        wd_sc = sb("wd_sc", [P, KP, H], U8)
        picked_sc = sb("picked_sc", [P, S], U8)
        v_sc = sb("v_sc", [P, KP, S], U8)
        warm = sb("warm", [P, 1], F32)

        nc.gpsimd.memset(wd_sc[:].rearrange("p a c -> p (a c)").bitcast(I32), 0)
        nc.gpsimd.memset(tab_sc[32:64, :].bitcast(I32), 0)
        nc.vector.memset(warm[:], 0.0)
        nc.vector.memset(tab_sc[64:P, :].bitcast(I32), 0)
        nc.vector.memset(v_sc[:].rearrange("p a c -> p (a c)").bitcast(I32), 0)
        nc.scalar.activation(out=warm[:], in_=warm[:], func=ACT.Sigmoid)

        wd_raw = {}
        tab = [sb("tab%d" % a, [P, T], I32) for a in range(KP)]

        def load_uses(a, dst, cols=slice(0, M)):
            rows = uses[PASS * a : PASS * (a + 1), cols].rearrange("(p i) c -> p i c", i=PACK)
            nc.sync.dma_start(out=dst, in_=rows)

        def load_channels(dst, src, b, cols=slice(None)):
            nc.sync.dma_start(out=dst, in_=src[PASS * b : PASS * (b + 1), cols].rearrange("(p i) c -> p i c", i=PACK))

        def load_tab(a):
            nc.sync.dma_start(out=tab[a][:], in_=tab_words[a].rearrange("p t i -> p (t i)").bitcast(I32))

        def load_wd(b):
            shape = [P, KP, 2 * PASS]
            wd_raw[b] = placed_at(wd1_at, "wd_raw1", shape, U8) if b else sb("wd_raw0", shape, U8)
            src = wd_words.rearrange("a p c -> p a c")[:, :, 2 * PASS * b : 2 * PASS * (b + 1)]
            nc.sync.dma_start(out=wd_raw[b][:].bitcast(I32), in_=src.bitcast(I32))

        def load_wu(b):
            src = wu_words.rearrange("a p c i -> p a (c i)")[:, :, PACK * PASS * b : PACK * PASS * (b + 1)]
            nc.sync.dma_start(out=wu[b], in_=src.bitcast(I32))

        nc.sync.dma_start(out=tab_sc[0:32, :].bitcast(I32), in_=tab_scales.rearrange("a q c -> q a c").bitcast(I32))
        nc.sync.dma_start(offs_sb[:], offs)
        load_tab(0)
        nc.sync.dma_start(offs2_sb[:], offs2)
        for quad in QUADRANTS:
            nc.sync.dma_start(
                out=wd_sc[32 * quad : 32 * quad + 4, :, :].bitcast(I32),
                in_=wd_scales[:, 4 * quad : 4 * quad + 4, :].rearrange("a r c -> r a c").bitcast(I32),
            )
        load_tab(1)
        load_wd(0)
        nc.vector.tensor_copy(picked_sc[:], tab_sc.indirect(offs_sb[:]))
        for quad in QUADRANTS:
            nc.sync.dma_start(
                out=v_sc[32 * quad : 32 * quad + 4, :, :].bitcast(I32),
                in_=picked_sc[8 * quad : 8 * quad + 8, :].bitcast(I32),
            )
        floats = placed_at(0, "floats", [P, float_columns], F32)
        wu_sc = placed_at(wu_sc_at, "wu_sc", [P, H], U8)
        wu_all = placed_at(wu_at, "wu_all", [P, RP * KP * PASS], I32)

        def four_rows(start, width):
            return floats[:, start : start + PACK * width].rearrange("p (i c) -> p i c", i=PACK)

        wgt_sb = floats[:, 0:M]
        wu = [wu_all[:, KP * PASS * b : KP * PASS * (b + 1)].rearrange("p (a c) -> p a c", a=KP) for b in range(RP)]
        nc.gpsimd.memset(wu_sc[:].bitcast(I32), 0)
        uses_raw = [None]
        uses0 = [four_rows(M + PACK * (M // 2) * c, M // 2) for c in range(2)]
        old0 = four_rows(M + PACK * M, M)
        old1 = [four_rows(M + PACK * (2 * M + M // 2 * c), M // 2) for c in range(2)]

        def old_sites(b, t, tiles=1):
            return old1[t // 2][:, :, sites(t % 2, tiles)] if b else old0[:, :, sites(t, tiles)]

        wo_raw = [four_rows(M + PACK * (M + RP * M + N * b), N) for b in range(RP)]

        def interleaved(tile):
            return tile.rearrange("p (c j) i -> p c i j", j=2)

        def planar(tile):
            return tile.rearrange("p i (c j) -> p c i j", j=2)

        v = [sb("v%d" % a, [P, S], U32) for a in range(KP)]
        list_columns = BANK // LIST

        def gather_words(a, s):
            entries = offs_sb[:, list_columns * s : list_columns * (s + 1)]
            nc.vector.tensor_copy(v[a][:, BANK * s : BANK * (s + 1)], tab[a][:].bitcast(U32).indirect(entries))

        wd = [[sb("wd%d_%d" % (b, pair), [P, KP, PASS], U8) for pair in range(2)] for b in range(RP)]
        wd_s = [sb("wd_s%d" % b, [P, KP, PASS], U8) for b in range(RP)]

        def slot_major(copy, dst, src, slots=slice(0, PACK)):
            copy(
                out=dst.rearrange("p a (i c) -> p a i c", c=P),
                in_=src.rearrange("p a (c i) -> p a i c", i=PACK)[:, :, slots],
            )

        def order_wd(b, pair):
            slot_major(nc.scalar.copy, wd[b][pair][:].bitcast(U16), wd_raw[b][:].bitcast(U16), slice(2 * pair, 2 * pair + 2))

        gather_words(0, 0)
        uses_raw.append(placed_at(uses1_at, "uses1", [P, PACK, M], F32)[:])
        load_wd(1)
        load_uses(0, uses0[0], sites(0, 2))
        nc.sync.dma_start(out=wgt_sb, in_=wgt)
        load_uses(0, uses0[1], sites(2, 2))
        gather_words(0, 1)
        gather_words(1, 0)
        gather_words(1, 1)
        for b in range(RP):
            slot_major(nc.gpsimd.tensor_copy, wd_s[b][:], wd_sc[:, :, PASS * b : PASS * (b + 1)])
        for pair in range(2):
            order_wd(0, pair)

        load_uses(1, uses_raw[1])
        load_channels(old0, old, 0)
        for quad in QUADRANTS:
            nc.sync.dma_start(
                out=wu_sc[32 * quad : 32 * quad + 8, :].bitcast(I32),
                in_=wu_scales[:, 4 * quad : 4 * quad + 4, :].bitcast(I32),
            )
        for b in range(RP):
            load_wu(b)
        for c in range(2):
            load_channels(old1[c], old, 1, sites(2 * c, 2))
        for b in range(RP):
            load_channels(wo_raw[b], wo, b)

        uses_bf = {1: sb("uses_bf1", [P, M, PACK], BF16)}
        u_codes = [sb("u_codes%d" % a, [P, M], U32) for a in range(KP)]
        u_sc = [sb("u_sc%d" % a, [P, M], U8) for a in range(KP)]

        def quantize(codes, scales, src):
            nc.vector.quantize_mx(out=codes.bitcast(FP8X4), scales=scales, in_=src.rearrange("p c i -> p (c i)"))

        def round_uses(a, copy):
            copy(out=interleaved(uses_bf[a][:]), in_=planar(uses_raw[a]))

        def quantize_uses(a):
            quantize(u_codes[a][:], u_sc[a][:], uses_bf[a][:])

        ident = sb("ident", [P, P], F32)
        make_identity(nc, ident[:])

        h = {}
        h_bank = {}
        gate = [sb("gate%d" % b, [P, MT, PASS], F32) for b in range(RP)]
        neg_x = [sb("neg_x%d" % b, [P, PACK, M], F32) for b in range(RP)]

        def bank_tile(n):
            return psum.tile([P, BANK], F32, name="bank", tag="bank%d" % n)

        def feed_bank(n):
            return bank_tile(MT + n)

        def site_bank(t):
            return bank_tile(t)


        def h_pass(b, i, s, a):
            if a == 0:
                h_bank[b, i, s] = (site_bank if b == 0 and i < 2 else feed_bank)(SH * (i % 2) + s)
            nc.tensor.matmul_mx(
                out=h_bank[b, i, s][:],
                lhsT=wd[b][i // 2][:, a, 2 * P * (i % 2) : 2 * P * (i % 2 + 1)].bitcast(FP4X4),
                lhsT_scale=wd_s[b][:, a, P * i : P * (i + 1)],
                rhs=v[a][:, BANK * s : BANK * (s + 1)].bitcast(FP8X4),
                rhs_scale=v_sc[:, a, BANK * s : BANK * (s + 1)],
                start=(a == 0),
                stop=(a == KP - 1),
            )

        def h_copy(b, i, s):
            if s == 0 and b == 1 and i >= EARLY_SLOTS:
                h[b, i] = placed_at(uses1_at + 4 * S * (i - EARLY_SLOTS), "h%d_%d" % (b, i), [P, S], F32)
            elif s == 0:
                h[b, i] = sb("h%d_%d" % (b, i), [P, S], F32)
            dst = h[b, i][:, BANK * s : BANK * (s + 1)]
            if (b, i, s) == (0, 0, 1):
                nc.vector.tensor_scalar_mul(dst, h_bank[b, i, s][:], -1.0)
            else:
                nc.scalar.activation(out=dst, in_=h_bank[b, i, s][:], func=ACT.Copy, scale=-1.0)

        def make_h(b, i):
            for s in range(SH):
                for a in range(KP):
                    h_pass(b, i, s, a)
                h_copy(b, i, s)

        def pick(b, i):
            nc.vector.tensor_tensor(neg_x[b][:, i, :], h[b, i][:].indirect(offs2_sb[:]), wgt_sb, ALU.mult)

        def make_gate(b, t):
            bank = feed_bank(t)
            for a in range(KP):
                nc.tensor.matmul_mx(
                    out=bank[:],
                    lhsT=u_codes[a][:, sites(t)].bitcast(FP8X4),
                    lhsT_scale=u_sc[a][:, sites(t)],
                    rhs=wu[b][:, a, :].bitcast(FP8X4),
                    rhs_scale=wu_sc[4 * a : P, PASS * b : PASS * (b + 1)],
                    start=(a == 0),
                    stop=(a == KP - 1),
                )
            nc.scalar.activation(
                out=gate[b][:, t, :].rearrange("m (i p) -> m i p", i=PACK),
                in_=bank[:].rearrange("m (p i) -> m i p", i=PACK),
                func=ACT.Sigmoid,
            )

        def turn(bank, src):
            view = bank[:].rearrange("p (i m) -> p i m", i=PACK)
            for i in range(PACK):
                nc.tensor.transpose(view[:, i, :], src[:, P * i : P * (i + 1)], ident[:])
            return view

        z_codes = [sb("z_codes%d" % b, [P, M], U32) for b in range(RP)]
        z_sc = [sb("z_sc%d" % b, [P, M], U8) for b in range(RP)]
        z_bf = [sb("z_bf%d" % b, [P, M, PACK], BF16) for b in range(RP)]

        def make_z(b, t, step):
            dst = interleaved(z_bf[b][:, sites(t), :])
            nc.vector.tensor_tensor(dst, planar(old_sites(b, t)), planar(step), ALU.subtract)

        def quantize_z(b, t, tiles=1):
            quantize(z_codes[b][:, sites(t, tiles)], z_sc[b][:, sites(t, tiles)], z_bf[b][:, sites(t, tiles), :])

        wo_codes = sb("wo_codes", [P, RP * N], U32)
        wo_sc = sb("wo_sc", [P, RP * N], U8)
        out_bank = {}

        def project(b, t):
            apart = t == MT - 1
            if b == 0:
                out_bank[t] = [feed_bank(n)[:, 0:P] for n in range(NT)] if apart else site_bank(t)
            for n in range(NT):
                rows = slice(N * b + P * n, N * b + P * (n + 1))
                nc.tensor.matmul_mx(
                    out=out_bank[t][n] if apart else out_bank[t][:, P * n : P * (n + 1)],
                    lhsT=wo_codes[:, rows].bitcast(FP8X4),
                    lhsT_scale=wo_sc[:, rows],
                    rhs=z_codes[b][:, sites(t)].bitcast(FP8X4),
                    rhs_scale=z_sc[b][:, sites(t)],
                    start=(b == 0 and (apart or n == 0)),
                    stop=(b == RP - 1 and (apart or n == NT - 1)),
                )

        def store(t):
            if t == MT - 1:
                for n in range(NT):
                    res = sb("last_res%d" % n, [P, P], F32)
                    (nc.scalar.copy if n % 2 else nc.vector.tensor_copy)(out=res[:], in_=out_bank[t][n])
                    nc.sync.dma_start(out=out[P * n : P * (n + 1), sites(t)], in_=res[:])
                return
            res = sb("res%d" % t, [P, NT, P], F32)
            nc.scalar.copy(out=res[:].rearrange("p n m -> p (n m)"), in_=out_bank[t][:, 0 : NT * P])
            nc.sync.dma_start(out=out[:, sites(t)].rearrange("(n p) m -> p n m", p=P), in_=res[:])

        def warm_up(bank, lhsT, lhsT_scale, rhs, rhs_scale):
            nc.tensor.matmul_mx(
                out=bank[:],
                lhsT=lhsT.bitcast(FP8X4),
                lhsT_scale=lhsT_scale,
                rhs=rhs.bitcast(FP8X4),
                rhs_scale=rhs_scale,
                start=True,
                stop=True,
            )

        unread = feed_bank(MT - 1)
        for s in (0, 1, 1):
            warm_up(unread, v[0][:, 0:P], picked_sc[:, 0:P], v[0][:, BANK * s : BANK * (s + 1)], picked_sc[:, 0:BANK])

        for i, s, a in ((0, 0, 0), (0, 0, 1), (1, 0, 0), (1, 0, 1), (0, 1, 0), (0, 1, 1), (1, 1, 0), (1, 1, 1)):
            h_pass(0, i, s, a)
        for s in range(SH):
            for i in range(2):
                h_copy(0, i, s)
        order_wd(1, 0)
        for i in range(2, PACK):
            make_h(0, i)
        order_wd(1, 1)
        early_bf = sb("early_bf", [P, M // 2, PACK], BF16)
        nc.vector.tensor_copy(out=interleaved(early_bf[:]), in_=planar(uses0[0]))
        pick(0, 0)
        quantize(u_codes[0][:, sites(0, 2)], u_sc[0][:, sites(0, 2)], early_bf[:])
        late_bf = sb("late_bf", [P, M // 2, PACK], BF16, tag="h0_0")
        nc.vector.tensor_copy(out=interleaved(late_bf[:]), in_=planar(uses0[1]))
        for i in range(EARLY_SLOTS):
            make_h(1, i)
        for i in range(EARLY_SLOTS, PACK):
            for s in range(SH):
                for a in range(KP):
                    h_pass(1, i, s, a)
        pick(0, 1)
        quantize(u_codes[0][:, sites(2, 2)], u_sc[0][:, sites(2, 2)], late_bf[:])
        for i in range(2, PACK):
            pick(0, i)

        turned_difference = {}

        def add_turned(src, t, i, start, stop):
            dst = turned_difference[t][:, P * i : P * (i + 1)]
            nc.tensor.matmul(out=dst, lhsT=src[:, i, sites(t)], rhs=ident[:], is_transpose=True, start=start, stop=stop)

        def make_turned_differences(tiles):
            for t in tiles:
                turned_difference[t] = site_bank(t)
                for i in range(PACK):
                    add_turned(old0, t, i, i == 0, False)
                for i in range(PACK - 1):
                    add_turned(neg_x[0], t, i, False, False)
            for t in tiles:
                add_turned(neg_x[0], t, PACK - 1, False, True)

        make_turned_differences(range(MT - 1))
        unread = site_bank(MT - 1)
        for repeat in range(LATE_WARM_PASSES):
            warm_up(unread, u_codes[0][:, 0:P], u_sc[0][:, 0:P], wu[0][:, 0, :], wu_sc[:, 0:PASS])
        make_turned_differences([MT - 1])
        round_uses(1, nc.scalar.copy)
        quantize_uses(1)
        for i in range(EARLY_SLOTS, PACK):
            for s in range(SH):
                h_copy(1, i, s)
        for t in range(MT):
            make_gate(0, t)
        for i in range(PACK):
            pick(1, i)

        difference = placed_at(difference_at, "difference", [P, PACK, M], F32)
        for t, tiles in ((0, 1), (1, 1), (2, 2)):
            part = sites(t, tiles)
            nc.gpsimd.tensor_tensor(difference[:, :, part], old_sites(1, t, tiles), neg_x[1][:, :, part], ALU.add)
        for t in range(MT):
            make_gate(1, t)

        turned_step = placed_at(turned_step_at, "turned_step", [P, MT, PASS], F32)
        for t in range(MT):
            nc.vector.tensor_tensor(turned_step[:, t, :], turned_difference[t][:], gate[0][:, t, :], ALU.mult)
        last = MT - 1
        for t in range(last):
            make_z(0, t, turn(site_bank(t), turned_step[:, t, :]))
        gate_back = [turn(feed_bank(t), gate[1][:, t, :]) for t in range(MT)]

        wo_bf = sb("wo_bf", [P, RP * N, PACK], BF16, tag="gate0")
        piece = N // 2

        def round_wo(b):
            for c in range(0, N, piece):
                dst, src = wo_bf[:, N * b + c : N * b + c + piece, :], wo_raw[b][:, :, c : c + piece]
                if b == RP - 1 and c == 0:
                    nc.gpsimd.tensor_scalar(dst, src.rearrange("p i c -> p c i"), 1.0, 0.0, ALU.mult, ALU.add)
                else:
                    nc.scalar.copy(out=interleaved(dst), in_=planar(src))

        round_wo(0)
        neg_old = sb("neg_old", [P, PASS], F32)
        bank = site_bank(last)
        for i in range(PACK):
            nc.tensor.transpose(bank[:, P * i : P * (i + 1)], old0[:, i, sites(last)], ident[:])
        nc.scalar.activation(out=neg_old[:], in_=bank[:], func=ACT.Copy, scale=-1.0)
        round_wo(1)
        bank = site_bank(last)
        for i in range(PACK):
            for src, first in ((turned_step[:, last, :], True), (neg_old[:], False)):
                slot = slice(P * i, P * (i + 1))
                nc.tensor.matmul(
                    out=bank[:, slot], lhsT=src[:, slot], rhs=ident[:], is_transpose=True, start=first, stop=not first
                )
        nc.scalar.activation(
            out=z_bf[0][:, sites(last), :], in_=bank[:].rearrange("p (i m) -> p m i", i=PACK), func=ACT.Copy, scale=-1.0
        )

        def quantize_wo(part):
            c0, c1 = ((0, PASS), (PASS, RP * N))[part]
            quantize(wo_codes[:, c0:c1], wo_sc[:, c0:c1], wo_bf[:, c0:c1, :])

        step = sb("step", [P, PACK, M], F32)

        def make_step(t):
            nc.vector.tensor_tensor(step[:, :, sites(t)], gate_back[t], difference[:, :, sites(t)], ALU.mult)

        for t in range(MT):
            make_step(t)

        quantize_z(0, 0, 2)
        make_z(1, 0, step[:, :, sites(0)])
        quantize_wo(0)
        quantize_z(0, 2)
        for t in range(last):
            project(0, t)
        make_z(1, 1, step[:, :, sites(1)])
        quantize_wo(1)

        def finish(t):
            quantize_z(1, t)
            project(1, t)
            store(t)

        finish(0)
        make_z(1, 2, step[:, :, sites(2)])
        finish(1)
        finish(2)
        make_z(1, last, step[:, :, sites(last)])
        quantize_z(0, last)
        project(0, last)
        finish(last)
